import numpy as np
import ml_dtypes


def mxq(x, axis, fmt="e4m3"):
    dtype, down = {"e4m3": (ml_dtypes.float8_e4m3fn, 7), "e5m2": (ml_dtypes.float8_e5m2, 14)}[fmt]
    v = np.moveaxis(np.asarray(x, np.float32).astype(ml_dtypes.bfloat16).astype(np.float64), axis, -1)
    blocks = v.reshape(v.shape[:-1] + (-1, 32))
    amax = np.abs(blocks).max(-1, keepdims=True)
    byte = np.maximum(np.where(amax > 0, np.frexp(amax)[1] - 1 + 127, 0) - down, 1)
    scale = np.exp2(byte - 127.0)
    codes = (blocks / scale).astype(np.float32).astype(dtype).astype(np.float64)
    return np.moveaxis((codes * scale).reshape(v.shape), -1, axis)


WIDE = False


def mx_kscale(k):
    if not WIDE:
        return np.ones(k)
    levels = np.array([10, -10, 5, -5, 0])
    if k % 512:
        return np.exp2(np.random.permutation(np.resize(levels, k // 32))).repeat(32)
    a = np.empty((k // 512, 16))
    for p in range(k // 512):
        a[p, :8] = np.random.permutation(np.resize(levels, 8))
        for g in range(8):
            far = levels[np.abs(levels - a[p, g]) >= 10]
            a[p, g + 8] = far[np.random.randint(len(far))]
    return np.exp2(a.ravel()).repeat(32)


def f64(x):
    return np.asarray(x).astype(np.float64)


def striped(idx):
    return np.tile(idx.reshape(-1, 16).T, (8, 1)).astype(np.uint16)


def unstriped(offs):
    return offs[:16].T.reshape(-1).astype(np.int64)


E2M1 = np.array([0.0, 0.5, 1.0, 1.5, 2.0, 3.0, 4.0, 6.0, -0.0, -0.5, -1.0, -1.5, -2.0, -3.0, -4.0, -6.0])


def pack_fp4(w):
    k, n = w.shape
    w = f64(np.asarray(w, np.float32).astype(ml_dtypes.bfloat16)).reshape(k // 32, 32, n)
    amax = np.abs(w).max(1)
    mant, ex = np.frexp(amax / 6.0)
    byte = np.clip(np.where(amax > 0, np.where(mant > 0.5, ex, ex - 1) + 127, 1), 1, 254)
    scaled = (w * np.exp2(127.0 - byte)[:, None, :]).reshape(k, n).astype(np.float32)
    c = np.ascontiguousarray(scaled.reshape(k // 512, 128, 4, n).transpose(0, 1, 3, 2)).astype(ml_dtypes.float4_e2m1fn).view(np.uint8) & 0xF
    words = (c[..., 0::2] | (c[..., 1::2] << 4)).reshape(k // 512, 128, 2 * n)
    return np.ascontiguousarray(words), np.ascontiguousarray(byte.astype(np.uint8).reshape(k // 512, 16, n))


def unpack_fp4(words, scales):
    g, _, n = scales.shape
    words = np.ascontiguousarray(words).reshape(g, 128, n, 2)
    nib = np.empty((g, 128, n, 4), np.uint8)
    nib[..., 0::2] = words & 0xF
    nib[..., 1::2] = words >> 4
    vals = E2M1[nib] * np.repeat(np.exp2(scales.astype(np.float64) - 127.0), 8, axis=1)[..., None]
    return vals.transpose(0, 1, 3, 2).reshape(g * 512, n)


K, T, S, H, N = 1024, 2048, 1024, 512, 128


def setup_inputs():
    n = np.random.standard_normal
    s = mx_kscale(K)[:, None]
    u = mx_kscale(H)
    packed_w2 = pack_fp4(n((H, N)) / np.sqrt(H) / u[:, None])
    return {
        "xT": (n((K, T)) * s).astype(np.float32),
        "w1": (n((K, H)) / np.sqrt(K) / s * u).astype(np.float32),
        "w2_words": packed_w2[0],
        "w2_scales": packed_w2[1],
        "pos": (0.5 * n((H, S)) * u[:, None]).astype(np.float32),
        "offs": striped(np.random.permutation(T)[(T * np.random.uniform(0, 1, S) ** 4).astype(np.int64)]),
    }


def reference(xT, w1, w2_words, w2_scales, pos, offs):
    xq = mxq(f64(xT)[:, unstriped(offs)], 0, "e4m3")
    h = (mxq(f64(w1), 0, "e4m3").T @ xq) + f64(pos)
    return unpack_fp4(w2_words, w2_scales).T @ mxq(h, 0, "e4m3")

@@ -1,0 +1,220 @@
+from contextlib import ExitStack
+
+import concourse.mybir as mybir
+
+K, T, S, H, N = 1024, 2048, 1024, 512, 128
+FLOPS = 2 * K * H * S + 2 * H * N * S
+
+F32 = mybir.dt.float32
+BF16 = mybir.dt.bfloat16
+I32 = mybir.dt.int32
+U32 = mybir.dt.uint32
+U16 = mybir.dt.uint16
+U8 = mybir.dt.uint8
+FP8X4 = mybir.dt.float8_e4m3fn_x4
+FP4X4 = mybir.dt.float4_e2m1fn_x4
+
+P = 128
+PACK = 4
+K_PASS = P * PACK
+PASSES = K // K_PASS
+BLOCK = 128
+BLOCKS = S // BLOCK
+HALF = S // 2
+X_LOADS = ((1024, 1024), (1024, 512, 256, 256))
+UNIT = 512
+W_LOAD = 256
+POS_LOAD = 512
+H_BANKS = 4
+OUT_GROUPS = (2, 2, 2, 1, 1)
+
+
+def tile_picked_embpos_none_e_kernel(tc, xT, w1, w2_words, w2_scales, pos, offs, out):
+    nc = tc.nc
+    with ExitStack() as ctx:
+        keep = ctx.enter_context(tc.tile_pool(name="keep", bufs=1))
+        psum_h = ctx.enter_context(tc.psum_pool(name="psum_h", bufs=H_BANKS))
+        psum_o = ctx.enter_context(tc.psum_pool(name="psum_o", bufs=2))
+
+        offsets = keep.tile([P, S // 16], U16, name="offsets")
+
+        w2_codes = keep.tile([P, 2 * N], U8, name="w2_codes", align_bytes=64)
+        w2_plane = keep.tile([P, N], U8, name="w2_plane", align_bytes=64)
+        x_plane = keep.tile([P, T], U8, name="x_plane", align_bytes=64)
+        nc.vector.memset(w2_plane[:].bitcast(I32), 0)
+        nc.vector.memset(x_plane[:].bitcast(I32), 0)
+
+        x_raw = []
+        for g in range(PASSES):
+            rows = xT[g * K_PASS : (g + 1) * K_PASS, :].rearrange("(p j) t -> p j t", j=PACK)
+            start = 0
+            for width in X_LOADS[g]:
+                raw = keep.tile([P, PACK, width], F32, name="x_raw_%d_%d" % (g, start))
+                nc.sync.dma_start(out=raw[:], in_=rows[:, :, start : start + width])
+                if not x_raw:
+                    nc.sync.dma_start(offsets[:], offs)
+                x_raw.append((g, start, width, raw))
+                start += width
+
+        nc.scalar.dma_start(out=w2_codes[:].bitcast(I32), in_=w2_words[0].bitcast(I32))
+        for q in range(4):
+            nc.scalar.dma_start(
+                out=w2_plane[32 * q : 32 * q + 4, :].bitcast(I32),
+                in_=w2_scales[0, 4 * q : 4 * q + 4, :].bitcast(I32),
+            )
+
+        w_raw = []
+        for g in range(PASSES):
+            rows = w1[g * K_PASS : (g + 1) * K_PASS, :].rearrange("(p j) c -> p j c", j=PACK)
+            for start in range(0, H, W_LOAD):
+                raw = keep.tile([P, PACK, W_LOAD], F32, name="w_raw_%d_%d" % (g, start))
+                nc.sync.dma_start(out=raw[:], in_=rows[:, :, start : start + W_LOAD])
+                w_raw.append((g, start, raw))
+
+        pos_rows = pos.rearrange("(p t) s -> p t s", t=PACK)
+        pos_sb = []
+        for start in range(0, S, POS_LOAD):
+            piece = keep.tile([P, PACK, POS_LOAD], F32, name="pos_%d" % start)
+            nc.sync.dma_start(out=piece[:], in_=pos_rows[:, :, start : start + POS_LOAD])
+            pos_sb.append(piece)
+
+        x_codes = [keep.tile([P, T], U32, name="x_codes_%d" % g, align_bytes=64) for g in range(PASSES)]
+
+        def plane_rows(plane, g, cols):
+            return plane[4 * g : P, cols]
+
+        def quantise_x(g, start, width, raw):
+            for u0 in range(0, width, UNIT):
+                n = min(UNIT, width - u0)
+                grouped = keep.tile([P, n, PACK], BF16, name="x_bf_%d_%d" % (g, start + u0), align_bytes=64)
+                cut = n // 2 if start + u0 + n < T or g == 0 else n * 5 // 8
+                nc.vector.tensor_copy(
+                    out=grouped[:, :cut, :].rearrange("p (c i) j -> p c j i", i=4),
+                    in_=raw[:, :, u0 : u0 + cut].rearrange("p j (c i) -> p c j i", i=4),
+                )
+                nc.scalar.copy(
+                    out=grouped[:, cut:, :].rearrange("p (c i) j -> p c j i", i=4),
+                    in_=raw[:, :, u0 + cut : u0 + n].rearrange("p j (c i) -> p c j i", i=4),
+                )
+                cols = slice(start + u0, start + u0 + n)
+                nc.vector.quantize_mx(
+                    out=x_codes[g][:, cols].bitcast(FP8X4),
+                    scales=plane_rows(x_plane, g, cols),
+                    in_=grouped[:].rearrange("p n j -> p (n j)"),
+                )
+
+        def gather(name, window, dtype, start, count, tag=None):
+            picked = keep.tile([P, count], dtype, name=name, tag=tag or name, align_bytes=64)
+            nc.vector.tensor_copy(picked[:], window[:].indirect(offsets[:, start // 16 : (start + count) // 16]))
+            return picked
+
+        w_codes = [keep.tile([P, H], U32, name="w_codes_%d" % g, align_bytes=64) for g in range(PASSES)]
+        w_plane = [keep.tile([P, H], U8, name="w_plane_%d" % g, align_bytes=64) for g in range(PASSES)]
+        w_bf = [keep.tile([P, PACK, P, PACK], BF16, name="w_bf_%d" % g, tag="w_bf_%d" % g, align_bytes=64) for g in range(PASSES)]
+
+        def weave_w(g, start, raw):
+            m0 = start // PACK
+            nc.scalar.copy(
+                out=w_bf[g][:, :, m0 : m0 + W_LOAD // PACK, :].rearrange("p t m j -> p m j t"),
+                in_=raw[:].rearrange("p j (m t) -> p m j t", t=PACK),
+            )
+
+        def quantise_w(g):
+            for t0 in range(0, PACK, 2):
+                cols = slice(t0 * P, (t0 + 2) * P)
+                nc.vector.quantize_mx(
+                    out=w_codes[g][:, cols].bitcast(FP8X4),
+                    scales=w_plane[g][:, cols],
+                    in_=w_bf[g][:, t0 : t0 + 2, :, :].rearrange("p t m j -> p (t m j)"),
+                )
+
+        for g, start, width, raw in x_raw:
+            if g == 0:
+                quantise_x(g, start, width, raw)
+        picked_0 = gather("picked_0", x_codes[0], U32, 0, S)
+        for g, start, width, raw in x_raw:
+            if g == 1:
+                quantise_x(g, start, width, raw)
+        for g, start, raw in w_raw:
+            weave_w(g, start, raw)
+
+        picked_plane, picked_1 = [], []
+        for half in range(2):
+            picked_plane.append(gather("picked_plane_%d" % half, x_plane, U8, half * HALF, HALF, "w_bf_0" if half else None))
+            picked_1.append(gather("picked_1_%d" % half, x_codes[1], U32, half * HALF, HALF))
+            quantise_w(half)
+
+        banks = {}
+
+        def first_product(b, g):
+            if g == 0:
+                banks[b] = psum_h.tile([P, PACK, BLOCK], F32, name="h_bank")
+            half, local = divmod(b * BLOCK, HALF)
+            cols = slice(local, local + BLOCK)
+            moving = picked_0[:, b * BLOCK : (b + 1) * BLOCK] if g == 0 else picked_1[half][:, cols]
+            for t in range(PACK):
+                w_cols = slice(t * P, (t + 1) * P)
+                nc.tensor.matmul_mx(
+                    out=banks[b][:, t, :],
+                    lhsT=w_codes[g][:, w_cols].bitcast(FP8X4),
+                    lhsT_scale=w_plane[g][:, w_cols],
+                    rhs=moving.bitcast(FP8X4),
+                    rhs_scale=plane_rows(picked_plane[half], g, cols),
+                    start=(g == 0 and t == 0),
+                    stop=(g == PASSES - 1 and t == PACK - 1),
+                )
+
+        group_of = []
+        for index, size in enumerate(OUT_GROUPS):
+            group_of.extend([index] * size)
+        h_bf = [keep.tile([P, size * BLOCK, PACK], BF16, name="h_bf_%d" % i, align_bytes=64) for i, size in enumerate(OUT_GROUPS)]
+
+        def add_pos(b):
+            index = group_of[b]
+            local = (b - group_of.index(index)) * BLOCK
+            piece, col = divmod(b * BLOCK, POS_LOAD)
+            nc.vector.tensor_tensor(
+                out=h_bf[index][:, local : local + BLOCK, :].rearrange("p (c i) t -> p c t i", i=4),
+                in0=banks[b][:].rearrange("p t (c i) -> p c t i", i=4),
+                in1=pos_sb[piece][:, :, col : col + BLOCK].rearrange("p t (c i) -> p c t i", i=4),
+                op=mybir.AluOpType.add,
+            )
+
+        def second_product(index):
+            width = OUT_GROUPS[index] * BLOCK
+            start = group_of.index(index) * BLOCK
+            h_codes = keep.tile([P, width], U32, name="h_codes_%d" % index, align_bytes=64)
+            h_plane = keep.tile([P, width], U8, name="h_plane_%d" % index, align_bytes=64)
+            nc.vector.quantize_mx(
+                out=h_codes[:].bitcast(FP8X4),
+                scales=h_plane[:],
+                in_=h_bf[index][:].rearrange("p n t -> p (n t)"),
+            )
+            acc = psum_o.tile([P, width], F32, name="out_bank")
+            nc.tensor.matmul_mx(
+                out=acc[:],
+                lhsT=w2_codes[:].bitcast(FP4X4),
+                lhsT_scale=w2_plane[:],
+                rhs=h_codes[:].bitcast(FP8X4),
+                rhs_scale=h_plane[:],
+                start=True,
+                stop=True,
+            )
+            result = keep.tile([P, width], F32, name="result_%d" % index)
+            nc.scalar.copy(out=result[:], in_=acc[:])
+            nc.sync.dma_start(out=out[:, start : start + width], in_=result[:])
+
+        for b in range(H_BANKS):
+            first_product(b, 0)
+        waiting = None
+        for b in range(BLOCKS):
+            if b >= H_BANKS:
+                first_product(b, 0)
+            first_product(b, 1)
+            add_pos(b)
+            if waiting is not None:
+                second_product(waiting)
+                waiting = None
+            if b + 1 == BLOCKS or group_of[b + 1] != group_of[b]:
+                waiting = group_of[b]
+        second_product(waiting)

@@ -21,10 +21,12 @@ PASSES = K // K_PASS
 BLOCK = 128
 BLOCKS = S // BLOCK
 HALF = S // 2
-X_LOADS = ((1024, 1024), (1024, 512, 256, 256))
+X_LOADS = ((1280, 768), (1024, 512, 256, 256))
+VECTOR_EIGHTHS = ((4, 4, 4, 4, 4), (4, 4, 4, 4, 5))
+W_VECTOR = (16, 32)
 UNIT = 512
-W_LOAD = 256
-POS_LOAD = 512
+W_LOAD = 512
+POS_LOADS = (640, 384)
 H_BANKS = 4
 OUT_GROUPS = (2, 2, 2, 1, 1)
 
@@ -41,7 +43,7 @@ def tile_picked_embpos_none_e_kernel(tc, xT, w1, w2_words, w2_scales, pos, offs,
         w2_codes = keep.tile([P, 2 * N], U8, name="w2_codes", align_bytes=64)
         w2_plane = keep.tile([P, N], U8, name="w2_plane", align_bytes=64)
         x_plane = keep.tile([P, T], U8, name="x_plane", align_bytes=64)
-        nc.vector.memset(w2_plane[:].bitcast(I32), 0)
+        nc.gpsimd.memset(w2_plane[:].bitcast(I32), 0)
         nc.vector.memset(x_plane[:].bitcast(I32), 0)
 
         x_raw = []
@@ -53,12 +55,12 @@ def tile_picked_embpos_none_e_kernel(tc, xT, w1, w2_words, w2_scales, pos, offs,
                 nc.sync.dma_start(out=raw[:], in_=rows[:, :, start : start + width])
                 if not x_raw:
                     nc.sync.dma_start(offsets[:], offs)
+                    nc.sync.dma_start(out=w2_codes[:].bitcast(I32), in_=w2_words[0].bitcast(I32))
                 x_raw.append((g, start, width, raw))
                 start += width
 
-        nc.scalar.dma_start(out=w2_codes[:].bitcast(I32), in_=w2_words[0].bitcast(I32))
         for q in range(4):
-            nc.scalar.dma_start(
+            nc.gpsimd.dma_start(
                 out=w2_plane[32 * q : 32 * q + 4, :].bitcast(I32),
                 in_=w2_scales[0, 4 * q : 4 * q + 4, :].bitcast(I32),
             )
@@ -67,27 +69,31 @@ def tile_picked_embpos_none_e_kernel(tc, xT, w1, w2_words, w2_scales, pos, offs,
         for g in range(PASSES):
             rows = w1[g * K_PASS : (g + 1) * K_PASS, :].rearrange("(p j) c -> p j c", j=PACK)
             for start in range(0, H, W_LOAD):
-                raw = keep.tile([P, PACK, W_LOAD], F32, name="w_raw_%d_%d" % (g, start))
+                raw = keep.tile([P, PACK, W_LOAD], F32, name="w_raw_%d_%d" % (g, start), tag="w_raw_%d_%d" % (g, start), align_bytes=64)
                 nc.sync.dma_start(out=raw[:], in_=rows[:, :, start : start + W_LOAD])
                 w_raw.append((g, start, raw))
 
         pos_rows = pos.rearrange("(p t) s -> p t s", t=PACK)
         pos_sb = []
-        for start in range(0, S, POS_LOAD):
-            piece = keep.tile([P, PACK, POS_LOAD], F32, name="pos_%d" % start)
-            nc.sync.dma_start(out=piece[:], in_=pos_rows[:, :, start : start + POS_LOAD])
-            pos_sb.append(piece)
+        start = 0
+        for width in POS_LOADS:
+            piece = keep.tile([P, PACK, width], F32, name="pos_%d" % start)
+            nc.sync.dma_start(out=piece[:], in_=pos_rows[:, :, start : start + width])
+            pos_sb.extend(piece[:, :, col : col + BLOCK] for col in range(0, width, BLOCK))
+            start += width
 
         x_codes = [keep.tile([P, T], U32, name="x_codes_%d" % g, align_bytes=64) for g in range(PASSES)]
 
         def plane_rows(plane, g, cols):
             return plane[4 * g : P, cols]
 
+        shares = [list(s) for s in VECTOR_EIGHTHS]
+
         def quantise_x(g, start, width, raw):
             for u0 in range(0, width, UNIT):
                 n = min(UNIT, width - u0)
                 grouped = keep.tile([P, n, PACK], BF16, name="x_bf_%d_%d" % (g, start + u0), align_bytes=64)
-                cut = n // 2 if start + u0 + n < T or g == 0 else n * 5 // 8
+                cut = n * shares[g].pop(0) // 8
                 nc.vector.tensor_copy(
                     out=grouped[:, :cut, :].rearrange("p (c i) j -> p c j i", i=4),
                     in_=raw[:, :, u0 : u0 + cut].rearrange("p j (c i) -> p c j i", i=4),
@@ -113,11 +119,10 @@ def tile_picked_embpos_none_e_kernel(tc, xT, w1, w2_words, w2_scales, pos, offs,
         w_bf = [keep.tile([P, PACK, P, PACK], BF16, name="w_bf_%d" % g, tag="w_bf_%d" % g, align_bytes=64) for g in range(PASSES)]
 
         def weave_w(g, start, raw):
-            m0 = start // PACK
-            nc.scalar.copy(
-                out=w_bf[g][:, :, m0 : m0 + W_LOAD // PACK, :].rearrange("p t m j -> p m j t"),
-                in_=raw[:].rearrange("p j (m t) -> p m j t", t=PACK),
-            )
+            woven = w_bf[g][:].rearrange("p t m j -> p m j t")
+            source = raw[:].rearrange("p j (m t) -> p m j t", t=PACK)
+            nc.scalar.copy(out=woven[:, W_VECTOR[g] :], in_=source[:, W_VECTOR[g] :])
+            nc.vector.tensor_copy(out=woven[:, : W_VECTOR[g]], in_=source[:, : W_VECTOR[g]])
 
         def quantise_w(g):
             for t0 in range(0, PACK, 2):
@@ -135,13 +140,12 @@ def tile_picked_embpos_none_e_kernel(tc, xT, w1, w2_words, w2_scales, pos, offs,
         for g, start, width, raw in x_raw:
             if g == 1:
                 quantise_x(g, start, width, raw)
-        for g, start, raw in w_raw:
-            weave_w(g, start, raw)
 
         picked_plane, picked_1 = [], []
         for half in range(2):
-            picked_plane.append(gather("picked_plane_%d" % half, x_plane, U8, half * HALF, HALF, "w_bf_0" if half else None))
-            picked_1.append(gather("picked_1_%d" % half, x_codes[1], U32, half * HALF, HALF))
+            picked_plane.append(gather("picked_plane_%d" % half, x_plane, U8, half * HALF, HALF))
+            picked_1.append(gather("picked_1_%d" % half, x_codes[1], U32, half * HALF, HALF, "w_bf_0" if half else None))
+            weave_w(*w_raw[half])
             quantise_w(half)
 
         banks = {}
@@ -172,11 +176,10 @@ def tile_picked_embpos_none_e_kernel(tc, xT, w1, w2_words, w2_scales, pos, offs,
         def add_pos(b):
             index = group_of[b]
             local = (b - group_of.index(index)) * BLOCK
-            piece, col = divmod(b * BLOCK, POS_LOAD)
             nc.vector.tensor_tensor(
                 out=h_bf[index][:, local : local + BLOCK, :].rearrange("p (c i) t -> p c t i", i=4),
                 in0=banks[b][:].rearrange("p t (c i) -> p c t i", i=4),
-                in1=pos_sb[piece][:, :, col : col + BLOCK].rearrange("p t (c i) -> p c t i", i=4),
+                in1=pos_sb[b].rearrange("p t (c i) -> p c t i", i=4),
                 op=mybir.AluOpType.add,
             )
 

@@ -23,11 +23,10 @@ BLOCKS = S // BLOCK
 HALF = S // 2
 X_LOADS = ((1280, 768), (1024, 512, 256, 256))
 VECTOR_EIGHTHS = ((4, 4, 4, 4, 4), (4, 4, 4, 4, 5))
-W_VECTOR = (16, 32)
 UNIT = 512
-W_LOAD = 512
-POS_LOADS = (640, 384)
-H_BANKS = 4
+W_LOAD = 256
+POS_LOAD = 512
+H_BANKS = 6
 OUT_GROUPS = (2, 2, 2, 1, 1)
 
 
@@ -75,12 +74,10 @@ def tile_picked_embpos_none_e_kernel(tc, xT, w1, w2_words, w2_scales, pos, offs,
 
         pos_rows = pos.rearrange("(p t) s -> p t s", t=PACK)
         pos_sb = []
-        start = 0
-        for width in POS_LOADS:
-            piece = keep.tile([P, PACK, width], F32, name="pos_%d" % start)
-            nc.sync.dma_start(out=piece[:], in_=pos_rows[:, :, start : start + width])
-            pos_sb.extend(piece[:, :, col : col + BLOCK] for col in range(0, width, BLOCK))
-            start += width
+        for start in range(0, S, POS_LOAD):
+            piece = keep.tile([P, PACK, POS_LOAD], F32, name="pos_%d" % start)
+            nc.sync.dma_start(out=piece[:], in_=pos_rows[:, :, start : start + POS_LOAD])
+            pos_sb.append(piece)
 
         x_codes = [keep.tile([P, T], U32, name="x_codes_%d" % g, align_bytes=64) for g in range(PASSES)]
 
@@ -119,10 +116,11 @@ def tile_picked_embpos_none_e_kernel(tc, xT, w1, w2_words, w2_scales, pos, offs,
         w_bf = [keep.tile([P, PACK, P, PACK], BF16, name="w_bf_%d" % g, tag="w_bf_%d" % g, align_bytes=64) for g in range(PASSES)]
 
         def weave_w(g, start, raw):
-            woven = w_bf[g][:].rearrange("p t m j -> p m j t")
-            source = raw[:].rearrange("p j (m t) -> p m j t", t=PACK)
-            nc.scalar.copy(out=woven[:, W_VECTOR[g] :], in_=source[:, W_VECTOR[g] :])
-            nc.vector.tensor_copy(out=woven[:, : W_VECTOR[g]], in_=source[:, : W_VECTOR[g]])
+            m0 = start // PACK
+            nc.scalar.copy(
+                out=w_bf[g][:, :, m0 : m0 + W_LOAD // PACK, :].rearrange("p t m j -> p m j t"),
+                in_=raw[:].rearrange("p j (m t) -> p m j t", t=PACK),
+            )
 
         def quantise_w(g):
             for t0 in range(0, PACK, 2):
@@ -140,12 +138,13 @@ def tile_picked_embpos_none_e_kernel(tc, xT, w1, w2_words, w2_scales, pos, offs,
         for g, start, width, raw in x_raw:
             if g == 1:
                 quantise_x(g, start, width, raw)
+        for g, start, raw in w_raw:
+            weave_w(g, start, raw)
 
         picked_plane, picked_1 = [], []
         for half in range(2):
-            picked_plane.append(gather("picked_plane_%d" % half, x_plane, U8, half * HALF, HALF))
-            picked_1.append(gather("picked_1_%d" % half, x_codes[1], U32, half * HALF, HALF, "w_bf_0" if half else None))
-            weave_w(*w_raw[half])
+            picked_plane.append(gather("picked_plane_%d" % half, x_plane, U8, half * HALF, HALF, "w_bf_0" if half else None))
+            picked_1.append(gather("picked_1_%d" % half, x_codes[1], U32, half * HALF, HALF, "w_raw_0_%d" % (H - W_LOAD) if half else None))
             quantise_w(half)
 
         banks = {}
@@ -176,10 +175,11 @@ def tile_picked_embpos_none_e_kernel(tc, xT, w1, w2_words, w2_scales, pos, offs,
         def add_pos(b):
             index = group_of[b]
             local = (b - group_of.index(index)) * BLOCK
+            piece, col = divmod(b * BLOCK, POS_LOAD)
             nc.vector.tensor_tensor(
                 out=h_bf[index][:, local : local + BLOCK, :].rearrange("p (c i) t -> p c t i", i=4),
                 in0=banks[b][:].rearrange("p t (c i) -> p c t i", i=4),
-                in1=pos_sb[b].rearrange("p t (c i) -> p c t i", i=4),
+                in1=pos_sb[piece][:, :, col : col + BLOCK].rearrange("p t (c i) -> p c t i", i=4),
                 op=mybir.AluOpType.add,
             )
 

@@ -21,13 +21,14 @@ PASSES = K // K_PASS
 BLOCK = 128
 BLOCKS = S // BLOCK
 HALF = S // 2
-X_LOADS = ((1280, 768), (1024, 512, 256, 256))
-VECTOR_EIGHTHS = ((4, 4, 4, 4, 4), (4, 4, 4, 4, 5))
-UNIT = 512
-W_LOAD = 256
-POS_LOAD = 512
-H_BANKS = 6
-OUT_GROUPS = (2, 2, 2, 1, 1)
+X_LOADS = (((512, 512, 256), (512, 256)), ((256, 512), (512,), (512,), (256,)))
+VECTOR_EIGHTHS = ((4, 4, 4, 5, 5), (0, 3, 5, 5, 3))
+POS_LOADS = (640, 384)
+GPSIMD_BLOCKS = 1
+LAG = (1, 1, 1, 1)
+H_BANKS = 5
+W_VECTOR_COLUMNS = 64
+OUT_GROUPS = (4, 2, 1, 1)
 
 
 def tile_picked_embpos_none_e_kernel(tc, xT, w1, w2_words, w2_scales, pos, offs, out):
@@ -35,7 +36,7 @@ def tile_picked_embpos_none_e_kernel(tc, xT, w1, w2_words, w2_scales, pos, offs,
     with ExitStack() as ctx:
         keep = ctx.enter_context(tc.tile_pool(name="keep", bufs=1))
         psum_h = ctx.enter_context(tc.psum_pool(name="psum_h", bufs=H_BANKS))
-        psum_o = ctx.enter_context(tc.psum_pool(name="psum_o", bufs=2))
+        psum_o = ctx.enter_context(tc.psum_pool(name="psum_o", bufs=3))
 
         offsets = keep.tile([P, S // 16], U16, name="offsets")
 
@@ -49,13 +50,14 @@ def tile_picked_embpos_none_e_kernel(tc, xT, w1, w2_words, w2_scales, pos, offs,
         for g in range(PASSES):
             rows = xT[g * K_PASS : (g + 1) * K_PASS, :].rearrange("(p j) t -> p j t", j=PACK)
             start = 0
-            for width in X_LOADS[g]:
+            for units in X_LOADS[g]:
+                width = sum(units)
                 raw = keep.tile([P, PACK, width], F32, name="x_raw_%d_%d" % (g, start))
                 nc.sync.dma_start(out=raw[:], in_=rows[:, :, start : start + width])
                 if not x_raw:
                     nc.sync.dma_start(offsets[:], offs)
                     nc.sync.dma_start(out=w2_codes[:].bitcast(I32), in_=w2_words[0].bitcast(I32))
-                x_raw.append((g, start, width, raw))
+                x_raw.append((g, start, units, raw))
                 start += width
 
         for q in range(4):
@@ -67,17 +69,18 @@ def tile_picked_embpos_none_e_kernel(tc, xT, w1, w2_words, w2_scales, pos, offs,
         w_raw = []
         for g in range(PASSES):
             rows = w1[g * K_PASS : (g + 1) * K_PASS, :].rearrange("(p j) c -> p j c", j=PACK)
-            for start in range(0, H, W_LOAD):
-                raw = keep.tile([P, PACK, W_LOAD], F32, name="w_raw_%d_%d" % (g, start), tag="w_raw_%d_%d" % (g, start), align_bytes=64)
-                nc.sync.dma_start(out=raw[:], in_=rows[:, :, start : start + W_LOAD])
-                w_raw.append((g, start, raw))
+            raw = keep.tile([P, PACK, H], F32, name="w_raw_%d" % g, tag="w_raw_%d" % g, align_bytes=64)
+            nc.sync.dma_start(out=raw[:], in_=rows)
+            w_raw.append(raw)
 
         pos_rows = pos.rearrange("(p t) s -> p t s", t=PACK)
         pos_sb = []
-        for start in range(0, S, POS_LOAD):
-            piece = keep.tile([P, PACK, POS_LOAD], F32, name="pos_%d" % start)
-            nc.sync.dma_start(out=piece[:], in_=pos_rows[:, :, start : start + POS_LOAD])
-            pos_sb.append(piece)
+        start = 0
+        for width in POS_LOADS:
+            piece = keep.tile([P, PACK, width], F32, name="pos_%d" % start)
+            nc.sync.dma_start(out=piece[:], in_=pos_rows[:, :, start : start + width])
+            pos_sb.extend(piece[:, :, c : c + BLOCK] for c in range(0, width, BLOCK))
+            start += width
 
         x_codes = [keep.tile([P, T], U32, name="x_codes_%d" % g, align_bytes=64) for g in range(PASSES)]
 
@@ -86,15 +89,16 @@ def tile_picked_embpos_none_e_kernel(tc, xT, w1, w2_words, w2_scales, pos, offs,
 
         shares = [list(s) for s in VECTOR_EIGHTHS]
 
-        def quantise_x(g, start, width, raw):
-            for u0 in range(0, width, UNIT):
-                n = min(UNIT, width - u0)
+        def quantise_x(g, start, units, raw):
+            u0 = 0
+            for n in units:
                 grouped = keep.tile([P, n, PACK], BF16, name="x_bf_%d_%d" % (g, start + u0), align_bytes=64)
                 cut = n * shares[g].pop(0) // 8
-                nc.vector.tensor_copy(
-                    out=grouped[:, :cut, :].rearrange("p (c i) j -> p c j i", i=4),
-                    in_=raw[:, :, u0 : u0 + cut].rearrange("p j (c i) -> p c j i", i=4),
-                )
+                if cut:
+                    nc.vector.tensor_copy(
+                        out=grouped[:, :cut, :].rearrange("p (c i) j -> p c j i", i=4),
+                        in_=raw[:, :, u0 : u0 + cut].rearrange("p j (c i) -> p c j i", i=4),
+                    )
                 nc.scalar.copy(
                     out=grouped[:, cut:, :].rearrange("p (c i) j -> p c j i", i=4),
                     in_=raw[:, :, u0 + cut : u0 + n].rearrange("p j (c i) -> p c j i", i=4),
@@ -105,6 +109,7 @@ def tile_picked_embpos_none_e_kernel(tc, xT, w1, w2_words, w2_scales, pos, offs,
                     scales=plane_rows(x_plane, g, cols),
                     in_=grouped[:].rearrange("p n j -> p (n j)"),
                 )
+                u0 += n
 
         def gather(name, window, dtype, start, count, tag=None):
             picked = keep.tile([P, count], dtype, name=name, tag=tag or name, align_bytes=64)
@@ -113,56 +118,60 @@ def tile_picked_embpos_none_e_kernel(tc, xT, w1, w2_words, w2_scales, pos, offs,
 
         w_codes = [keep.tile([P, H], U32, name="w_codes_%d" % g, align_bytes=64) for g in range(PASSES)]
         w_plane = [keep.tile([P, H], U8, name="w_plane_%d" % g, align_bytes=64) for g in range(PASSES)]
-        w_bf = [keep.tile([P, PACK, P, PACK], BF16, name="w_bf_%d" % g, tag="w_bf_%d" % g, align_bytes=64) for g in range(PASSES)]
+        w_bf = {}
 
-        def weave_w(g, start, raw):
-            m0 = start // PACK
-            nc.scalar.copy(
-                out=w_bf[g][:, :, m0 : m0 + W_LOAD // PACK, :].rearrange("p t m j -> p m j t"),
-                in_=raw[:].rearrange("p j (m t) -> p m j t", t=PACK),
+        def weave_w(g, u):
+            name = "w_bf_%d_%d" % (g, u)
+            w_bf[g, u] = keep.tile([P, 2, P, PACK], BF16, name=name, tag=name, align_bytes=64)
+            woven = w_bf[g, u][:].rearrange("p t m j -> p m j t")
+            source = w_raw[g][:].rearrange("p j (m t) -> p m j t", t=PACK)[:, :, :, 2 * u : 2 * u + 2]
+            cut = P - W_VECTOR_COLUMNS if (g, u) == (1, 1) else P
+            nc.scalar.copy(out=woven[:, :cut], in_=source[:, :cut])
+            if cut < P:
+                nc.vector.tensor_copy(out=woven[:, cut:], in_=source[:, cut:])
+
+        def quantise_w(g, u):
+            cols = slice(2 * u * P, 2 * (u + 1) * P)
+            nc.vector.quantize_mx(
+                out=w_codes[g][:, cols].bitcast(FP8X4),
+                scales=w_plane[g][:, cols],
+                in_=w_bf[g, u][:].rearrange("p t m j -> p (t m j)"),
             )
 
-        def quantise_w(g):
-            for t0 in range(0, PACK, 2):
-                cols = slice(t0 * P, (t0 + 2) * P)
-                nc.vector.quantize_mx(
-                    out=w_codes[g][:, cols].bitcast(FP8X4),
-                    scales=w_plane[g][:, cols],
-                    in_=w_bf[g][:, t0 : t0 + 2, :, :].rearrange("p t m j -> p (t m j)"),
-                )
-
-        for g, start, width, raw in x_raw:
+        for g, start, units, raw in x_raw:
             if g == 0:
-                quantise_x(g, start, width, raw)
+                quantise_x(g, start, units, raw)
         picked_0 = gather("picked_0", x_codes[0], U32, 0, S)
-        for g, start, width, raw in x_raw:
+        for g, start, units, raw in x_raw:
             if g == 1:
-                quantise_x(g, start, width, raw)
-        for g, start, raw in w_raw:
-            weave_w(g, start, raw)
+                quantise_x(g, start, units, raw)
+        for g in range(PASSES):
+            for u in range(2):
+                weave_w(g, u)
 
-        picked_plane, picked_1 = [], []
-        for half in range(2):
-            picked_plane.append(gather("picked_plane_%d" % half, x_plane, U8, half * HALF, HALF, "w_bf_0" if half else None))
-            picked_1.append(gather("picked_1_%d" % half, x_codes[1], U32, half * HALF, HALF, "w_raw_0_%d" % (H - W_LOAD) if half else None))
-            quantise_w(half)
+        picked_plane = gather("picked_plane", x_plane, U8, 0, S)
+        quantise_w(0, 0)
+        picked_1 = [gather("picked_1_0", x_codes[1], U32, 0, HALF, "w_bf_0_0")]
+        for g, u in ((0, 1), (1, 0), (1, 1)):
+            quantise_w(g, u)
+        picked_1.append(gather("picked_1_1", x_codes[1], U32, HALF, HALF, "w_raw_1"))
 
         banks = {}
 
-        def first_product(b, g):
-            if g == 0:
+        def first_product(b, g, tiles=range(PACK)):
+            if b not in banks:
                 banks[b] = psum_h.tile([P, PACK, BLOCK], F32, name="h_bank")
             half, local = divmod(b * BLOCK, HALF)
             cols = slice(local, local + BLOCK)
             moving = picked_0[:, b * BLOCK : (b + 1) * BLOCK] if g == 0 else picked_1[half][:, cols]
-            for t in range(PACK):
+            for t in tiles:
                 w_cols = slice(t * P, (t + 1) * P)
                 nc.tensor.matmul_mx(
                     out=banks[b][:, t, :],
                     lhsT=w_codes[g][:, w_cols].bitcast(FP8X4),
                     lhsT_scale=w_plane[g][:, w_cols],
                     rhs=moving.bitcast(FP8X4),
-                    rhs_scale=plane_rows(picked_plane[half], g, cols),
+                    rhs_scale=plane_rows(picked_plane, g, slice(b * BLOCK, (b + 1) * BLOCK)),
                     start=(g == 0 and t == 0),
                     stop=(g == PASSES - 1 and t == PACK - 1),
                 )
@@ -175,13 +184,23 @@ def tile_picked_embpos_none_e_kernel(tc, xT, w1, w2_words, w2_scales, pos, offs,
         def add_pos(b):
             index = group_of[b]
             local = (b - group_of.index(index)) * BLOCK
-            piece, col = divmod(b * BLOCK, POS_LOAD)
-            nc.vector.tensor_tensor(
-                out=h_bf[index][:, local : local + BLOCK, :].rearrange("p (c i) t -> p c t i", i=4),
-                in0=banks[b][:].rearrange("p t (c i) -> p c t i", i=4),
-                in1=pos_sb[piece][:, :, col : col + BLOCK].rearrange("p t (c i) -> p c t i", i=4),
-                op=mybir.AluOpType.add,
-            )
+            woven = h_bf[index][:, local : local + BLOCK, :]
+            if b < GPSIMD_BLOCKS:
+                product = keep.tile([P, BLOCK, PACK], F32, name="product_%d" % b)
+                nc.scalar.copy(out=product[:], in_=banks[b][:].rearrange("p t n -> p n t"))
+                nc.gpsimd.tensor_tensor(
+                    out=woven,
+                    in0=product[:],
+                    in1=pos_sb[b].rearrange("p t n -> p n t"),
+                    op=mybir.AluOpType.add,
+                )
+            else:
+                nc.vector.tensor_tensor(
+                    out=woven.rearrange("p (c i) t -> p c t i", i=4),
+                    in0=banks[b][:].rearrange("p t (c i) -> p c t i", i=4),
+                    in1=pos_sb[b].rearrange("p t (c i) -> p c t i", i=4),
+                    op=mybir.AluOpType.add,
+                )
 
         def second_product(index):
             width = OUT_GROUPS[index] * BLOCK
@@ -207,17 +226,18 @@ def tile_picked_embpos_none_e_kernel(tc, xT, w1, w2_words, w2_scales, pos, offs,
             nc.scalar.copy(out=result[:], in_=acc[:])
             nc.sync.dma_start(out=out[:, start : start + width], in_=result[:])
 
-        for b in range(H_BANKS):
-            first_product(b, 0)
-        waiting = None
+        for tiles in ((0, 1), (2, 3)):
+            for b in range(H_BANKS):
+                first_product(b, 0, tiles)
+        ends = [group_of.index(i) + size - 1 for i, size in enumerate(OUT_GROUPS)]
+        done = 0
         for b in range(BLOCKS):
             if b >= H_BANKS:
                 first_product(b, 0)
             first_product(b, 1)
             add_pos(b)
-            if waiting is not None:
-                second_product(waiting)
-                waiting = None
-            if b + 1 == BLOCKS or group_of[b + 1] != group_of[b]:
-                waiting = group_of[b]
-        second_product(waiting)
+            while done < len(ends) and ends[done] + LAG[done] <= b:
+                second_product(done)
+                done += 1
+        for index in range(done, len(ends)):
+            second_product(index)

@@ -149,12 +149,24 @@ def tile_picked_embpos_none_e_kernel(tc, xT, w1, w2_words, w2_scales, pos, offs,
             for u in range(2):
                 weave_w(g, u)
 
-        picked_plane = gather("picked_plane", x_plane, U8, 0, S)
+        picked_plane = [gather("picked_plane_%d" % half, x_plane, U8, half * HALF, HALF) for half in range(2)]
         quantise_w(0, 0)
         picked_1 = [gather("picked_1_0", x_codes[1], U32, 0, HALF, "w_bf_0_0")]
         for g, u in ((0, 1), (1, 0), (1, 1)):
             quantise_w(g, u)
         picked_1.append(gather("picked_1_1", x_codes[1], U32, HALF, HALF, "w_raw_1"))
+
+        warm = psum_o.tile([P, HALF], F32, name="out_bank")
+        for i in range(4):
+            nc.tensor.matmul_mx(
+                out=warm[:],
+                lhsT=picked_0[:, :P].bitcast(FP8X4),
+                lhsT_scale=picked_plane[0][:, :P],
+                rhs=picked_0[:, :HALF].bitcast(FP8X4),
+                rhs_scale=picked_plane[0][:],
+                start=True,
+                stop=True,
+            )
 
         banks = {}
 
@@ -171,7 +183,7 @@ def tile_picked_embpos_none_e_kernel(tc, xT, w1, w2_words, w2_scales, pos, offs,
                     lhsT=w_codes[g][:, w_cols].bitcast(FP8X4),
                     lhsT_scale=w_plane[g][:, w_cols],
                     rhs=moving.bitcast(FP8X4),
-                    rhs_scale=plane_rows(picked_plane, g, slice(b * BLOCK, (b + 1) * BLOCK)),
+                    rhs_scale=plane_rows(picked_plane[half], g, cols),
                     start=(g == 0 and t == 0),
                     stop=(g == PASSES - 1 and t == PACK - 1),
                 )

@@ -26,7 +26,7 @@ VECTOR_EIGHTHS = ((4, 4, 4, 5, 5), (0, 3, 5, 5, 3))
 POS_LOADS = (640, 384)
 GPSIMD_BLOCKS = 1
 LAG = (1, 1, 1, 1)
-H_BANKS = 5
+H_BANKS = 4
 W_VECTOR_COLUMNS = 64
 OUT_GROUPS = (4, 2, 1, 1)
 
@@ -36,7 +36,7 @@ def tile_picked_embpos_none_e_kernel(tc, xT, w1, w2_words, w2_scales, pos, offs,
     with ExitStack() as ctx:
         keep = ctx.enter_context(tc.tile_pool(name="keep", bufs=1))
         psum_h = ctx.enter_context(tc.psum_pool(name="psum_h", bufs=H_BANKS))
-        psum_o = ctx.enter_context(tc.psum_pool(name="psum_o", bufs=3))
+        psum_o = ctx.enter_context(tc.psum_pool(name="psum_o", bufs=4))
 
         offsets = keep.tile([P, S // 16], U16, name="offsets")
 
@@ -157,7 +157,7 @@ def tile_picked_embpos_none_e_kernel(tc, xT, w1, w2_words, w2_scales, pos, offs,
         picked_1.append(gather("picked_1_1", x_codes[1], U32, HALF, HALF, "w_raw_1"))
 
         warm = psum_o.tile([P, HALF], F32, name="out_bank")
-        for i in range(4):
+        for i in range(3):
             nc.tensor.matmul_mx(
                 out=warm[:],
                 lhsT=picked_0[:, :P].bitcast(FP8X4),

@@ -21,14 +21,17 @@ PASSES = K // K_PASS
 BLOCK = 128
 BLOCKS = S // BLOCK
 HALF = S // 2
-X_LOADS = (((512, 512, 256), (512, 256)), ((256, 512), (512,), (512,), (256,)))
-VECTOR_EIGHTHS = ((4, 4, 4, 5, 5), (0, 3, 5, 5, 3))
-POS_LOADS = (640, 384)
-GPSIMD_BLOCKS = 1
-LAG = (1, 1, 1, 1)
+PAIR_LOADS = ((1024, 1024), (1024, 1024), (1024, 1024), (512, 1024, 512))
+VECTOR_COLUMNS = ((640, 672), (512, 672), (512, 640), (0, 512, 256))
+PIECES = (256, 256, 512)
+SCALAR_JOINS = (2, 0)
+POS_LOADS = (384, 384, 256)
+GPSIMD_BLOCKS = (1,)
 H_BANKS = 4
-W_VECTOR_COLUMNS = 64
+WARM = 3
+W_VECTOR_COLUMNS = 0
 OUT_GROUPS = (4, 2, 1, 1)
+QUANTISE_AFTER = (4, 6, 7, 7)
 
 
 def tile_picked_embpos_none_e_kernel(tc, xT, w1, w2_words, w2_scales, pos, offs, out):
@@ -36,29 +39,28 @@ def tile_picked_embpos_none_e_kernel(tc, xT, w1, w2_words, w2_scales, pos, offs,
     with ExitStack() as ctx:
         keep = ctx.enter_context(tc.tile_pool(name="keep", bufs=1))
         psum_h = ctx.enter_context(tc.psum_pool(name="psum_h", bufs=H_BANKS))
-        psum_o = ctx.enter_context(tc.psum_pool(name="psum_o", bufs=4))
+        psum_o = ctx.enter_context(tc.psum_pool(name="psum_o", bufs=8 - H_BANKS))
 
         offsets = keep.tile([P, S // 16], U16, name="offsets")
-
         w2_codes = keep.tile([P, 2 * N], U8, name="w2_codes", align_bytes=64)
         w2_plane = keep.tile([P, N], U8, name="w2_plane", align_bytes=64)
-        x_plane = keep.tile([P, T], U8, name="x_plane", align_bytes=64)
         nc.gpsimd.memset(w2_plane[:].bitcast(I32), 0)
-        nc.vector.memset(x_plane[:].bitcast(I32), 0)
 
         x_raw = []
-        for g in range(PASSES):
-            rows = xT[g * K_PASS : (g + 1) * K_PASS, :].rearrange("(p j) t -> p j t", j=PACK)
+        for pair in range(2 * PASSES):
+            g, u = divmod(pair, 2)
+            rows = xT[g * K_PASS : (g + 1) * K_PASS, :].rearrange("(p j) t -> p (j t)", j=PACK)[:, 2 * u * T : 2 * (u + 1) * T]
+            raw = keep.tile([P, 2 * T], F32, name="x_raw_%d" % pair, tag="x_raw_%d" % pair, align_bytes=64)
+            loads = []
             start = 0
-            for units in X_LOADS[g]:
-                width = sum(units)
-                raw = keep.tile([P, PACK, width], F32, name="x_raw_%d_%d" % (g, start))
-                nc.sync.dma_start(out=raw[:], in_=rows[:, :, start : start + width])
-                if not x_raw:
-                    nc.sync.dma_start(offsets[:], offs)
-                    nc.sync.dma_start(out=w2_codes[:].bitcast(I32), in_=w2_words[0].bitcast(I32))
-                x_raw.append((g, start, units, raw))
+            for width in PAIR_LOADS[pair]:
+                run = slice(T + start if start else 0, T + start + width)
+                nc.sync.dma_start(out=raw[:, run], in_=rows[:, run])
+                loads.append((start, width, raw[:].rearrange("p (e t) -> p e t", e=2)[:, :, start : start + width]))
                 start += width
+            if pair == 0:
+                nc.sync.dma_start(offsets[:], offs)
+            x_raw.append(loads)
 
         for q in range(4):
             nc.gpsimd.dma_start(
@@ -76,45 +78,50 @@ def tile_picked_embpos_none_e_kernel(tc, xT, w1, w2_words, w2_scales, pos, offs,
         pos_rows = pos.rearrange("(p t) s -> p t s", t=PACK)
         pos_sb = []
         start = 0
-        for width in POS_LOADS:
-            piece = keep.tile([P, PACK, width], F32, name="pos_%d" % start)
+        for i, width in enumerate(POS_LOADS):
+            piece = keep.tile([P, PACK, width], F32, name="pos_%d" % i, tag="pos_%d" % i, align_bytes=64)
             nc.sync.dma_start(out=piece[:], in_=pos_rows[:, :, start : start + width])
             pos_sb.extend(piece[:, :, c : c + BLOCK] for c in range(0, width, BLOCK))
             start += width
+        nc.sync.dma_start(out=w2_codes[:].bitcast(I32), in_=w2_words[0].bitcast(I32))
 
-        x_codes = [keep.tile([P, T], U32, name="x_codes_%d" % g, align_bytes=64) for g in range(PASSES)]
-
-        def plane_rows(plane, g, cols):
-            return plane[4 * g : P, cols]
-
-        shares = [list(s) for s in VECTOR_EIGHTHS]
-
-        def quantise_x(g, start, units, raw):
-            u0 = 0
-            for n in units:
-                grouped = keep.tile([P, n, PACK], BF16, name="x_bf_%d_%d" % (g, start + u0), align_bytes=64)
-                cut = n * shares[g].pop(0) // 8
+        def weave_pair(pair):
+            table = keep.tile([P, T, 2], BF16, name="table_%d" % pair, align_bytes=64)
+            for (start, width, raw), share in zip(x_raw[pair], VECTOR_COLUMNS[pair]):
+                cut = width - share
                 if cut:
-                    nc.vector.tensor_copy(
-                        out=grouped[:, :cut, :].rearrange("p (c i) j -> p c j i", i=4),
-                        in_=raw[:, :, u0 : u0 + cut].rearrange("p j (c i) -> p c j i", i=4),
+                    nc.scalar.copy(
+                        out=table[:, start : start + cut, :].rearrange("p (c i) e -> p c e i", i=4),
+                        in_=raw[:, :, :cut].rearrange("p e (c i) -> p c e i", i=4),
                     )
-                nc.scalar.copy(
-                    out=grouped[:, cut:, :].rearrange("p (c i) j -> p c j i", i=4),
-                    in_=raw[:, :, u0 + cut : u0 + n].rearrange("p j (c i) -> p c j i", i=4),
-                )
-                cols = slice(start + u0, start + u0 + n)
-                nc.vector.quantize_mx(
-                    out=x_codes[g][:, cols].bitcast(FP8X4),
-                    scales=plane_rows(x_plane, g, cols),
-                    in_=grouped[:].rearrange("p n j -> p (n j)"),
-                )
-                u0 += n
+                if share:
+                    nc.vector.tensor_copy(
+                        out=table[:, start + cut : start + width, :].rearrange("p (c i) e -> p c e i", i=4),
+                        in_=raw[:, :, cut:].rearrange("p e (c i) -> p c e i", i=4),
+                    )
+            return table[:].rearrange("p t e -> p (t e)").bitcast(U32)
 
-        def gather(name, window, dtype, start, count, tag=None):
-            picked = keep.tile([P, count], dtype, name=name, tag=tag or name, align_bytes=64)
-            nc.vector.tensor_copy(picked[:], window[:].indirect(offsets[:, start // 16 : (start + count) // 16]))
-            return picked
+        def gather(picked, window, start, count):
+            nc.vector.tensor_copy(picked, window.indirect(offsets[:, start // 16 : (start + count) // 16]))
+
+        x_codes = [keep.tile([P, S], U32, name="x_codes_%d" % g, align_bytes=64) for g in range(PASSES)]
+        x_plane = [keep.tile([P, S], U8, name="x_plane_%d" % g, align_bytes=64) for g in range(PASSES)]
+
+        def join(g, i, picked, start, count):
+            name = "joined_%d_%d" % (g, i)
+            joined = keep.tile([P, count, PACK], BF16, name=name, tag="x_raw_2" if (g, i) == (0, 1) else name, align_bytes=64)
+            words = joined[:].rearrange("p n j -> p (n j)")
+            source = picked[:, :, start : start + count].rearrange("p u n -> p n u")
+            if i < SCALAR_JOINS[g]:
+                nc.scalar.copy(out=words.bitcast(U32).rearrange("p (n u) -> p n u", u=2), in_=source)
+            else:
+                source = picked[:].bitcast(I32)[:, :, start : start + count].rearrange("p u n -> p n u")
+                nc.vector.tensor_copy(out=words.bitcast(I32).rearrange("p (n u) -> p n u", u=2), in_=source)
+            return words
+
+        def quantise_x(g, words, start, count):
+            cols = slice(start, start + count)
+            nc.vector.quantize_mx(out=x_codes[g][:, cols].bitcast(FP8X4), scales=x_plane[g][:, cols], in_=words)
 
         w_codes = [keep.tile([P, H], U32, name="w_codes_%d" % g, align_bytes=64) for g in range(PASSES)]
         w_plane = [keep.tile([P, H], U8, name="w_plane_%d" % g, align_bytes=64) for g in range(PASSES)]
@@ -126,7 +133,8 @@ def tile_picked_embpos_none_e_kernel(tc, xT, w1, w2_words, w2_scales, pos, offs,
             woven = w_bf[g, u][:].rearrange("p t m j -> p m j t")
             source = w_raw[g][:].rearrange("p j (m t) -> p m j t", t=PACK)[:, :, :, 2 * u : 2 * u + 2]
             cut = P - W_VECTOR_COLUMNS if (g, u) == (1, 1) else P
-            nc.scalar.copy(out=woven[:, :cut], in_=source[:, :cut])
+            if cut:
+                nc.scalar.copy(out=woven[:, :cut], in_=source[:, :cut])
             if cut < P:
                 nc.vector.tensor_copy(out=woven[:, cut:], in_=source[:, cut:])
 
@@ -138,32 +146,45 @@ def tile_picked_embpos_none_e_kernel(tc, xT, w1, w2_words, w2_scales, pos, offs,
                 in_=w_bf[g, u][:].rearrange("p t m j -> p (t m j)"),
             )
 
-        for g, start, units, raw in x_raw:
-            if g == 0:
-                quantise_x(g, start, units, raw)
-        picked_0 = gather("picked_0", x_codes[0], U32, 0, S)
-        for g, start, units, raw in x_raw:
-            if g == 1:
-                quantise_x(g, start, units, raw)
+        picked = [keep.tile([P, 2, S], U32, name="picked_%d" % g, align_bytes=64) for g in range(PASSES)]
+        gather(picked[0][:, 0, :], weave_pair(0), 0, S)
+        window = weave_pair(1)
+        for i in range(2):
+            gather(picked[0][:, 1, i * HALF : (i + 1) * HALF], window, i * HALF, HALF)
+        quantise_x(0, join(0, 0, picked[0], 0, HALF), 0, HALF)
+        gather(picked[1][:, 0, :], weave_pair(2), 0, S)
+        quantise_x(0, join(0, 1, picked[0], HALF, HALF), HALF, HALF)
+        window = weave_pair(3)
+        quarter = S // 4
+        joined = []
+        for i in range(5):
+            if i < 4:
+                gather(picked[1][:, 1, i * quarter : (i + 1) * quarter], window, i * quarter, quarter)
+            if 2 <= i:
+                if i < 4:
+                    quantise_x(1, joined[i - 2], (i - 2) * quarter, quarter)
+            if 1 <= i <= 2:
+                joined.append(join(1, i - 1, picked[1], (i - 1) * quarter, quarter))
+        joined.append(join(1, 2, picked[1], HALF, HALF))
+        starts = [0, quarter, HALF]
+
         for g in range(PASSES):
             for u in range(2):
                 weave_w(g, u)
+            for u in range(2):
+                quantise_w(g, u)
 
-        picked_plane = [gather("picked_plane_%d" % half, x_plane, U8, half * HALF, HALF) for half in range(2)]
-        quantise_w(0, 0)
-        picked_1 = [gather("picked_1_0", x_codes[1], U32, 0, HALF, "w_bf_0_0")]
-        for g, u in ((0, 1), (1, 0), (1, 1)):
-            quantise_w(g, u)
-        picked_1.append(gather("picked_1_1", x_codes[1], U32, HALF, HALF, "w_raw_1"))
+        late_codes = keep.tile([P, PIECES[-1]], U32, name="late_codes", tag="w_raw_1", align_bytes=64)
+        nc.vector.quantize_mx(out=late_codes[:].bitcast(FP8X4), scales=x_plane[1][:, starts[-1] :], in_=joined[-1])
 
         warm = psum_o.tile([P, HALF], F32, name="out_bank")
-        for i in range(3):
+        for i in range(WARM):
             nc.tensor.matmul_mx(
                 out=warm[:],
-                lhsT=picked_0[:, :P].bitcast(FP8X4),
-                lhsT_scale=picked_plane[0][:, :P],
-                rhs=picked_0[:, :HALF].bitcast(FP8X4),
-                rhs_scale=picked_plane[0][:],
+                lhsT=x_codes[1][:, :P].bitcast(FP8X4),
+                lhsT_scale=x_plane[1][:, :P],
+                rhs=x_codes[0][:, :HALF].bitcast(FP8X4),
+                rhs_scale=x_plane[0][:, :HALF],
                 start=True,
                 stop=True,
             )
@@ -173,9 +194,10 @@ def tile_picked_embpos_none_e_kernel(tc, xT, w1, w2_words, w2_scales, pos, offs,
         def first_product(b, g, tiles=range(PACK)):
             if b not in banks:
                 banks[b] = psum_h.tile([P, PACK, BLOCK], F32, name="h_bank")
-            half, local = divmod(b * BLOCK, HALF)
-            cols = slice(local, local + BLOCK)
-            moving = picked_0[:, b * BLOCK : (b + 1) * BLOCK] if g == 0 else picked_1[half][:, cols]
+            cols = slice(b * BLOCK, (b + 1) * BLOCK)
+            moving = x_codes[g][:, cols]
+            if g == 1 and cols.start >= starts[-1]:
+                moving = late_codes[:, cols.start - starts[-1] : cols.stop - starts[-1]]
             for t in tiles:
                 w_cols = slice(t * P, (t + 1) * P)
                 nc.tensor.matmul_mx(
@@ -183,7 +205,7 @@ def tile_picked_embpos_none_e_kernel(tc, xT, w1, w2_words, w2_scales, pos, offs,
                     lhsT=w_codes[g][:, w_cols].bitcast(FP8X4),
                     lhsT_scale=w_plane[g][:, w_cols],
                     rhs=moving.bitcast(FP8X4),
-                    rhs_scale=plane_rows(picked_plane[half], g, cols),
+                    rhs_scale=x_plane[g][:, cols],
                     start=(g == 0 and t == 0),
                     stop=(g == PASSES - 1 and t == PACK - 1),
                 )
@@ -197,7 +219,7 @@ def tile_picked_embpos_none_e_kernel(tc, xT, w1, w2_words, w2_scales, pos, offs,
             index = group_of[b]
             local = (b - group_of.index(index)) * BLOCK
             woven = h_bf[index][:, local : local + BLOCK, :]
-            if b < GPSIMD_BLOCKS:
+            if b in GPSIMD_BLOCKS:
                 product = keep.tile([P, BLOCK, PACK], F32, name="product_%d" % b)
                 nc.scalar.copy(out=product[:], in_=banks[b][:].rearrange("p t n -> p n t"))
                 nc.gpsimd.tensor_tensor(
@@ -241,15 +263,12 @@ def tile_picked_embpos_none_e_kernel(tc, xT, w1, w2_words, w2_scales, pos, offs,
         for tiles in ((0, 1), (2, 3)):
             for b in range(H_BANKS):
                 first_product(b, 0, tiles)
-        ends = [group_of.index(i) + size - 1 for i, size in enumerate(OUT_GROUPS)]
         done = 0
         for b in range(BLOCKS):
             if b >= H_BANKS:
                 first_product(b, 0)
             first_product(b, 1)
             add_pos(b)
-            while done < len(ends) and ends[done] + LAG[done] <= b:
+            while done < len(OUT_GROUPS) and QUANTISE_AFTER[done] <= b:
                 second_product(done)
                 done += 1
-        for index in range(done, len(ends)):
-            second_product(index)

@@ -21,15 +21,15 @@ PASSES = K // K_PASS
 BLOCK = 128
 BLOCKS = S // BLOCK
 HALF = S // 2
-PAIR_LOADS = ((1024, 1024), (1024, 1024), (1024, 1024), (512, 1024, 512))
-VECTOR_COLUMNS = ((640, 672), (512, 672), (512, 640), (0, 512, 256))
+PAIR_LOADS = ((1024, 512, 512), (1024, 512, 512), (512, 1024, 512), (512, 1024, 512))
+VECTOR_COLUMNS = ((640, 384, 384), (384, 512, 384), (0, 480, 384), (0, 512, 352))
 PIECES = (256, 256, 512)
 SCALAR_JOINS = (2, 0)
 POS_LOADS = (384, 384, 256)
 GPSIMD_BLOCKS = (1,)
-H_BANKS = 4
+H_BANKS = 5
 WARM = 3
-W_VECTOR_COLUMNS = 0
+W_VECTOR_COLUMNS = 64
 OUT_GROUPS = (4, 2, 1, 1)
 QUANTISE_AFTER = (4, 6, 7, 7)
 
@@ -50,10 +50,17 @@ def tile_picked_embpos_none_e_kernel(tc, xT, w1, w2_words, w2_scales, pos, offs,
         for pair in range(2 * PASSES):
             g, u = divmod(pair, 2)
             rows = xT[g * K_PASS : (g + 1) * K_PASS, :].rearrange("(p j) t -> p (j t)", j=PACK)[:, 2 * u * T : 2 * (u + 1) * T]
-            raw = keep.tile([P, 2 * T], F32, name="x_raw_%d" % pair, tag="x_raw_%d" % pair, align_bytes=64)
+            if pair < 2:
+                raw = keep.tile([P, 2 * T], F32, name="x_raw_%d" % pair)
             loads = []
             start = 0
-            for width in PAIR_LOADS[pair]:
+            for width in PAIR_LOADS[pair] if pair >= 2 else ():
+                name = "x_raw_%d_%d" % (pair, start + width)
+                piece = keep.tile([P, 2, width], F32, name=name, tag=name, align_bytes=64)
+                nc.sync.dma_start(out=piece[:], in_=rows.rearrange("p (e t) -> p e t", e=2)[:, :, start : start + width])
+                loads.append((start, width, piece[:]))
+                start += width
+            for width in PAIR_LOADS[pair] if pair < 2 else ():
                 run = slice(T + start if start else 0, T + start + width)
                 nc.sync.dma_start(out=raw[:, run], in_=rows[:, run])
                 loads.append((start, width, raw[:].rearrange("p (e t) -> p e t", e=2)[:, :, start : start + width]))
@@ -85,7 +92,7 @@ def tile_picked_embpos_none_e_kernel(tc, xT, w1, w2_words, w2_scales, pos, offs,
             start += width
         nc.sync.dma_start(out=w2_codes[:].bitcast(I32), in_=w2_words[0].bitcast(I32))
 
-        def weave_pair(pair):
+        def weave_pair(pair, after_first=None):
             table = keep.tile([P, T, 2], BF16, name="table_%d" % pair, align_bytes=64)
             for (start, width, raw), share in zip(x_raw[pair], VECTOR_COLUMNS[pair]):
                 cut = width - share
@@ -99,6 +106,8 @@ def tile_picked_embpos_none_e_kernel(tc, xT, w1, w2_words, w2_scales, pos, offs,
                         out=table[:, start + cut : start + width, :].rearrange("p (c i) e -> p c e i", i=4),
                         in_=raw[:, :, cut:].rearrange("p e (c i) -> p c e i", i=4),
                     )
+                if after_first and start == 0:
+                    after_first()
             return table[:].rearrange("p t e -> p (t e)").bitcast(U32)
 
         def gather(picked, window, start, count):
@@ -109,7 +118,7 @@ def tile_picked_embpos_none_e_kernel(tc, xT, w1, w2_words, w2_scales, pos, offs,
 
         def join(g, i, picked, start, count):
             name = "joined_%d_%d" % (g, i)
-            joined = keep.tile([P, count, PACK], BF16, name=name, tag="x_raw_2" if (g, i) == (0, 1) else name, align_bytes=64)
+            joined = keep.tile([P, count, PACK], BF16, name=name, tag={(0, 0): "x_raw_2_512", (0, 1): "x_raw_2_2048", (1, 2): "w_raw_0"}.get((g, i), name), align_bytes=64)
             words = joined[:].rearrange("p n j -> p (n j)")
             source = picked[:, :, start : start + count].rearrange("p u n -> p n u")
             if i < SCALAR_JOINS[g]:
@@ -151,8 +160,8 @@ def tile_picked_embpos_none_e_kernel(tc, xT, w1, w2_words, w2_scales, pos, offs,
         window = weave_pair(1)
         for i in range(2):
             gather(picked[0][:, 1, i * HALF : (i + 1) * HALF], window, i * HALF, HALF)
-        quantise_x(0, join(0, 0, picked[0], 0, HALF), 0, HALF)
-        gather(picked[1][:, 0, :], weave_pair(2), 0, S)
+        window = weave_pair(2, lambda: quantise_x(0, join(0, 0, picked[0], 0, HALF), 0, HALF))
+        gather(picked[1][:, 0, :], window, 0, S)
         quantise_x(0, join(0, 1, picked[0], HALF, HALF), HALF, HALF)
         window = weave_pair(3)
         quarter = S // 4
@@ -165,7 +174,6 @@ def tile_picked_embpos_none_e_kernel(tc, xT, w1, w2_words, w2_scales, pos, offs,
                     quantise_x(1, joined[i - 2], (i - 2) * quarter, quarter)
             if 1 <= i <= 2:
                 joined.append(join(1, i - 1, picked[1], (i - 1) * quarter, quarter))
-        joined.append(join(1, 2, picked[1], HALF, HALF))
         starts = [0, quarter, HALF]
 
         for g in range(PASSES):
@@ -173,6 +181,8 @@ def tile_picked_embpos_none_e_kernel(tc, xT, w1, w2_words, w2_scales, pos, offs,
                 weave_w(g, u)
             for u in range(2):
                 quantise_w(g, u)
+            if g == 0:
+                joined.append(join(1, 2, picked[1], HALF, HALF))
 
         late_codes = keep.tile([P, PIECES[-1]], U32, name="late_codes", tag="w_raw_1", align_bytes=64)
         nc.vector.quantize_mx(out=late_codes[:].bitcast(FP8X4), scales=x_plane[1][:, starts[-1] :], in_=joined[-1])

@@ -25,11 +25,12 @@ PAIR_LOADS = ((1024, 512, 512), (1024, 512, 512), (512, 1024, 512), (512, 1024, 
 VECTOR_COLUMNS = ((640, 384, 384), (384, 512, 384), (0, 480, 384), (0, 512, 352))
 PIECES = (256, 256, 512)
 SCALAR_JOINS = (2, 0)
+GPSIMD_JOINS = ((1, 0), (1, 1))
 POS_LOADS = (384, 384, 256)
 GPSIMD_BLOCKS = (1,)
-H_BANKS = 5
-WARM = 3
-W_VECTOR_COLUMNS = 64
+H_BANKS = 4
+WARM = 2
+W_VECTOR_COLUMNS = 32
 OUT_GROUPS = (4, 2, 1, 1)
 QUANTISE_AFTER = (4, 6, 7, 7)
 
@@ -121,7 +122,9 @@ def tile_picked_embpos_none_e_kernel(tc, xT, w1, w2_words, w2_scales, pos, offs,
             joined = keep.tile([P, count, PACK], BF16, name=name, tag={(0, 0): "x_raw_2_512", (0, 1): "x_raw_2_2048", (1, 2): "w_raw_0"}.get((g, i), name), align_bytes=64)
             words = joined[:].rearrange("p n j -> p (n j)")
             source = picked[:, :, start : start + count].rearrange("p u n -> p n u")
-            if i < SCALAR_JOINS[g]:
+            if (g, i) in GPSIMD_JOINS:
+                nc.gpsimd.tensor_copy(out=words.bitcast(U32).rearrange("p (n u) -> p n u", u=2), in_=source)
+            elif i < SCALAR_JOINS[g]:
                 nc.scalar.copy(out=words.bitcast(U32).rearrange("p (n u) -> p n u", u=2), in_=source)
             else:
                 source = picked[:].bitcast(I32)[:, :, start : start + count].rearrange("p u n -> p n u")
@@ -166,14 +169,12 @@ def tile_picked_embpos_none_e_kernel(tc, xT, w1, w2_words, w2_scales, pos, offs,
         window = weave_pair(3)
         quarter = S // 4
         joined = []
-        for i in range(5):
-            if i < 4:
-                gather(picked[1][:, 1, i * quarter : (i + 1) * quarter], window, i * quarter, quarter)
-            if 2 <= i:
-                if i < 4:
-                    quantise_x(1, joined[i - 2], (i - 2) * quarter, quarter)
-            if 1 <= i <= 2:
-                joined.append(join(1, i - 1, picked[1], (i - 1) * quarter, quarter))
+        for i in range(4):
+            gather(picked[1][:, 1, i * quarter : (i + 1) * quarter], window, i * quarter, quarter)
+            if i < 2:
+                joined.append(join(1, i, picked[1], i * quarter, quarter))
+        for i in range(2):
+            quantise_x(1, joined[i], i * quarter, quarter)
         starts = [0, quarter, HALF]
 
         for g in range(PASSES):

@@ -30,9 +30,9 @@ POS_LOADS = (384, 384, 256)
 GPSIMD_BLOCKS = (1,)
 H_BANKS = 4
 WARM = 2
-W_VECTOR_COLUMNS = 32
+W_VECTOR_COLUMNS = 96
 OUT_GROUPS = (4, 2, 1, 1)
-QUANTISE_AFTER = (4, 6, 7, 7)
+QUANTISE_AFTER = (5, 5, 7, 7)
 
 
 def tile_picked_embpos_none_e_kernel(tc, xT, w1, w2_words, w2_scales, pos, offs, out):
@@ -224,14 +224,21 @@ def tile_picked_embpos_none_e_kernel(tc, xT, w1, w2_words, w2_scales, pos, offs,
         group_of = []
         for index, size in enumerate(OUT_GROUPS):
             group_of.extend([index] * size)
-        h_bf = [keep.tile([P, size * BLOCK, PACK], BF16, name="h_bf_%d" % i, align_bytes=64) for i, size in enumerate(OUT_GROUPS)]
+        h_bf = {}
 
         def add_pos(b):
+            first, size = (0, 4) if b < 4 else (b - b % 2, 2)
+            if b == first:
+                tag = "h_bf_%d" % (first % 6)
+                whole = keep.tile([P, size * BLOCK, PACK], BF16, name="h_bf_%d" % first, tag=tag, align_bytes=64)
+                for index in set(group_of[first : first + size]):
+                    local = (group_of.index(index) - first) * BLOCK
+                    h_bf[index] = whole[:, local : local + OUT_GROUPS[index] * BLOCK, :]
             index = group_of[b]
             local = (b - group_of.index(index)) * BLOCK
             woven = h_bf[index][:, local : local + BLOCK, :]
             if b in GPSIMD_BLOCKS:
-                product = keep.tile([P, BLOCK, PACK], F32, name="product_%d" % b)
+                product = keep.tile([P, BLOCK, PACK], F32, name="product", tag="product", align_bytes=64)
                 nc.scalar.copy(out=product[:], in_=banks[b][:].rearrange("p t n -> p n t"))
                 nc.gpsimd.tensor_tensor(
                     out=woven,
@@ -250,12 +257,13 @@ def tile_picked_embpos_none_e_kernel(tc, xT, w1, w2_words, w2_scales, pos, offs,
         def second_product(index):
             width = OUT_GROUPS[index] * BLOCK
             start = group_of.index(index) * BLOCK
-            h_codes = keep.tile([P, width], U32, name="h_codes_%d" % index, align_bytes=64)
+            name = "h_codes_%d" % index
+            h_codes = keep.tile([P, width], U32, name=name, tag="product" if index == 1 else name, align_bytes=64)
             h_plane = keep.tile([P, width], U8, name="h_plane_%d" % index, align_bytes=64)
             nc.vector.quantize_mx(
                 out=h_codes[:].bitcast(FP8X4),
                 scales=h_plane[:],
-                in_=h_bf[index][:].rearrange("p n t -> p (n t)"),
+                in_=h_bf[index].rearrange("p n t -> p (n t)"),
             )
             acc = psum_o.tile([P, width], F32, name="out_bank")
             nc.tensor.matmul_mx(

@@ -21,18 +21,17 @@ PASSES = K // K_PASS
 BLOCK = 128
 BLOCKS = S // BLOCK
 HALF = S // 2
-PAIR_LOADS = ((1024, 512, 512), (1024, 512, 512), (512, 1024, 512), (512, 1024, 512))
-VECTOR_COLUMNS = ((640, 384, 384), (384, 512, 384), (0, 480, 384), (0, 512, 352))
-PIECES = (256, 256, 512)
-SCALAR_JOINS = (2, 0)
-GPSIMD_JOINS = ((1, 0), (1, 1))
+QUARTER = S // 4
+RUN_PAIRS = 4
+PAIR_LOADS = ((1024, 1024), (1024, 512, 512), (512, 1024, 512), (512, 1024, 512))
+VECTOR_COLUMNS = ((640, 672), (384, 512, 384), (0, 640, 384), (0, 576, 352))
 POS_LOADS = (384, 384, 256)
-GPSIMD_BLOCKS = (1,)
+GPSIMD_BLOCK = 1
 H_BANKS = 4
-WARM = 2
+WARM_UPS = 2
 W_VECTOR_COLUMNS = 96
+WALK = 4
 OUT_GROUPS = (4, 2, 1, 1)
-QUANTISE_AFTER = (5, 5, 7, 7)
 
 
 def tile_picked_embpos_none_e_kernel(tc, xT, w1, w2_words, w2_scales, pos, offs, out):
@@ -42,33 +41,38 @@ def tile_picked_embpos_none_e_kernel(tc, xT, w1, w2_words, w2_scales, pos, offs,
         psum_h = ctx.enter_context(tc.psum_pool(name="psum_h", bufs=H_BANKS))
         psum_o = ctx.enter_context(tc.psum_pool(name="psum_o", bufs=8 - H_BANKS))
 
+        def tile(name, shape, dtype, after=None):
+            return keep.tile(shape, dtype, name=name, tag=after or name, align_bytes=64)
+
         offsets = keep.tile([P, S // 16], U16, name="offsets")
-        w2_codes = keep.tile([P, 2 * N], U8, name="w2_codes", align_bytes=64)
-        w2_plane = keep.tile([P, N], U8, name="w2_plane", align_bytes=64)
+        w2_codes = tile("w2_codes", [P, 2 * N], U8)
+        w2_plane = tile("w2_plane", [P, N], U8)
         nc.gpsimd.memset(w2_plane[:].bitcast(I32), 0)
 
         x_raw = []
         for pair in range(2 * PASSES):
             g, u = divmod(pair, 2)
-            rows = xT[g * K_PASS : (g + 1) * K_PASS, :].rearrange("(p j) t -> p (j t)", j=PACK)[:, 2 * u * T : 2 * (u + 1) * T]
-            if pair < 2:
-                raw = keep.tile([P, 2 * T], F32, name="x_raw_%d" % pair)
-            loads = []
+            rows = xT[g * K_PASS : (g + 1) * K_PASS, :].rearrange("(p j) t -> p j t", j=PACK)[:, 2 * u : 2 * u + 2, :]
+            pieces = []
             start = 0
-            for width in PAIR_LOADS[pair] if pair >= 2 else ():
-                name = "x_raw_%d_%d" % (pair, start + width)
-                piece = keep.tile([P, 2, width], F32, name=name, tag=name, align_bytes=64)
-                nc.sync.dma_start(out=piece[:], in_=rows.rearrange("p (e t) -> p e t", e=2)[:, :, start : start + width])
-                loads.append((start, width, piece[:]))
-                start += width
-            for width in PAIR_LOADS[pair] if pair < 2 else ():
-                run = slice(T + start if start else 0, T + start + width)
-                nc.sync.dma_start(out=raw[:, run], in_=rows[:, run])
-                loads.append((start, width, raw[:].rearrange("p (e t) -> p e t", e=2)[:, :, start : start + width]))
-                start += width
+            if pair < RUN_PAIRS:
+                raw = tile("x_raw_%d_%d" % (pair, T), [P, 2, T], F32)
+                for width in PAIR_LOADS[pair]:
+                    run = slice(T + start if start else 0, T + start + width)
+                    nc.sync.dma_start(
+                        out=raw[:].rearrange("p e t -> p (e t)")[:, run], in_=rows.rearrange("p e t -> p (e t)")[:, run]
+                    )
+                    pieces.append(raw[:, :, start : start + width])
+                    start += width
+            else:
+                for width in PAIR_LOADS[pair]:
+                    raw = tile("x_raw_%d_%d" % (pair, start + width), [P, 2, width], F32)
+                    nc.sync.dma_start(out=raw[:], in_=rows[:, :, start : start + width])
+                    pieces.append(raw[:])
+                    start += width
             if pair == 0:
                 nc.sync.dma_start(offsets[:], offs)
-            x_raw.append(loads)
+            x_raw.append(pieces)
 
         for q in range(4):
             nc.gpsimd.dma_start(
@@ -76,125 +80,130 @@ def tile_picked_embpos_none_e_kernel(tc, xT, w1, w2_words, w2_scales, pos, offs,
                 in_=w2_scales[0, 4 * q : 4 * q + 4, :].bitcast(I32),
             )
 
-        w_raw = []
+        w_rows = [w1[g * K_PASS : (g + 1) * K_PASS, :].rearrange("(p j) c -> p j c", j=PACK) for g in range(PASSES)]
+        w_raw = [tile("w_raw_%d" % g, [P, PACK, H], F32) for g in range(PASSES)]
         for g in range(PASSES):
-            rows = w1[g * K_PASS : (g + 1) * K_PASS, :].rearrange("(p j) c -> p j c", j=PACK)
-            raw = keep.tile([P, PACK, H], F32, name="w_raw_%d" % g, tag="w_raw_%d" % g, align_bytes=64)
-            nc.sync.dma_start(out=raw[:], in_=rows)
-            w_raw.append(raw)
+            nc.sync.dma_start(out=w_raw[g][:], in_=w_rows[g])
 
         pos_rows = pos.rearrange("(p t) s -> p t s", t=PACK)
         pos_sb = []
         start = 0
-        for i, width in enumerate(POS_LOADS):
-            piece = keep.tile([P, PACK, width], F32, name="pos_%d" % i, tag="pos_%d" % i, align_bytes=64)
+        for width in POS_LOADS:
+            piece = tile("pos_%d" % start, [P, PACK, width], F32)
             nc.sync.dma_start(out=piece[:], in_=pos_rows[:, :, start : start + width])
             pos_sb.extend(piece[:, :, c : c + BLOCK] for c in range(0, width, BLOCK))
             start += width
         nc.sync.dma_start(out=w2_codes[:].bitcast(I32), in_=w2_words[0].bitcast(I32))
 
-        def weave_pair(pair, after_first=None):
-            table = keep.tile([P, T, 2], BF16, name="table_%d" % pair, align_bytes=64)
-            for (start, width, raw), share in zip(x_raw[pair], VECTOR_COLUMNS[pair]):
-                cut = width - share
-                if cut:
-                    nc.scalar.copy(
-                        out=table[:, start : start + cut, :].rearrange("p (c i) e -> p c e i", i=4),
-                        in_=raw[:, :, :cut].rearrange("p e (c i) -> p c e i", i=4),
-                    )
-                if share:
-                    nc.vector.tensor_copy(
-                        out=table[:, start + cut : start + width, :].rearrange("p (c i) e -> p c e i", i=4),
-                        in_=raw[:, :, cut:].rearrange("p e (c i) -> p c e i", i=4),
-                    )
-                if after_first and start == 0:
-                    after_first()
-            return table[:].rearrange("p t e -> p (t e)").bitcast(U32)
-
-        def gather(picked, window, start, count):
-            nc.vector.tensor_copy(picked, window.indirect(offsets[:, start // 16 : (start + count) // 16]))
-
-        x_codes = [keep.tile([P, S], U32, name="x_codes_%d" % g, align_bytes=64) for g in range(PASSES)]
-        x_plane = [keep.tile([P, S], U8, name="x_plane_%d" % g, align_bytes=64) for g in range(PASSES)]
-
-        def join(g, i, picked, start, count):
-            name = "joined_%d_%d" % (g, i)
-            joined = keep.tile([P, count, PACK], BF16, name=name, tag={(0, 0): "x_raw_2_512", (0, 1): "x_raw_2_2048", (1, 2): "w_raw_0"}.get((g, i), name), align_bytes=64)
-            words = joined[:].rearrange("p n j -> p (n j)")
-            source = picked[:, :, start : start + count].rearrange("p u n -> p n u")
-            if (g, i) in GPSIMD_JOINS:
-                nc.gpsimd.tensor_copy(out=words.bitcast(U32).rearrange("p (n u) -> p n u", u=2), in_=source)
-            elif i < SCALAR_JOINS[g]:
-                nc.scalar.copy(out=words.bitcast(U32).rearrange("p (n u) -> p n u", u=2), in_=source)
-            else:
-                source = picked[:].bitcast(I32)[:, :, start : start + count].rearrange("p u n -> p n u")
-                nc.vector.tensor_copy(out=words.bitcast(I32).rearrange("p (n u) -> p n u", u=2), in_=source)
-            return words
-
-        def quantise_x(g, words, start, count):
-            cols = slice(start, start + count)
-            nc.vector.quantize_mx(out=x_codes[g][:, cols].bitcast(FP8X4), scales=x_plane[g][:, cols], in_=words)
-
-        w_codes = [keep.tile([P, H], U32, name="w_codes_%d" % g, align_bytes=64) for g in range(PASSES)]
-        w_plane = [keep.tile([P, H], U8, name="w_plane_%d" % g, align_bytes=64) for g in range(PASSES)]
-        w_bf = {}
-
-        def weave_w(g, u):
-            name = "w_bf_%d_%d" % (g, u)
-            w_bf[g, u] = keep.tile([P, 2, P, PACK], BF16, name=name, tag=name, align_bytes=64)
-            woven = w_bf[g, u][:].rearrange("p t m j -> p m j t")
-            source = w_raw[g][:].rearrange("p j (m t) -> p m j t", t=PACK)[:, :, :, 2 * u : 2 * u + 2]
-            cut = P - W_VECTOR_COLUMNS if (g, u) == (1, 1) else P
+        def weave_piece(table, pair, index):
+            start = sum(PAIR_LOADS[pair][:index])
+            width = PAIR_LOADS[pair][index]
+            cut = width - VECTOR_COLUMNS[pair][index]
+            raw = x_raw[pair][index]
             if cut:
-                nc.scalar.copy(out=woven[:, :cut], in_=source[:, :cut])
-            if cut < P:
-                nc.vector.tensor_copy(out=woven[:, cut:], in_=source[:, cut:])
+                nc.scalar.copy(
+                    out=table[:, start : start + cut, :].rearrange("p (c i) e -> p c e i", i=4),
+                    in_=raw[:, :, :cut].rearrange("p e (c i) -> p c e i", i=4),
+                )
+            if cut < width:
+                nc.vector.tensor_copy(
+                    out=table[:, start + cut : start + width, :].rearrange("p (c i) e -> p c e i", i=4),
+                    in_=raw[:, :, cut:].rearrange("p e (c i) -> p c e i", i=4),
+                )
 
-        def quantise_w(g, u):
-            cols = slice(2 * u * P, 2 * (u + 1) * P)
-            nc.vector.quantize_mx(
-                out=w_codes[g][:, cols].bitcast(FP8X4),
-                scales=w_plane[g][:, cols],
-                in_=w_bf[g, u][:].rearrange("p t m j -> p (t m j)"),
+        tables = [tile("table_%d" % pair, [P, T, 2], BF16) for pair in range(2 * PASSES)]
+        picked = [tile("picked_%d" % g, [P, 2, S], U32) for g in range(PASSES)]
+
+        def weave_pair(pair, first=0):
+            for index in range(first, len(PAIR_LOADS[pair])):
+                weave_piece(tables[pair], pair, index)
+
+        def gather(pair, start, count):
+            window = tables[pair][:].rearrange("p t e -> p (t e)").bitcast(U32)
+            nc.vector.tensor_copy(
+                picked[pair // 2][:, pair % 2, start : start + count],
+                window.indirect(offsets[:, start // 16 : (start + count) // 16]),
             )
 
-        picked = [keep.tile([P, 2, S], U32, name="picked_%d" % g, align_bytes=64) for g in range(PASSES)]
-        gather(picked[0][:, 0, :], weave_pair(0), 0, S)
-        window = weave_pair(1)
+        def join(copy, g, joined, start, count):
+            copy(
+                out=joined.rearrange("p n j -> p (n j)").bitcast(U32).rearrange("p (n u) -> p n u", u=2),
+                in_=picked[g][:, :, start : start + count].rearrange("p u n -> p n u"),
+            )
+
+        x_plane = [tile("x_plane_%d" % g, [P, S], U8) for g in range(PASSES)]
+        x_codes = [{}, {}]
+
+        def quantise_x(g, codes, joined, start, count):
+            nc.vector.quantize_mx(
+                out=codes.bitcast(FP8X4), scales=x_plane[g][:, start : start + count], in_=joined.rearrange("p n j -> p (n j)")
+            )
+            for c in range(0, count, BLOCK):
+                x_codes[g][(start + c) // BLOCK] = codes[:, c : c + BLOCK]
+
+        weave_pair(0)
+        gather(0, 0, S)
+        weave_pair(1)
+        joined = tile("joined_0_0", [P, HALF, PACK], BF16)
         for i in range(2):
-            gather(picked[0][:, 1, i * HALF : (i + 1) * HALF], window, i * HALF, HALF)
-        window = weave_pair(2, lambda: quantise_x(0, join(0, 0, picked[0], 0, HALF), 0, HALF))
-        gather(picked[1][:, 0, :], window, 0, S)
-        quantise_x(0, join(0, 1, picked[0], HALF, HALF), HALF, HALF)
-        window = weave_pair(3)
-        quarter = S // 4
-        joined = []
+            gather(1, i * QUARTER, QUARTER)
+            join(nc.gpsimd.tensor_copy, 0, joined[:, i * QUARTER : (i + 1) * QUARTER, :], i * QUARTER, QUARTER)
+        gather(1, HALF, HALF)
+        first_codes = tile("x_codes_0", [P, S], U32)
+        quantise_x(0, first_codes[:, :HALF], joined[:], 0, HALF)
+        weave_pair(2)
+        gather(2, 0, S)
+        joined = tile("joined_0_1", [P, HALF, PACK], BF16, "x_raw_2_%d" % T)
+        join(nc.gpsimd.tensor_copy, 0, joined[:], HALF, HALF)
+        quantise_x(0, first_codes[:, HALF:], joined[:], HALF, HALF)
+
+        weave_pair(3)
+        joined = tile("joined_1_0", [P, HALF, PACK], BF16)
         for i in range(4):
-            gather(picked[1][:, 1, i * quarter : (i + 1) * quarter], window, i * quarter, quarter)
+            gather(3, i * QUARTER, QUARTER)
             if i < 2:
-                joined.append(join(1, i, picked[1], i * quarter, quarter))
+                join(nc.gpsimd.tensor_copy, 1, joined[:, i * QUARTER : (i + 1) * QUARTER, :], i * QUARTER, QUARTER)
+        early_codes = tile("x_codes_1_0", [P, HALF], U32)
         for i in range(2):
-            quantise_x(1, joined[i], i * quarter, quarter)
-        starts = [0, quarter, HALF]
+            cols = slice(i * QUARTER, (i + 1) * QUARTER)
+            quantise_x(1, early_codes[:, cols], joined[:, cols, :], i * QUARTER, QUARTER)
 
-        for g in range(PASSES):
-            for u in range(2):
-                weave_w(g, u)
-            for u in range(2):
-                quantise_w(g, u)
-            if g == 0:
-                joined.append(join(1, 2, picked[1], HALF, HALF))
+        w_codes = [tile("w_codes_%d" % g, [P, H], U32) for g in range(PASSES)]
+        w_plane = [tile("w_plane_%d" % g, [P, H], U8) for g in range(PASSES)]
 
-        late_codes = keep.tile([P, PIECES[-1]], U32, name="late_codes", tag="w_raw_1", align_bytes=64)
-        nc.vector.quantize_mx(out=late_codes[:].bitcast(FP8X4), scales=x_plane[1][:, starts[-1] :], in_=joined[-1])
+        def weave_w(g, u):
+            woven = tile("w_bf_%d_%d" % (g, u), [P, 2, P, PACK], BF16)
+            target = woven[:].rearrange("p t m j -> p m j t")
+            source = w_raw[g][:].rearrange("p j (m t) -> p m j t", t=PACK)[:, :, :, 2 * u : 2 * u + 2]
+            cut = P - W_VECTOR_COLUMNS if (g, u) == (1, 1) else P
+            nc.scalar.copy(out=target[:, :cut], in_=source[:, :cut])
+            if cut < P:
+                nc.vector.tensor_copy(out=target[:, cut:], in_=source[:, cut:])
+            return woven
+
+        def weights_of_pass(g):
+            for u, woven in enumerate([weave_w(g, u) for u in range(2)]):
+                cols = slice(2 * u * P, 2 * (u + 1) * P)
+                nc.vector.quantize_mx(
+                    out=w_codes[g][:, cols].bitcast(FP8X4), scales=w_plane[g][:, cols], in_=woven[:].rearrange("p t m j -> p (t m j)")
+                )
+
+        weights_of_pass(0)
+        late = tile("joined_1_1", [P, HALF, PACK], BF16, "w_raw_0")
+        nc.vector.tensor_copy(
+            out=late[:].rearrange("p n j -> p (n j)").bitcast(I32).rearrange("p (n u) -> p n u", u=2),
+            in_=picked[1][:].bitcast(I32)[:, :, HALF:].rearrange("p u n -> p n u"),
+        )
+        weights_of_pass(1)
+        quantise_x(1, tile("x_codes_1_1", [P, HALF], U32, "w_raw_1")[:], late[:], HALF, HALF)
 
         warm = psum_o.tile([P, HALF], F32, name="out_bank")
-        for i in range(WARM):
+        for i in range(WARM_UPS):
             nc.tensor.matmul_mx(
                 out=warm[:],
-                lhsT=x_codes[1][:, :P].bitcast(FP8X4),
+                lhsT=x_codes[1][0].bitcast(FP8X4),
                 lhsT_scale=x_plane[1][:, :P],
-                rhs=x_codes[0][:, :HALF].bitcast(FP8X4),
+                rhs=first_codes[:, :HALF].bitcast(FP8X4),
                 rhs_scale=x_plane[0][:, :HALF],
                 start=True,
                 stop=True,
@@ -205,65 +214,53 @@ def tile_picked_embpos_none_e_kernel(tc, xT, w1, w2_words, w2_scales, pos, offs,
         def first_product(b, g, tiles=range(PACK)):
             if b not in banks:
                 banks[b] = psum_h.tile([P, PACK, BLOCK], F32, name="h_bank")
-            cols = slice(b * BLOCK, (b + 1) * BLOCK)
-            moving = x_codes[g][:, cols]
-            if g == 1 and cols.start >= starts[-1]:
-                moving = late_codes[:, cols.start - starts[-1] : cols.stop - starts[-1]]
             for t in tiles:
                 w_cols = slice(t * P, (t + 1) * P)
                 nc.tensor.matmul_mx(
                     out=banks[b][:, t, :],
                     lhsT=w_codes[g][:, w_cols].bitcast(FP8X4),
                     lhsT_scale=w_plane[g][:, w_cols],
-                    rhs=moving.bitcast(FP8X4),
-                    rhs_scale=x_plane[g][:, cols],
+                    rhs=x_codes[g][b].bitcast(FP8X4),
+                    rhs_scale=x_plane[g][:, b * BLOCK : (b + 1) * BLOCK],
                     start=(g == 0 and t == 0),
                     stop=(g == PASSES - 1 and t == PACK - 1),
                 )
 
-        group_of = []
-        for index, size in enumerate(OUT_GROUPS):
-            group_of.extend([index] * size)
-        h_bf = {}
+        h_early = tile("h_early", [P, 4 * BLOCK, PACK], BF16)
+        h_tiles = {}
+
+        def h_columns(start, width):
+            if start < 4 * BLOCK:
+                return h_early[:, start : start + width, :]
+            first = 4 * BLOCK if start < 6 * BLOCK else 6 * BLOCK
+            if first not in h_tiles:
+                last = 6 * BLOCK if first == 4 * BLOCK else S
+                h_tiles[first] = tile("h_%d" % first, [P, last - first, PACK], BF16, None if first == 4 * BLOCK else "h_early")
+            return h_tiles[first][:, start - first : start - first + width, :]
 
         def add_pos(b):
-            first, size = (0, 4) if b < 4 else (b - b % 2, 2)
-            if b == first:
-                tag = "h_bf_%d" % (first % 6)
-                whole = keep.tile([P, size * BLOCK, PACK], BF16, name="h_bf_%d" % first, tag=tag, align_bytes=64)
-                for index in set(group_of[first : first + size]):
-                    local = (group_of.index(index) - first) * BLOCK
-                    h_bf[index] = whole[:, local : local + OUT_GROUPS[index] * BLOCK, :]
-            index = group_of[b]
-            local = (b - group_of.index(index)) * BLOCK
-            woven = h_bf[index][:, local : local + BLOCK, :]
-            if b in GPSIMD_BLOCKS:
-                product = keep.tile([P, BLOCK, PACK], F32, name="product", tag="product", align_bytes=64)
+            woven_h = h_columns(b * BLOCK, BLOCK)
+            if b == GPSIMD_BLOCK:
+                product = tile("product", [P, BLOCK, PACK], F32)
                 nc.scalar.copy(out=product[:], in_=banks[b][:].rearrange("p t n -> p n t"))
                 nc.gpsimd.tensor_tensor(
-                    out=woven,
-                    in0=product[:],
-                    in1=pos_sb[b].rearrange("p t n -> p n t"),
-                    op=mybir.AluOpType.add,
+                    out=woven_h, in0=product[:], in1=pos_sb[b].rearrange("p t n -> p n t"), op=mybir.AluOpType.add
                 )
             else:
                 nc.vector.tensor_tensor(
-                    out=woven.rearrange("p (c i) t -> p c t i", i=4),
-                    in0=banks[b][:].rearrange("p t (c i) -> p c t i", i=4),
-                    in1=pos_sb[b].rearrange("p t (c i) -> p c t i", i=4),
+                    out=woven_h.rearrange("p (c i) t -> p c t i", i=WALK),
+                    in0=banks[b][:].rearrange("p t (c i) -> p c t i", i=WALK),
+                    in1=pos_sb[b].rearrange("p t (c i) -> p c t i", i=WALK),
                     op=mybir.AluOpType.add,
                 )
 
         def second_product(index):
             width = OUT_GROUPS[index] * BLOCK
-            start = group_of.index(index) * BLOCK
-            name = "h_codes_%d" % index
-            h_codes = keep.tile([P, width], U32, name=name, tag="product" if index == 1 else name, align_bytes=64)
-            h_plane = keep.tile([P, width], U8, name="h_plane_%d" % index, align_bytes=64)
+            start = sum(OUT_GROUPS[:index]) * BLOCK
+            h_codes = tile("h_codes_%d" % index, [P, width], U32, "product" if index == 1 else None)
+            h_plane = tile("h_plane_%d" % index, [P, width], U8)
             nc.vector.quantize_mx(
-                out=h_codes[:].bitcast(FP8X4),
-                scales=h_plane[:],
-                in_=h_bf[index].rearrange("p n t -> p (n t)"),
+                out=h_codes[:].bitcast(FP8X4), scales=h_plane[:], in_=h_columns(start, width).rearrange("p n t -> p (n t)")
             )
             acc = psum_o.tile([P, width], F32, name="out_bank")
             nc.tensor.matmul_mx(
@@ -275,19 +272,17 @@ def tile_picked_embpos_none_e_kernel(tc, xT, w1, w2_words, w2_scales, pos, offs,
                 start=True,
                 stop=True,
             )
-            result = keep.tile([P, width], F32, name="result_%d" % index)
+            result = tile("result_%d" % index, [P, width], F32)
             nc.scalar.copy(out=result[:], in_=acc[:])
             nc.sync.dma_start(out=out[:, start : start + width], in_=result[:])
 
         for tiles in ((0, 1), (2, 3)):
             for b in range(H_BANKS):
                 first_product(b, 0, tiles)
-        done = 0
         for b in range(BLOCKS):
             if b >= H_BANKS:
                 first_product(b, 0)
             first_product(b, 1)
             add_pos(b)
-            while done < len(OUT_GROUPS) and QUANTISE_AFTER[done] <= b:
-                second_product(done)
-                done += 1
+            for index in {5: (0, 1), 7: (2, 3)}.get(b, ()):
+                second_product(index)

@@ -23,8 +23,8 @@ BLOCKS = S // BLOCK
 HALF = S // 2
 QUARTER = S // 4
 RUN_PAIRS = 4
-PAIR_LOADS = ((1024, 1024), (1024, 512, 512), (512, 1024, 512), (512, 1024, 512))
-VECTOR_COLUMNS = ((640, 672), (384, 512, 384), (0, 640, 384), (0, 576, 352))
+PAIR_LOADS = ((1280, 768), (768, 768, 512), (512, 1024, 512), (512, 1024, 512))
+VECTOR_COLUMNS = ((832, 512), (320, 512, 384), (0, 640, 384), (0, 576, 352))
 POS_LOADS = (384, 384, 256)
 GPSIMD_BLOCK = 1
 H_BANKS = 4

@@ -28,7 +28,6 @@ VECTOR_COLUMNS = ((832, 512), (320, 512, 384), (0, 640, 384), (0, 576, 352))
 POS_LOADS = (384, 384, 256)
 GPSIMD_BLOCK = 1
 H_BANKS = 4
-WARM_UPS = 2
 W_VECTOR_COLUMNS = 96
 WALK = 4
 OUT_GROUPS = (4, 2, 1, 1)
@@ -163,10 +162,7 @@ def tile_picked_embpos_none_e_kernel(tc, xT, w1, w2_words, w2_scales, pos, offs,
             gather(3, i * QUARTER, QUARTER)
             if i < 2:
                 join(nc.gpsimd.tensor_copy, 1, joined[:, i * QUARTER : (i + 1) * QUARTER, :], i * QUARTER, QUARTER)
-        early_codes = tile("x_codes_1_0", [P, HALF], U32)
-        for i in range(2):
-            cols = slice(i * QUARTER, (i + 1) * QUARTER)
-            quantise_x(1, early_codes[:, cols], joined[:, cols, :], i * QUARTER, QUARTER)
+        quantise_x(1, tile("x_codes_1_0", [P, QUARTER], U32)[:], joined[:, :QUARTER, :], 0, QUARTER)
 
         w_codes = [tile("w_codes_%d" % g, [P, H], U32) for g in range(PASSES)]
         w_plane = [tile("w_plane_%d" % g, [P, H], U8) for g in range(PASSES)]
@@ -189,6 +185,7 @@ def tile_picked_embpos_none_e_kernel(tc, xT, w1, w2_words, w2_scales, pos, offs,
                 )
 
         weights_of_pass(0)
+        quantise_x(1, tile("x_codes_1_q", [P, QUARTER], U32, "w_bf_0_0")[:], joined[:, QUARTER:, :], QUARTER, QUARTER)
         late = tile("joined_1_1", [P, HALF, PACK], BF16, "w_raw_0")
         nc.vector.tensor_copy(
             out=late[:].rearrange("p n j -> p (n j)").bitcast(I32).rearrange("p (n u) -> p n u", u=2),
@@ -196,18 +193,6 @@ def tile_picked_embpos_none_e_kernel(tc, xT, w1, w2_words, w2_scales, pos, offs,
         )
         weights_of_pass(1)
         quantise_x(1, tile("x_codes_1_1", [P, HALF], U32, "w_raw_1")[:], late[:], HALF, HALF)
-
-        warm = psum_o.tile([P, HALF], F32, name="out_bank")
-        for i in range(WARM_UPS):
-            nc.tensor.matmul_mx(
-                out=warm[:],
-                lhsT=x_codes[1][0].bitcast(FP8X4),
-                lhsT_scale=x_plane[1][:, :P],
-                rhs=first_codes[:, :HALF].bitcast(FP8X4),
-                rhs_scale=x_plane[0][:, :HALF],
-                start=True,
-                stop=True,
-            )
 
         banks = {}
 

@@ -40,6 +40,8 @@ def tile_picked_embpos_none_e_kernel(tc, xT, w1, w2_words, w2_scales, pos, offs,
         psum_h = ctx.enter_context(tc.psum_pool(name="psum_h", bufs=H_BANKS))
         psum_o = ctx.enter_context(tc.psum_pool(name="psum_o", bufs=8 - H_BANKS))
 
+        shared = ctx.enter_context(tc.tile_pool(name="shared", bufs=1))
+
         def tile(name, shape, dtype, after=None):
             return keep.tile(shape, dtype, name=name, tag=after or name, align_bytes=64)
 
@@ -73,12 +75,6 @@ def tile_picked_embpos_none_e_kernel(tc, xT, w1, w2_words, w2_scales, pos, offs,
                 nc.sync.dma_start(offsets[:], offs)
             x_raw.append(pieces)
 
-        for q in range(4):
-            nc.gpsimd.dma_start(
-                out=w2_plane[32 * q : 32 * q + 4, :].bitcast(I32),
-                in_=w2_scales[0, 4 * q : 4 * q + 4, :].bitcast(I32),
-            )
-
         w_rows = [w1[g * K_PASS : (g + 1) * K_PASS, :].rearrange("(p j) c -> p j c", j=PACK) for g in range(PASSES)]
         w_raw = [tile("w_raw_%d" % g, [P, PACK, H], F32) for g in range(PASSES)]
         for g in range(PASSES):
@@ -93,6 +89,11 @@ def tile_picked_embpos_none_e_kernel(tc, xT, w1, w2_words, w2_scales, pos, offs,
             pos_sb.extend(piece[:, :, c : c + BLOCK] for c in range(0, width, BLOCK))
             start += width
         nc.sync.dma_start(out=w2_codes[:].bitcast(I32), in_=w2_words[0].bitcast(I32))
+        for q in range(4):
+            nc.sync.dma_start(
+                out=w2_plane[32 * q : 32 * q + 4, :].bitcast(I32),
+                in_=w2_scales[0, 4 * q : 4 * q + 4, :].bitcast(I32),
+            )
 
         def weave_piece(table, pair, index):
             start = sum(PAIR_LOADS[pair][:index])
@@ -168,7 +169,10 @@ def tile_picked_embpos_none_e_kernel(tc, xT, w1, w2_words, w2_scales, pos, offs,
         w_plane = [tile("w_plane_%d" % g, [P, H], U8) for g in range(PASSES)]
 
         def weave_w(g, u):
-            woven = tile("w_bf_%d_%d" % (g, u), [P, 2, P, PACK], BF16)
+            if (g, u) == (0, 0):
+                woven = shared.tile([P, 2, P, PACK], BF16, name="w_bf_0_0", align_bytes=64, offset=0)
+            else:
+                woven = tile("w_bf_%d_%d" % (g, u), [P, 2, P, PACK], BF16)
             target = woven[:].rearrange("p t m j -> p m j t")
             source = w_raw[g][:].rearrange("p j (m t) -> p m j t", t=PACK)[:, :, :, 2 * u : 2 * u + 2]
             cut = P - W_VECTOR_COLUMNS if (g, u) == (1, 1) else P
@@ -177,21 +181,24 @@ def tile_picked_embpos_none_e_kernel(tc, xT, w1, w2_words, w2_scales, pos, offs,
                 nc.vector.tensor_copy(out=target[:, cut:], in_=source[:, cut:])
             return woven
 
-        def weights_of_pass(g):
-            for u, woven in enumerate([weave_w(g, u) for u in range(2)]):
-                cols = slice(2 * u * P, 2 * (u + 1) * P)
-                nc.vector.quantize_mx(
-                    out=w_codes[g][:, cols].bitcast(FP8X4), scales=w_plane[g][:, cols], in_=woven[:].rearrange("p t m j -> p (t m j)")
-                )
+        def quantise_w(g, u, woven):
+            cols = slice(2 * u * P, 2 * (u + 1) * P)
+            nc.vector.quantize_mx(
+                out=w_codes[g][:, cols].bitcast(FP8X4), scales=w_plane[g][:, cols], in_=woven[:].rearrange("p t m j -> p (t m j)")
+            )
 
-        weights_of_pass(0)
-        quantise_x(1, tile("x_codes_1_q", [P, QUARTER], U32, "w_bf_0_0")[:], joined[:, QUARTER:, :], QUARTER, QUARTER)
-        late = tile("joined_1_1", [P, HALF, PACK], BF16, "w_raw_0")
+        woven = [weave_w(0, u) for u in range(2)]
+        quantise_w(0, 0, woven[0])
+        quantise_x(1, shared.tile([P, QUARTER], U32, name="x_codes_1_q", align_bytes=64, offset=0)[:], joined[:, QUARTER:, :], QUARTER, QUARTER)
+        late = shared.tile([P, HALF, PACK], BF16, name="joined_1_1", align_bytes=64, offset=4 * QUARTER)
         nc.vector.tensor_copy(
             out=late[:].rearrange("p n j -> p (n j)").bitcast(I32).rearrange("p (n u) -> p n u", u=2),
             in_=picked[1][:].bitcast(I32)[:, :, HALF:].rearrange("p u n -> p n u"),
         )
-        weights_of_pass(1)
+        quantise_w(0, 1, woven[1])
+        woven = [weave_w(1, u) for u in range(2)]
+        for u in range(2):
+            quantise_w(1, u, woven[u])
         quantise_x(1, tile("x_codes_1_1", [P, HALF], U32, "w_raw_1")[:], late[:], HALF, HALF)
 
         banks = {}

@@ -13,6 +13,7 @@ U16 = mybir.dt.uint16
 U8 = mybir.dt.uint8
 FP8X4 = mybir.dt.float8_e4m3fn_x4
 FP4X4 = mybir.dt.float4_e2m1fn_x4
+COPY = mybir.ActivationFunctionType.Copy
 
 P = 128
 PACK = 4
@@ -22,25 +23,20 @@ BLOCK = 128
 BLOCKS = S // BLOCK
 HALF = S // 2
 QUARTER = S // 4
-RUN_PAIRS = 4
-PAIR_LOADS = ((1280, 768), (768, 768, 512), (512, 1024, 512), (512, 1024, 512))
-VECTOR_COLUMNS = ((832, 512), (320, 512, 384), (0, 640, 384), (0, 576, 352))
+WALK = 4
 POS_LOADS = (384, 384, 256)
 GPSIMD_BLOCK = 1
-H_BANKS = 4
-W_VECTOR_COLUMNS = 96
-WALK = 4
+W_VECTOR_COLUMNS = (64, 32)
 OUT_GROUPS = (4, 2, 1, 1)
+EARLY = 384
 
 
 def tile_picked_embpos_none_e_kernel(tc, xT, w1, w2_words, w2_scales, pos, offs, out):
     nc = tc.nc
     with ExitStack() as ctx:
         keep = ctx.enter_context(tc.tile_pool(name="keep", bufs=1))
-        psum_h = ctx.enter_context(tc.psum_pool(name="psum_h", bufs=H_BANKS))
-        psum_o = ctx.enter_context(tc.psum_pool(name="psum_o", bufs=8 - H_BANKS))
-
         shared = ctx.enter_context(tc.tile_pool(name="shared", bufs=1))
+        psum = ctx.enter_context(tc.psum_pool(name="psum", bufs=8))
 
         def tile(name, shape, dtype, after=None):
             return keep.tile(shape, dtype, name=name, tag=after or name, align_bytes=64)
@@ -50,35 +46,23 @@ def tile_picked_embpos_none_e_kernel(tc, xT, w1, w2_words, w2_scales, pos, offs,
         w2_plane = tile("w2_plane", [P, N], U8)
         nc.gpsimd.memset(w2_plane[:].bitcast(I32), 0)
 
-        x_raw = []
-        for pair in range(2 * PASSES):
-            g, u = divmod(pair, 2)
-            rows = xT[g * K_PASS : (g + 1) * K_PASS, :].rearrange("(p j) t -> p j t", j=PACK)[:, 2 * u : 2 * u + 2, :]
-            pieces = []
-            start = 0
-            if pair < RUN_PAIRS:
-                raw = tile("x_raw_%d_%d" % (pair, T), [P, 2, T], F32)
-                for width in PAIR_LOADS[pair]:
-                    run = slice(T + start if start else 0, T + start + width)
-                    nc.sync.dma_start(
-                        out=raw[:].rearrange("p e t -> p (e t)")[:, run], in_=rows.rearrange("p e t -> p (e t)")[:, run]
-                    )
-                    pieces.append(raw[:, :, start : start + width])
-                    start += width
-            else:
-                for width in PAIR_LOADS[pair]:
-                    raw = tile("x_raw_%d_%d" % (pair, start + width), [P, 2, width], F32)
-                    nc.sync.dma_start(out=raw[:], in_=rows[:, :, start : start + width])
-                    pieces.append(raw[:])
-                    start += width
-            if pair == 0:
-                nc.sync.dma_start(offsets[:], offs)
-            x_raw.append(pieces)
+        x_raw = [tile("x_raw_%d" % r, [P, T], F32) for r in range(PASSES * PACK)]
+        w_raw = [tile("w_raw_0", [P, PACK, H], F32), shared.tile([P, PACK, H], F32, name="w_raw_1", align_bytes=64, offset=0)]
 
-        w_rows = [w1[g * K_PASS : (g + 1) * K_PASS, :].rearrange("(p j) c -> p j c", j=PACK) for g in range(PASSES)]
-        w_raw = [tile("w_raw_%d" % g, [P, PACK, H], F32) for g in range(PASSES)]
-        for g in range(PASSES):
-            nc.sync.dma_start(out=w_raw[g][:], in_=w_rows[g])
+        def load_x(r):
+            g, j = divmod(r, PACK)
+            nc.sync.dma_start(out=x_raw[r][:], in_=xT[g * K_PASS : (g + 1) * K_PASS, :].rearrange("(p j) t -> p j t", j=PACK)[:, j, :])
+
+        def load_w(g):
+            nc.sync.dma_start(out=w_raw[g][:], in_=w1[g * K_PASS : (g + 1) * K_PASS, :].rearrange("(p j) c -> p j c", j=PACK))
+
+        load_x(0)
+        nc.sync.dma_start(offsets[:], offs)
+        for r in range(1, 7):
+            load_x(r)
+        load_w(0)
+        load_x(7)
+        load_w(1)
 
         pos_rows = pos.rearrange("(p t) s -> p t s", t=PACK)
         pos_sb = []
@@ -95,117 +79,71 @@ def tile_picked_embpos_none_e_kernel(tc, xT, w1, w2_words, w2_scales, pos, offs,
                 in_=w2_scales[0, 4 * q : 4 * q + 4, :].bitcast(I32),
             )
 
-        def weave_piece(table, pair, index):
-            start = sum(PAIR_LOADS[pair][:index])
-            width = PAIR_LOADS[pair][index]
-            cut = width - VECTOR_COLUMNS[pair][index]
-            raw = x_raw[pair][index]
-            if cut:
-                nc.scalar.copy(
-                    out=table[:, start : start + cut, :].rearrange("p (c i) e -> p c e i", i=4),
-                    in_=raw[:, :, :cut].rearrange("p e (c i) -> p c e i", i=4),
-                )
-            if cut < width:
-                nc.vector.tensor_copy(
-                    out=table[:, start + cut : start + width, :].rearrange("p (c i) e -> p c e i", i=4),
-                    in_=raw[:, :, cut:].rearrange("p e (c i) -> p c e i", i=4),
-                )
+        def looked_up(r, start, count):
+            return x_raw[r][:].indirect(offsets[:, start // 16 : (start + count) // 16])
 
-        tables = [tile("table_%d" % pair, [P, T, 2], BF16) for pair in range(2 * PASSES)]
-        picked = [tile("picked_%d" % g, [P, 2, S], U32) for g in range(PASSES)]
+        def gather_vector(target, r, start, count):
+            nc.vector.tensor_copy(target, looked_up(r, start, count))
 
-        def weave_pair(pair, first=0):
-            for index in range(first, len(PAIR_LOADS[pair])):
-                weave_piece(tables[pair], pair, index)
+        def gather_scalar(target, r, start, count):
+            nc.scalar.activation(out=target, in_=looked_up(r, start, count), func=COPY)
 
-        def gather(pair, start, count):
-            window = tables[pair][:].rearrange("p t e -> p (t e)").bitcast(U32)
-            nc.vector.tensor_copy(
-                picked[pair // 2][:, pair % 2, start : start + count],
-                window.indirect(offsets[:, start // 16 : (start + count) // 16]),
-            )
-
-        def join(copy, g, joined, start, count):
-            copy(
-                out=joined.rearrange("p n j -> p (n j)").bitcast(U32).rearrange("p (n u) -> p n u", u=2),
-                in_=picked[g][:, :, start : start + count].rearrange("p u n -> p n u"),
-            )
+        def weave(copy, woven, rows):
+            copy(out=woven.rearrange("p (c i) j -> p c j i", i=WALK), in_=rows.rearrange("p j (c i) -> p c j i", i=WALK))
 
         x_plane = [tile("x_plane_%d" % g, [P, S], U8) for g in range(PASSES)]
         x_codes = [{}, {}]
 
-        def quantise_x(g, codes, joined, start, count):
+        def quantise_x(g, codes, woven, start, count):
             nc.vector.quantize_mx(
-                out=codes.bitcast(FP8X4), scales=x_plane[g][:, start : start + count], in_=joined.rearrange("p n j -> p (n j)")
+                out=codes.bitcast(FP8X4), scales=x_plane[g][:, start : start + count], in_=woven.rearrange("p n j -> p (n j)")
             )
             for c in range(0, count, BLOCK):
                 x_codes[g][(start + c) // BLOCK] = codes[:, c : c + BLOCK]
 
-        weave_pair(0)
-        gather(0, 0, S)
-        weave_pair(1)
-        joined = tile("joined_0_0", [P, HALF, PACK], BF16)
-        for i in range(2):
-            gather(1, i * QUARTER, QUARTER)
-            join(nc.gpsimd.tensor_copy, 0, joined[:, i * QUARTER : (i + 1) * QUARTER, :], i * QUARTER, QUARTER)
-        gather(1, HALF, HALF)
-        first_codes = tile("x_codes_0", [P, S], U32)
-        quantise_x(0, first_codes[:, :HALF], joined[:], 0, HALF)
-        weave_pair(2)
-        gather(2, 0, S)
-        joined = tile("joined_0_1", [P, HALF, PACK], BF16, "x_raw_2_%d" % T)
-        join(nc.gpsimd.tensor_copy, 0, joined[:], HALF, HALF)
-        quantise_x(0, first_codes[:, HALF:], joined[:], HALF, HALF)
-
-        weave_pair(3)
-        joined = tile("joined_1_0", [P, HALF, PACK], BF16)
-        for i in range(4):
-            gather(3, i * QUARTER, QUARTER)
-            if i < 2:
-                join(nc.gpsimd.tensor_copy, 1, joined[:, i * QUARTER : (i + 1) * QUARTER, :], i * QUARTER, QUARTER)
-        quantise_x(1, tile("x_codes_1_0", [P, QUARTER], U32)[:], joined[:, :QUARTER, :], 0, QUARTER)
-
         w_codes = [tile("w_codes_%d" % g, [P, H], U32) for g in range(PASSES)]
         w_plane = [tile("w_plane_%d" % g, [P, H], U8) for g in range(PASSES)]
 
-        def weave_w(g, u):
-            if (g, u) == (0, 0):
-                woven = shared.tile([P, 2, P, PACK], BF16, name="w_bf_0_0", align_bytes=64, offset=0)
-            else:
-                woven = tile("w_bf_%d_%d" % (g, u), [P, 2, P, PACK], BF16)
-            target = woven[:].rearrange("p t m j -> p m j t")
-            source = w_raw[g][:].rearrange("p j (m t) -> p m j t", t=PACK)[:, :, :, 2 * u : 2 * u + 2]
-            cut = P - W_VECTOR_COLUMNS if (g, u) == (1, 1) else P
-            nc.scalar.copy(out=target[:, :cut], in_=source[:, :cut])
-            if cut < P:
-                nc.vector.tensor_copy(out=target[:, cut:], in_=source[:, cut:])
-            return woven
+        def weave_w(g):
+            woven = [tile("w_bf_%d_%d" % (g, u), [P, 2, P, PACK], BF16) for u in range(2)]
+            target = [woven[u][:].rearrange("p t m j -> p m j t") for u in range(2)]
+            source = [w_raw[g][:].rearrange("p j (m t) -> p m j t", t=PACK)[:, :, :, 2 * u : 2 * u + 2] for u in range(2)]
+            cut = P - W_VECTOR_COLUMNS[g]
+            nc.scalar.copy(out=target[1][:, :cut], in_=source[1][:, :cut])
+            nc.vector.tensor_copy(out=target[0], in_=source[0])
+            nc.vector.tensor_copy(out=target[1][:, cut:], in_=source[1][:, cut:])
+            for u in range(2):
+                cols = slice(2 * u * P, 2 * (u + 1) * P)
+                nc.vector.quantize_mx(
+                    out=w_codes[g][:, cols].bitcast(FP8X4), scales=w_plane[g][:, cols], in_=woven[u][:].rearrange("p t m j -> p (t m j)")
+                )
 
-        def quantise_w(g, u, woven):
-            cols = slice(2 * u * P, 2 * (u + 1) * P)
-            nc.vector.quantize_mx(
-                out=w_codes[g][:, cols].bitcast(FP8X4), scales=w_plane[g][:, cols], in_=woven[:].rearrange("p t m j -> p (t m j)")
-            )
+        rows = [tile("rows_0_%d" % i, [P, PACK, HALF], BF16) for i in range(2)]
+        for j in range(PACK):
+            gather_vector(rows[0][:, j, :], j, 0, HALF)
+            gather_scalar(rows[1][:, j, :], j, HALF, HALF)
+        woven = [tile("woven_0_%d" % i, [P, HALF, PACK], BF16) for i in range(2)]
+        first_codes = tile("x_codes_0", [P, S], U32)
+        for i in range(2):
+            weave(nc.vector.tensor_copy, woven[i][:], rows[i][:])
+        for i in range(2):
+            quantise_x(0, first_codes[:, i * HALF : (i + 1) * HALF], woven[i][:], i * HALF, HALF)
 
-        woven = [weave_w(0, u) for u in range(2)]
-        quantise_w(0, 0, woven[0])
-        quantise_x(1, shared.tile([P, QUARTER], U32, name="x_codes_1_q", align_bytes=64, offset=0)[:], joined[:, QUARTER:, :], QUARTER, QUARTER)
-        late = shared.tile([P, HALF, PACK], BF16, name="joined_1_1", align_bytes=64, offset=4 * QUARTER)
-        nc.vector.tensor_copy(
-            out=late[:].rearrange("p n j -> p (n j)").bitcast(I32).rearrange("p (n u) -> p n u", u=2),
-            in_=picked[1][:].bitcast(I32)[:, :, HALF:].rearrange("p u n -> p n u"),
-        )
-        quantise_w(0, 1, woven[1])
-        woven = [weave_w(1, u) for u in range(2)]
-        for u in range(2):
-            quantise_w(1, u, woven[u])
-        quantise_x(1, tile("x_codes_1_1", [P, HALF], U32, "w_raw_1")[:], late[:], HALF, HALF)
+        rows = [tile("rows_1_%d" % i, [P, PACK - 1, HALF], BF16) for i in range(2)]
+        for j in range(PACK - 1):
+            (gather_vector if j else gather_scalar)(rows[0][:, j, :], PACK + j, 0, HALF)
+            gather_scalar(rows[1][:, j, :], PACK + j, HALF, HALF)
+        woven_vector = tile("woven_1_vector", [P, HALF, PACK], BF16)
+        woven_early = tile("woven_1_early", [P, EARLY, PACK], BF16)
+        woven_late = tile("woven_1_late", [P, HALF - EARLY, PACK], BF16)
+        weave(nc.vector.tensor_copy, woven_vector[:, :, : PACK - 1], rows[0][:])
+        weave(nc.scalar.copy, woven_early[:, :, : PACK - 1], rows[1][:, :, :EARLY])
+        weave(nc.scalar.copy, woven_late[:, :, : PACK - 1], rows[1][:, :, EARLY:])
+        weave_w(0)
 
-        banks = {}
+        banks = [psum.tile([P, PACK, BLOCK], F32, name="bank") for b in range(BLOCKS)]
 
         def first_product(b, g, tiles=range(PACK)):
-            if b not in banks:
-                banks[b] = psum_h.tile([P, PACK, BLOCK], F32, name="h_bank")
             for t in tiles:
                 w_cols = slice(t * P, (t + 1) * P)
                 nc.tensor.matmul_mx(
@@ -218,6 +156,27 @@ def tile_picked_embpos_none_e_kernel(tc, xT, w1, w2_words, w2_scales, pos, offs,
                     stop=(g == PASSES - 1 and t == PACK - 1),
                 )
 
+        for b in range(BLOCKS):
+            first_product(b, 0)
+
+        last = PASSES * PACK - 1
+        for i in range(2):
+            gather_vector(woven_vector[:, i * QUARTER : (i + 1) * QUARTER, PACK - 1], last, i * QUARTER, QUARTER)
+        last_early = tile("last_early", [P, EARLY], BF16)
+        gather_scalar(last_early[:], last, HALF, EARLY)
+        nc.scalar.copy(out=woven_early[:, :, PACK - 1], in_=last_early[:])
+        second_codes = tile("x_codes_1", [P, HALF], U32)
+        for i in range(2):
+            part = slice(i * QUARTER, (i + 1) * QUARTER)
+            quantise_x(1, second_codes[:, part], woven_vector[:, part, :], i * QUARTER, QUARTER)
+        weave_w(1)
+        last_late = shared.tile([P, HALF - EARLY], BF16, name="last_late", align_bytes=64, offset=0)
+        gather_scalar(last_late[:], last, HALF + EARLY, HALF - EARLY)
+        nc.scalar.copy(out=woven_late[:, :, PACK - 1], in_=last_late[:])
+        early_codes = shared.tile([P, EARLY], U32, name="x_codes_1_early", align_bytes=64, offset=1024)
+        quantise_x(1, early_codes[:], woven_early[:], HALF, EARLY)
+        quantise_x(1, tile("x_codes_1_late", [P, HALF - EARLY], U32)[:], woven_late[:], HALF + EARLY, HALF - EARLY)
+
         h_early = tile("h_early", [P, 4 * BLOCK, PACK], BF16)
         h_tiles = {}
 
@@ -226,8 +185,8 @@ def tile_picked_embpos_none_e_kernel(tc, xT, w1, w2_words, w2_scales, pos, offs,
                 return h_early[:, start : start + width, :]
             first = 4 * BLOCK if start < 6 * BLOCK else 6 * BLOCK
             if first not in h_tiles:
-                last = 6 * BLOCK if first == 4 * BLOCK else S
-                h_tiles[first] = tile("h_%d" % first, [P, last - first, PACK], BF16, None if first == 4 * BLOCK else "h_early")
+                end = 6 * BLOCK if first == 4 * BLOCK else S
+                h_tiles[first] = tile("h_%d" % first, [P, end - first, PACK], BF16, None if first == 4 * BLOCK else "h_early")
             return h_tiles[first][:, start - first : start - first + width, :]
 
         def add_pos(b):
@@ -254,7 +213,7 @@ def tile_picked_embpos_none_e_kernel(tc, xT, w1, w2_words, w2_scales, pos, offs,
             nc.vector.quantize_mx(
                 out=h_codes[:].bitcast(FP8X4), scales=h_plane[:], in_=h_columns(start, width).rearrange("p n t -> p (n t)")
             )
-            acc = psum_o.tile([P, width], F32, name="out_bank")
+            acc = psum.tile([P, width], F32, name="acc", tag="bank")
             nc.tensor.matmul_mx(
                 out=acc[:],
                 lhsT=w2_codes[:].bitcast(FP4X4),
@@ -268,12 +227,7 @@ def tile_picked_embpos_none_e_kernel(tc, xT, w1, w2_words, w2_scales, pos, offs,
             nc.scalar.copy(out=result[:], in_=acc[:])
             nc.sync.dma_start(out=out[:, start : start + width], in_=result[:])
 
-        for tiles in ((0, 1), (2, 3)):
-            for b in range(H_BANKS):
-                first_product(b, 0, tiles)
         for b in range(BLOCKS):
-            if b >= H_BANKS:
-                first_product(b, 0)
             first_product(b, 1)
             add_pos(b)
             for index in {5: (0, 1), 7: (2, 3)}.get(b, ()):

@@ -26,17 +26,17 @@ QUARTER = S // 4
 WALK = 4
 POS_LOADS = (384, 384, 256)
 GPSIMD_BLOCK = 1
-W_VECTOR_COLUMNS = (64, 32)
+H_BANKS = 4
+W_VECTOR_COLUMNS = (32, 32)
 OUT_GROUPS = (4, 2, 1, 1)
-EARLY = 384
 
 
 def tile_picked_embpos_none_e_kernel(tc, xT, w1, w2_words, w2_scales, pos, offs, out):
     nc = tc.nc
     with ExitStack() as ctx:
         keep = ctx.enter_context(tc.tile_pool(name="keep", bufs=1))
-        shared = ctx.enter_context(tc.tile_pool(name="shared", bufs=1))
-        psum = ctx.enter_context(tc.psum_pool(name="psum", bufs=8))
+        psum_h = ctx.enter_context(tc.psum_pool(name="psum_h", bufs=H_BANKS))
+        psum_o = ctx.enter_context(tc.psum_pool(name="psum_o", bufs=8 - H_BANKS))
 
         def tile(name, shape, dtype, after=None):
             return keep.tile(shape, dtype, name=name, tag=after or name, align_bytes=64)
@@ -47,7 +47,7 @@ def tile_picked_embpos_none_e_kernel(tc, xT, w1, w2_words, w2_scales, pos, offs,
         nc.gpsimd.memset(w2_plane[:].bitcast(I32), 0)
 
         x_raw = [tile("x_raw_%d" % r, [P, T], F32) for r in range(PASSES * PACK)]
-        w_raw = [tile("w_raw_0", [P, PACK, H], F32), shared.tile([P, PACK, H], F32, name="w_raw_1", align_bytes=64, offset=0)]
+        w_raw = [tile("w_raw_0", [P, PACK, H], F32), tile("w_raw_1", [P, PACK, H], F32)]
 
         def load_x(r):
             g, j = divmod(r, PACK)
@@ -58,11 +58,10 @@ def tile_picked_embpos_none_e_kernel(tc, xT, w1, w2_words, w2_scales, pos, offs,
 
         load_x(0)
         nc.sync.dma_start(offsets[:], offs)
-        for r in range(1, 7):
+        for r in range(1, PASSES * PACK):
             load_x(r)
-        load_w(0)
-        load_x(7)
-        load_w(1)
+        for g in range(PASSES):
+            load_w(g)
 
         pos_rows = pos.rearrange("(p t) s -> p t s", t=PACK)
         pos_sb = []
@@ -111,39 +110,63 @@ def tile_picked_embpos_none_e_kernel(tc, xT, w1, w2_words, w2_scales, pos, offs,
             cut = P - W_VECTOR_COLUMNS[g]
             nc.scalar.copy(out=target[1][:, :cut], in_=source[1][:, :cut])
             nc.vector.tensor_copy(out=target[0], in_=source[0])
-            nc.vector.tensor_copy(out=target[1][:, cut:], in_=source[1][:, cut:])
+            if cut < P:
+                nc.vector.tensor_copy(out=target[1][:, cut:], in_=source[1][:, cut:])
             for u in range(2):
                 cols = slice(2 * u * P, 2 * (u + 1) * P)
                 nc.vector.quantize_mx(
                     out=w_codes[g][:, cols].bitcast(FP8X4), scales=w_plane[g][:, cols], in_=woven[u][:].rearrange("p t m j -> p (t m j)")
                 )
 
-        rows = [tile("rows_0_%d" % i, [P, PACK, HALF], BF16) for i in range(2)]
-        for j in range(PACK):
-            gather_vector(rows[0][:, j, :], j, 0, HALF)
-            gather_scalar(rows[1][:, j, :], j, HALF, HALF)
-        woven = [tile("woven_0_%d" % i, [P, HALF, PACK], BF16) for i in range(2)]
+        def halves(name, shape, dtype):
+            return [tile("%s_%d" % (name, i), shape, dtype) for i in range(2)]
+
+        def gather_pair(name, first):
+            rows = halves(name, [P, 2, HALF], BF16)
+            for e in range(2):
+                gather_vector(rows[0][:, e, :], first + e, 0, HALF)
+                gather_scalar(rows[1][:, e, :], first + e, HALF, HALF)
+            return rows
+
+        woven = halves("woven_0", [P, HALF, PACK], BF16)
         first_codes = tile("x_codes_0", [P, S], U32)
-        for i in range(2):
-            weave(nc.vector.tensor_copy, woven[i][:], rows[i][:])
+        for u in range(2):
+            rows = gather_pair("rows_0_%d" % u, 2 * u)
+            for i in range(2):
+                weave(nc.vector.tensor_copy, woven[i][:, :, 2 * u : 2 * u + 2], rows[i][:])
         for i in range(2):
             quantise_x(0, first_codes[:, i * HALF : (i + 1) * HALF], woven[i][:], i * HALF, HALF)
 
-        rows = [tile("rows_1_%d" % i, [P, PACK - 1, HALF], BF16) for i in range(2)]
-        for j in range(PACK - 1):
-            (gather_vector if j else gather_scalar)(rows[0][:, j, :], PACK + j, 0, HALF)
-            gather_scalar(rows[1][:, j, :], PACK + j, HALF, HALF)
-        woven_vector = tile("woven_1_vector", [P, HALF, PACK], BF16)
-        woven_early = tile("woven_1_early", [P, EARLY, PACK], BF16)
-        woven_late = tile("woven_1_late", [P, HALF - EARLY, PACK], BF16)
-        weave(nc.vector.tensor_copy, woven_vector[:, :, : PACK - 1], rows[0][:])
-        weave(nc.scalar.copy, woven_early[:, :, : PACK - 1], rows[1][:, :, :EARLY])
-        weave(nc.scalar.copy, woven_late[:, :, : PACK - 1], rows[1][:, :, EARLY:])
-        weave_w(0)
+        woven = halves("woven_1", [P, HALF, PACK], BF16)
+        rows = halves("rows_1_0", [P, 2, HALF], BF16)
+        for e in range(2):
+            (gather_vector if e else gather_scalar)(rows[0][:, e, :], PACK + e, 0, HALF)
+            gather_scalar(rows[1][:, e, :], PACK + e, HALF, HALF)
+        weave(nc.vector.tensor_copy, woven[0][:, :, :2], rows[0][:])
+        weave(nc.vector.tensor_copy, woven[1][:, :QUARTER, :2], rows[1][:, :, :QUARTER])
+        weave(nc.scalar.copy, woven[1][:, QUARTER:, :2], rows[1][:, :, QUARTER:])
+        rows = [tile("rows_1_1_%d" % i, [P, 2, QUARTER], BF16) for i in range(4)]
+        for i in range(4):
+            (gather_scalar if i // 2 else gather_vector)(rows[i][:, 0, :], PACK + 2, i * QUARTER, QUARTER)
+        for i in range(4):
+            (gather_scalar if i else gather_vector)(rows[i][:, 1, :], PACK + 3, i * QUARTER, QUARTER)
+        quarters = [woven[i // 2][:, i % 2 * QUARTER : (i % 2 + 1) * QUARTER, :] for i in range(4)]
+        weave(nc.scalar.copy, quarters[3][:, :, 2:], rows[3][:])
+        second_codes = tile("x_codes_1_0", [P, HALF], U32)
+        for i in range(2):
+            weave(nc.vector.tensor_copy, quarters[i][:, :, 2:], rows[i][:])
+        quantise_x(1, second_codes[:, :QUARTER], quarters[0], 0, QUARTER)
+        weave(nc.vector.tensor_copy, quarters[2][:, :, 2:], rows[2][:])
+        quantise_x(1, second_codes[:, QUARTER:], quarters[1], QUARTER, QUARTER)
+        for g in range(PASSES):
+            weave_w(g)
+        quantise_x(1, tile("x_codes_1_1", [P, HALF], U32, "w_raw_1")[:], woven[1][:], HALF, HALF)
 
-        banks = [psum.tile([P, PACK, BLOCK], F32, name="bank") for b in range(BLOCKS)]
+        banks = {}
 
         def first_product(b, g, tiles=range(PACK)):
+            if b not in banks:
+                banks[b] = psum_h.tile([P, PACK, BLOCK], F32, name="h_bank")
             for t in tiles:
                 w_cols = slice(t * P, (t + 1) * P)
                 nc.tensor.matmul_mx(
@@ -155,27 +178,6 @@ def tile_picked_embpos_none_e_kernel(tc, xT, w1, w2_words, w2_scales, pos, offs,
                     start=(g == 0 and t == 0),
                     stop=(g == PASSES - 1 and t == PACK - 1),
                 )
-
-        for b in range(BLOCKS):
-            first_product(b, 0)
-
-        last = PASSES * PACK - 1
-        for i in range(2):
-            gather_vector(woven_vector[:, i * QUARTER : (i + 1) * QUARTER, PACK - 1], last, i * QUARTER, QUARTER)
-        last_early = tile("last_early", [P, EARLY], BF16)
-        gather_scalar(last_early[:], last, HALF, EARLY)
-        nc.scalar.copy(out=woven_early[:, :, PACK - 1], in_=last_early[:])
-        second_codes = tile("x_codes_1", [P, HALF], U32)
-        for i in range(2):
-            part = slice(i * QUARTER, (i + 1) * QUARTER)
-            quantise_x(1, second_codes[:, part], woven_vector[:, part, :], i * QUARTER, QUARTER)
-        weave_w(1)
-        last_late = shared.tile([P, HALF - EARLY], BF16, name="last_late", align_bytes=64, offset=0)
-        gather_scalar(last_late[:], last, HALF + EARLY, HALF - EARLY)
-        nc.scalar.copy(out=woven_late[:, :, PACK - 1], in_=last_late[:])
-        early_codes = shared.tile([P, EARLY], U32, name="x_codes_1_early", align_bytes=64, offset=1024)
-        quantise_x(1, early_codes[:], woven_early[:], HALF, EARLY)
-        quantise_x(1, tile("x_codes_1_late", [P, HALF - EARLY], U32)[:], woven_late[:], HALF + EARLY, HALF - EARLY)
 
         h_early = tile("h_early", [P, 4 * BLOCK, PACK], BF16)
         h_tiles = {}
@@ -213,7 +215,7 @@ def tile_picked_embpos_none_e_kernel(tc, xT, w1, w2_words, w2_scales, pos, offs,
             nc.vector.quantize_mx(
                 out=h_codes[:].bitcast(FP8X4), scales=h_plane[:], in_=h_columns(start, width).rearrange("p n t -> p (n t)")
             )
-            acc = psum.tile([P, width], F32, name="acc", tag="bank")
+            acc = psum_o.tile([P, width], F32, name="out_bank")
             nc.tensor.matmul_mx(
                 out=acc[:],
                 lhsT=w2_codes[:].bitcast(FP4X4),
@@ -227,7 +229,12 @@ def tile_picked_embpos_none_e_kernel(tc, xT, w1, w2_words, w2_scales, pos, offs,
             nc.scalar.copy(out=result[:], in_=acc[:])
             nc.sync.dma_start(out=out[:, start : start + width], in_=result[:])
 
+        for tiles in ((0, 1), (2, 3)):
+            for b in range(H_BANKS):
+                first_product(b, 0, tiles)
         for b in range(BLOCKS):
+            if b >= H_BANKS:
+                first_product(b, 0)
             first_product(b, 1)
             add_pos(b)
             for index in {5: (0, 1), 7: (2, 3)}.get(b, ()):

@@ -121,42 +121,38 @@ def tile_picked_embpos_none_e_kernel(tc, xT, w1, w2_words, w2_scales, pos, offs,
         def halves(name, shape, dtype):
             return [tile("%s_%d" % (name, i), shape, dtype) for i in range(2)]
 
-        def gather_pair(name, first):
-            rows = halves(name, [P, 2, HALF], BF16)
-            for e in range(2):
-                gather_vector(rows[0][:, e, :], first + e, 0, HALF)
-                gather_scalar(rows[1][:, e, :], first + e, HALF, HALF)
-            return rows
+        def gather_row(rows, e, r, vector_entries):
+            gather_vector(rows[:, e, :vector_entries], r, 0, vector_entries)
+            gather_scalar(rows[:, e, vector_entries:], r, vector_entries, S - vector_entries)
 
+        rows = tile("rows_0", [P, PACK, S], BF16)
+        for j in range(PACK):
+            gather_row(rows, j, j, HALF if j < 2 else BLOCK)
         woven = halves("woven_0", [P, HALF, PACK], BF16)
         first_codes = tile("x_codes_0", [P, S], U32)
-        for u in range(2):
-            rows = gather_pair("rows_0_%d" % u, 2 * u)
-            for i in range(2):
-                weave(nc.vector.tensor_copy, woven[i][:, :, 2 * u : 2 * u + 2], rows[i][:])
+        for i in range(2):
+            weave(nc.vector.tensor_copy, woven[i][:], rows[:, :, i * HALF : (i + 1) * HALF])
         for i in range(2):
             quantise_x(0, first_codes[:, i * HALF : (i + 1) * HALF], woven[i][:], i * HALF, HALF)
 
         woven = halves("woven_1", [P, HALF, PACK], BF16)
-        rows = halves("rows_1_0", [P, 2, HALF], BF16)
+        rows = tile("rows_1_0", [P, 2, S], BF16)
         for e in range(2):
-            (gather_vector if e else gather_scalar)(rows[0][:, e, :], PACK + e, 0, HALF)
-            gather_scalar(rows[1][:, e, :], PACK + e, HALF, HALF)
-        weave(nc.vector.tensor_copy, woven[0][:, :, :2], rows[0][:])
-        weave(nc.vector.tensor_copy, woven[1][:, :QUARTER, :2], rows[1][:, :, :QUARTER])
-        weave(nc.scalar.copy, woven[1][:, QUARTER:, :2], rows[1][:, :, QUARTER:])
-        rows = [tile("rows_1_1_%d" % i, [P, 2, QUARTER], BF16) for i in range(4)]
-        for i in range(4):
-            (gather_scalar if i // 2 else gather_vector)(rows[i][:, 0, :], PACK + 2, i * QUARTER, QUARTER)
+            gather_row(rows, e, PACK + e, BLOCK)
+        for i in range(2):
+            weave(nc.vector.tensor_copy, woven[i][:, :, :2], rows[:, :, i * HALF : (i + 1) * HALF])
+        last_rows = tile("rows_1_1", [P, 2, S], BF16)
+        gather_row(last_rows, 0, PACK + 2, BLOCK)
+        rows = [last_rows[:, :, i * QUARTER : (i + 1) * QUARTER] for i in range(4)]
         for i in range(4):
             (gather_scalar if i else gather_vector)(rows[i][:, 1, :], PACK + 3, i * QUARTER, QUARTER)
         quarters = [woven[i // 2][:, i % 2 * QUARTER : (i % 2 + 1) * QUARTER, :] for i in range(4)]
-        weave(nc.scalar.copy, quarters[3][:, :, 2:], rows[3][:])
+        weave(nc.scalar.copy, quarters[3][:, :, 2:], rows[3])
         second_codes = tile("x_codes_1_0", [P, HALF], U32)
         for i in range(2):
-            weave(nc.vector.tensor_copy, quarters[i][:, :, 2:], rows[i][:])
+            weave(nc.vector.tensor_copy, quarters[i][:, :, 2:], rows[i])
         quantise_x(1, second_codes[:, :QUARTER], quarters[0], 0, QUARTER)
-        weave(nc.vector.tensor_copy, quarters[2][:, :, 2:], rows[2][:])
+        weave(nc.vector.tensor_copy, quarters[2][:, :, 2:], rows[2])
         quantise_x(1, second_codes[:, QUARTER:], quarters[1], QUARTER, QUARTER)
         for g in range(PASSES):
             weave_w(g)

@@ -25,10 +25,10 @@ HALF = S // 2
 QUARTER = S // 4
 WALK = 4
 POS_LOADS = (384, 384, 256)
-GPSIMD_BLOCK = 1
+GPSIMD_BLOCK = 3
 H_BANKS = 4
 W_VECTOR_COLUMNS = (32, 32)
-OUT_GROUPS = (4, 2, 1, 1)
+OUT_GROUPS = (2, 1, 4, 1)
 
 
 def tile_picked_embpos_none_e_kernel(tc, xT, w1, w2_words, w2_scales, pos, offs, out):
@@ -175,55 +175,56 @@ def tile_picked_embpos_none_e_kernel(tc, xT, w1, w2_words, w2_scales, pos, offs,
                     stop=(g == PASSES - 1 and t == PACK - 1),
                 )
 
-        h_early = tile("h_early", [P, 4 * BLOCK, PACK], BF16)
-        h_tiles = {}
-
-        def h_columns(start, width):
-            if start < 4 * BLOCK:
-                return h_early[:, start : start + width, :]
-            first = 4 * BLOCK if start < 6 * BLOCK else 6 * BLOCK
-            if first not in h_tiles:
-                end = 6 * BLOCK if first == 4 * BLOCK else S
-                h_tiles[first] = tile("h_%d" % first, [P, end - first, PACK], BF16, None if first == 4 * BLOCK else "h_early")
-            return h_tiles[first][:, start - first : start - first + width, :]
+        h_tiles = [
+            tile("h_%d" % index, [P, width * BLOCK, PACK], BF16, "h_0" if index == 2 else None) for index, width in enumerate(OUT_GROUPS)
+        ]
+        h_blocks = [h_tiles[index][:, c * BLOCK : (c + 1) * BLOCK, :] for index, width in enumerate(OUT_GROUPS) for c in range(width)]
 
         def add_pos(b):
-            woven_h = h_columns(b * BLOCK, BLOCK)
             if b == GPSIMD_BLOCK:
                 product = tile("product", [P, BLOCK, PACK], F32)
                 nc.scalar.copy(out=product[:], in_=banks[b][:].rearrange("p t n -> p n t"))
                 nc.gpsimd.tensor_tensor(
-                    out=woven_h, in0=product[:], in1=pos_sb[b].rearrange("p t n -> p n t"), op=mybir.AluOpType.add
+                    out=h_blocks[b], in0=product[:], in1=pos_sb[b].rearrange("p t n -> p n t"), op=mybir.AluOpType.add
                 )
             else:
                 nc.vector.tensor_tensor(
-                    out=woven_h.rearrange("p (c i) t -> p c t i", i=WALK),
+                    out=h_blocks[b].rearrange("p (c i) t -> p c t i", i=WALK),
                     in0=banks[b][:].rearrange("p t (c i) -> p c t i", i=WALK),
                     in1=pos_sb[b].rearrange("p t (c i) -> p c t i", i=WALK),
                     op=mybir.AluOpType.add,
                 )
 
-        def second_product(index):
-            width = OUT_GROUPS[index] * BLOCK
+        h_codes = tile("h_codes", [P, S], U32)
+        h_plane = tile("h_plane", [P, S], U8)
+        result = tile("result", [P, S], F32)
+
+        def quantise_h(index):
             start = sum(OUT_GROUPS[:index]) * BLOCK
-            h_codes = tile("h_codes_%d" % index, [P, width], U32, "product" if index == 1 else None)
-            h_plane = tile("h_plane_%d" % index, [P, width], U8)
+            cols = slice(start, start + OUT_GROUPS[index] * BLOCK)
             nc.vector.quantize_mx(
-                out=h_codes[:].bitcast(FP8X4), scales=h_plane[:], in_=h_columns(start, width).rearrange("p n t -> p (n t)")
+                out=h_codes[:, cols].bitcast(FP8X4), scales=h_plane[:, cols], in_=h_tiles[index][:].rearrange("p n t -> p (n t)")
             )
-            acc = psum_o.tile([P, width], F32, name="out_bank")
-            nc.tensor.matmul_mx(
-                out=acc[:],
-                lhsT=w2_codes[:].bitcast(FP4X4),
-                lhsT_scale=w2_plane[:],
-                rhs=h_codes[:].bitcast(FP8X4),
-                rhs_scale=h_plane[:],
-                start=True,
-                stop=True,
-            )
-            result = tile("result_%d" % index, [P, width], F32)
-            nc.scalar.copy(out=result[:], in_=acc[:])
-            nc.sync.dma_start(out=out[:, start : start + width], in_=result[:])
+
+        def second_product(copy, start, widths):
+            acc = psum_o.tile([P, sum(widths)], F32, name="out_bank")
+            at = 0
+            for width in widths:
+                cols = slice(start + at, start + at + width)
+                nc.tensor.matmul_mx(
+                    out=acc[:, at : at + width],
+                    lhsT=w2_codes[:].bitcast(FP4X4),
+                    lhsT_scale=w2_plane[:],
+                    rhs=h_codes[:, cols].bitcast(FP8X4),
+                    rhs_scale=h_plane[:, cols],
+                    start=True,
+                    stop=True,
+                )
+                at += width
+            copy(out=result[:, start : start + at], in_=acc[:])
+
+        def store(start, width):
+            nc.sync.dma_start(out=out[:, start : start + width], in_=result[:, start : start + width])
 
         for tiles in ((0, 1), (2, 3)):
             for b in range(H_BANKS):
@@ -233,5 +234,15 @@ def tile_picked_embpos_none_e_kernel(tc, xT, w1, w2_words, w2_scales, pos, offs,
                 first_product(b, 0)
             first_product(b, 1)
             add_pos(b)
-            for index in {5: (0, 1), 7: (2, 3)}.get(b, ()):
-                second_product(index)
+            if b == 2:
+                quantise_h(0)
+                quantise_h(1)
+                second_product(nc.scalar.copy, 0, (2 * BLOCK, BLOCK))
+                store(0, 3 * BLOCK)
+        quantise_h(2)
+        quantise_h(3)
+        second_product(nc.scalar.copy, 3 * BLOCK, (2 * BLOCK,))
+        store(3 * BLOCK, 2 * BLOCK)
+        second_product(nc.vector.tensor_copy, 5 * BLOCK, (2 * BLOCK,))
+        second_product(nc.scalar.copy, 7 * BLOCK, (BLOCK,))
+        store(5 * BLOCK, 3 * BLOCK)

@@ -28,7 +28,7 @@ POS_LOADS = (384, 384, 256)
 GPSIMD_BLOCK = 3
 H_BANKS = 4
 W_VECTOR_COLUMNS = (32, 32)
-OUT_GROUPS = (2, 1, 4, 1)
+OUT_GROUPS = (2, 1, 2, 2, 1)
 
 
 def tile_picked_embpos_none_e_kernel(tc, xT, w1, w2_words, w2_scales, pos, offs, out):
@@ -127,7 +127,7 @@ def tile_picked_embpos_none_e_kernel(tc, xT, w1, w2_words, w2_scales, pos, offs,
 
         rows = tile("rows_0", [P, PACK, S], BF16)
         for j in range(PACK):
-            gather_row(rows, j, j, HALF if j < 2 else BLOCK)
+            gather_row(rows, j, j, HALF)
         woven = halves("woven_0", [P, HALF, PACK], BF16)
         first_codes = tile("x_codes_0", [P, S], U32)
         for i in range(2):
@@ -138,24 +138,23 @@ def tile_picked_embpos_none_e_kernel(tc, xT, w1, w2_words, w2_scales, pos, offs,
         woven = halves("woven_1", [P, HALF, PACK], BF16)
         rows = tile("rows_1_0", [P, 2, S], BF16)
         for e in range(2):
-            gather_row(rows, e, PACK + e, BLOCK)
+            gather_row(rows, e, PACK + e, QUARTER if e else BLOCK)
         for i in range(2):
             weave(nc.vector.tensor_copy, woven[i][:, :, :2], rows[:, :, i * HALF : (i + 1) * HALF])
         last_rows = tile("rows_1_1", [P, 2, S], BF16)
-        gather_row(last_rows, 0, PACK + 2, BLOCK)
+        gather_row(last_rows, 0, PACK + 2, QUARTER)
         rows = [last_rows[:, :, i * QUARTER : (i + 1) * QUARTER] for i in range(4)]
         for i in range(4):
             (gather_scalar if i else gather_vector)(rows[i][:, 1, :], PACK + 3, i * QUARTER, QUARTER)
         quarters = [woven[i // 2][:, i % 2 * QUARTER : (i % 2 + 1) * QUARTER, :] for i in range(4)]
         weave(nc.scalar.copy, quarters[3][:, :, 2:], rows[3])
-        second_codes = tile("x_codes_1_0", [P, HALF], U32)
         for i in range(2):
             weave(nc.vector.tensor_copy, quarters[i][:, :, 2:], rows[i])
-        quantise_x(1, second_codes[:, :QUARTER], quarters[0], 0, QUARTER)
+        quantise_x(1, tile("x_codes_1_0", [P, QUARTER], U32)[:], quarters[0], 0, QUARTER)
         weave(nc.vector.tensor_copy, quarters[2][:, :, 2:], rows[2])
-        quantise_x(1, second_codes[:, QUARTER:], quarters[1], QUARTER, QUARTER)
-        for g in range(PASSES):
-            weave_w(g)
+        weave_w(0)
+        quantise_x(1, tile("x_codes_1_q", [P, QUARTER], U32, "w_raw_0")[:], quarters[1], QUARTER, QUARTER)
+        weave_w(1)
         quantise_x(1, tile("x_codes_1_1", [P, HALF], U32, "w_raw_1")[:], woven[1][:], HALF, HALF)
 
         banks = {}
@@ -239,8 +238,8 @@ def tile_picked_embpos_none_e_kernel(tc, xT, w1, w2_words, w2_scales, pos, offs,
                 quantise_h(1)
                 second_product(nc.scalar.copy, 0, (2 * BLOCK, BLOCK))
                 store(0, 3 * BLOCK)
-        quantise_h(2)
-        quantise_h(3)
+        for index in (2, 3, 4):
+            quantise_h(index)
         second_product(nc.scalar.copy, 3 * BLOCK, (2 * BLOCK,))
         store(3 * BLOCK, 2 * BLOCK)
         second_product(nc.vector.tensor_copy, 5 * BLOCK, (2 * BLOCK,))

@@ -35,6 +35,7 @@ def tile_picked_embpos_none_e_kernel(tc, xT, w1, w2_words, w2_scales, pos, offs,
     nc = tc.nc
     with ExitStack() as ctx:
         keep = ctx.enter_context(tc.tile_pool(name="keep", bufs=1))
+        shared = ctx.enter_context(tc.tile_pool(name="shared", bufs=1))
         psum_h = ctx.enter_context(tc.psum_pool(name="psum_h", bufs=H_BANKS))
         psum_o = ctx.enter_context(tc.psum_pool(name="psum_o", bufs=8 - H_BANKS))
 
@@ -47,7 +48,7 @@ def tile_picked_embpos_none_e_kernel(tc, xT, w1, w2_words, w2_scales, pos, offs,
         nc.gpsimd.memset(w2_plane[:].bitcast(I32), 0)
 
         x_raw = [tile("x_raw_%d" % r, [P, T], F32) for r in range(PASSES * PACK)]
-        w_raw = [tile("w_raw_0", [P, PACK, H], F32), tile("w_raw_1", [P, PACK, H], F32)]
+        w_raw = [tile("w_raw_0", [P, PACK, H], F32), shared.tile([P, PACK, H], F32, name="w_raw_1", align_bytes=64, offset=0)]
 
         def load_x(r):
             g, j = divmod(r, PACK)
@@ -89,6 +90,9 @@ def tile_picked_embpos_none_e_kernel(tc, xT, w1, w2_words, w2_scales, pos, offs,
 
         def weave(copy, woven, rows):
             copy(out=woven.rearrange("p (c i) j -> p c j i", i=WALK), in_=rows.rearrange("p j (c i) -> p c j i", i=WALK))
+
+        def lay_pair(copy, places, rows):
+            copy(out=places, in_=rows.rearrange("p e n -> p n e"))
 
         x_plane = [tile("x_plane_%d" % g, [P, S], U8) for g in range(PASSES)]
         x_codes = [{}, {}]
@@ -135,27 +139,27 @@ def tile_picked_embpos_none_e_kernel(tc, xT, w1, w2_words, w2_scales, pos, offs,
         for i in range(2):
             quantise_x(0, first_codes[:, i * HALF : (i + 1) * HALF], woven[i][:], i * HALF, HALF)
 
-        woven = halves("woven_1", [P, HALF, PACK], BF16)
-        rows = tile("rows_1_0", [P, 2, S], BF16)
-        for e in range(2):
-            gather_row(rows, e, PACK + e, QUARTER if e else BLOCK)
-        for i in range(2):
-            weave(nc.vector.tensor_copy, woven[i][:, :, :2], rows[:, :, i * HALF : (i + 1) * HALF])
-        last_rows = tile("rows_1_1", [P, 2, S], BF16)
-        gather_row(last_rows, 0, PACK + 2, QUARTER)
-        rows = [last_rows[:, :, i * QUARTER : (i + 1) * QUARTER] for i in range(4)]
+        early = 3 * QUARTER
+        woven = tile("woven_1", [P, early, PACK], BF16)
+        rows = tile("rows_1", [P, PACK, S], BF16)
+        for j in range(PACK - 1):
+            gather_row(rows, j, PACK + j, QUARTER if j else BLOCK)
+            if j == 1:
+                lay_pair(nc.vector.tensor_copy, woven[:, :HALF, :2], rows[:, :2, :HALF])
+                lay_pair(nc.vector.tensor_copy, woven[:, HALF:, :2], rows[:, :2, HALF:early])
         for i in range(4):
-            (gather_scalar if i else gather_vector)(rows[i][:, 1, :], PACK + 3, i * QUARTER, QUARTER)
-        quarters = [woven[i // 2][:, i % 2 * QUARTER : (i % 2 + 1) * QUARTER, :] for i in range(4)]
-        weave(nc.scalar.copy, quarters[3][:, :, 2:], rows[3])
-        for i in range(2):
-            weave(nc.vector.tensor_copy, quarters[i][:, :, 2:], rows[i])
-        quantise_x(1, tile("x_codes_1_0", [P, QUARTER], U32)[:], quarters[0], 0, QUARTER)
-        weave(nc.vector.tensor_copy, quarters[2][:, :, 2:], rows[2])
-        weave_w(0)
-        quantise_x(1, tile("x_codes_1_q", [P, QUARTER], U32, "w_raw_0")[:], quarters[1], QUARTER, QUARTER)
-        weave_w(1)
-        quantise_x(1, tile("x_codes_1_1", [P, HALF], U32, "w_raw_1")[:], woven[1][:], HALF, HALF)
+            (gather_scalar if i else gather_vector)(rows[:, PACK - 1, i * QUARTER : (i + 1) * QUARTER], 2 * PACK - 1, i * QUARTER, QUARTER)
+        for i in range(3):
+            part = slice(i * QUARTER, (i + 1) * QUARTER)
+            lay_pair(nc.vector.tensor_copy, woven[:, part, 2:], rows[:, 2:, part])
+            if i == 1:
+                quantise_x(1, tile("x_codes_1_0", [P, QUARTER], U32)[:], woven[:, :QUARTER, :], 0, QUARTER)
+        for g in range(PASSES):
+            weave_w(g)
+        middle_codes = shared.tile([P, HALF], U32, name="x_codes_1_1", align_bytes=64, offset=0)
+        quantise_x(1, middle_codes[:], woven[:, QUARTER:, :], QUARTER, HALF)
+        late = shared.tile([P, QUARTER, PACK], BF16, name="woven_late", align_bytes=64, offset=4 * HALF)
+        weave(nc.scalar.copy, late[:], rows[:, :, early:])
 
         banks = {}
 
@@ -233,6 +237,8 @@ def tile_picked_embpos_none_e_kernel(tc, xT, w1, w2_words, w2_scales, pos, offs,
                 first_product(b, 0)
             first_product(b, 1)
             add_pos(b)
+            if b == 1:
+                quantise_x(1, tile("x_codes_1_2", [P, QUARTER], U32)[:], late[:], early, QUARTER)
             if b == 2:
                 quantise_h(0)
                 quantise_h(1)

@@ -27,7 +27,7 @@ WALK = 4
 POS_LOADS = (384, 384, 256)
 GPSIMD_BLOCK = 3
 H_BANKS = 4
-W_VECTOR_COLUMNS = (32, 32)
+W_VECTOR_COLUMNS = (32, 48)
 OUT_GROUPS = (2, 1, 2, 2, 1)
 
 
@@ -48,7 +48,7 @@ def tile_picked_embpos_none_e_kernel(tc, xT, w1, w2_words, w2_scales, pos, offs,
         nc.gpsimd.memset(w2_plane[:].bitcast(I32), 0)
 
         x_raw = [tile("x_raw_%d" % r, [P, T], F32) for r in range(PASSES * PACK)]
-        w_raw = [tile("w_raw_0", [P, PACK, H], F32), shared.tile([P, PACK, H], F32, name="w_raw_1", align_bytes=64, offset=0)]
+        w_raw = [shared.tile([P, PACK, H], F32, name="w_raw_0", align_bytes=64, offset=0), tile("w_raw_1", [P, PACK, H], F32)]
 
         def load_x(r):
             g, j = divmod(r, PACK)
@@ -90,9 +90,6 @@ def tile_picked_embpos_none_e_kernel(tc, xT, w1, w2_words, w2_scales, pos, offs,
 
         def weave(copy, woven, rows):
             copy(out=woven.rearrange("p (c i) j -> p c j i", i=WALK), in_=rows.rearrange("p j (c i) -> p c j i", i=WALK))
-
-        def lay_pair(copy, places, rows):
-            copy(out=places, in_=rows.rearrange("p e n -> p n e"))
 
         x_plane = [tile("x_plane_%d" % g, [P, S], U8) for g in range(PASSES)]
         x_codes = [{}, {}]
@@ -145,21 +142,24 @@ def tile_picked_embpos_none_e_kernel(tc, xT, w1, w2_words, w2_scales, pos, offs,
         for j in range(PACK - 1):
             gather_row(rows, j, PACK + j, QUARTER if j else BLOCK)
             if j == 1:
-                lay_pair(nc.vector.tensor_copy, woven[:, :HALF, :2], rows[:, :2, :HALF])
-                lay_pair(nc.vector.tensor_copy, woven[:, HALF:, :2], rows[:, :2, HALF:early])
+                weave(nc.vector.tensor_copy, woven[:, :HALF, :2], rows[:, :2, :HALF])
+                weave(nc.vector.tensor_copy, woven[:, HALF:, :2], rows[:, :2, HALF:early])
         for i in range(4):
             (gather_scalar if i else gather_vector)(rows[:, PACK - 1, i * QUARTER : (i + 1) * QUARTER], 2 * PACK - 1, i * QUARTER, QUARTER)
         for i in range(3):
             part = slice(i * QUARTER, (i + 1) * QUARTER)
-            lay_pair(nc.vector.tensor_copy, woven[:, part, 2:], rows[:, 2:, part])
+            weave(nc.vector.tensor_copy, woven[:, part, 2:], rows[:, 2:, part])
             if i == 1:
                 quantise_x(1, tile("x_codes_1_0", [P, QUARTER], U32)[:], woven[:, :QUARTER, :], 0, QUARTER)
-        for g in range(PASSES):
-            weave_w(g)
-        middle_codes = shared.tile([P, HALF], U32, name="x_codes_1_1", align_bytes=64, offset=0)
-        quantise_x(1, middle_codes[:], woven[:, QUARTER:, :], QUARTER, HALF)
-        late = shared.tile([P, QUARTER, PACK], BF16, name="woven_late", align_bytes=64, offset=4 * HALF)
+        weave_w(0)
+        second_codes = shared.tile([P, QUARTER], U32, name="x_codes_1_1", align_bytes=64, offset=0)
+        quantise_x(1, second_codes[:], woven[:, QUARTER:HALF, :], QUARTER, QUARTER)
+        late = shared.tile([P, QUARTER, PACK], BF16, name="woven_late", align_bytes=64, offset=4 * QUARTER)
         weave(nc.scalar.copy, late[:], rows[:, :, early:])
+        weave_w(1)
+        last_codes = tile("x_codes_1_2", [P, HALF], U32, "w_raw_1")
+        quantise_x(1, last_codes[:, :QUARTER], woven[:, HALF:, :], HALF, QUARTER)
+        quantise_x(1, last_codes[:, QUARTER:], late[:], early, QUARTER)
 
         banks = {}
 
@@ -237,8 +237,6 @@ def tile_picked_embpos_none_e_kernel(tc, xT, w1, w2_words, w2_scales, pos, offs,
                 first_product(b, 0)
             first_product(b, 1)
             add_pos(b)
-            if b == 1:
-                quantise_x(1, tile("x_codes_1_2", [P, QUARTER], U32)[:], late[:], early, QUARTER)
             if b == 2:
                 quantise_h(0)
                 quantise_h(1)

@@ -27,6 +27,7 @@ WALK = 4
 POS_LOADS = (384, 384, 256)
 GPSIMD_BLOCK = 3
 H_BANKS = 4
+WARM_UPS = 7
 W_VECTOR_COLUMNS = (32, 48)
 OUT_GROUPS = (2, 1, 2, 2, 1)
 
@@ -229,6 +230,17 @@ def tile_picked_embpos_none_e_kernel(tc, xT, w1, w2_words, w2_scales, pos, offs,
         def store(start, width):
             nc.sync.dma_start(out=out[:, start : start + width], in_=result[:, start : start + width])
 
+        warm = psum_o.tile([P, BLOCK], F32, name="out_bank")
+        for i in range(WARM_UPS):
+            nc.tensor.matmul_mx(
+                out=warm[:],
+                lhsT=x_codes[1][0].bitcast(FP8X4),
+                lhsT_scale=x_plane[1][:, :BLOCK],
+                rhs=x_codes[1][1].bitcast(FP8X4),
+                rhs_scale=x_plane[1][:, BLOCK : 2 * BLOCK],
+                start=True,
+                stop=True,
+            )
         for tiles in ((0, 1), (2, 3)):
             for b in range(H_BANKS):
                 first_product(b, 0, tiles)

@@ -28,7 +28,7 @@ POS_LOADS = (384, 384, 256)
 GPSIMD_BLOCK = 3
 H_BANKS = 4
 WARM_UPS = 7
-W_VECTOR_COLUMNS = (32, 48)
+W_VECTOR_COLUMNS = (48, 64)
 OUT_GROUPS = (2, 1, 2, 2, 1)
 
 

@@ -28,7 +28,7 @@ POS_LOADS = (384, 384, 256)
 GPSIMD_BLOCK = 3
 H_BANKS = 4
 WARM_UPS = 7
-W_VECTOR_COLUMNS = (48, 64)
+W_VECTOR_COLUMNS = (48, 40)
 OUT_GROUPS = (2, 1, 2, 2, 1)
 
 
@@ -137,7 +137,7 @@ def tile_picked_embpos_none_e_kernel(tc, xT, w1, w2_words, w2_scales, pos, offs,
         for i in range(2):
             quantise_x(0, first_codes[:, i * HALF : (i + 1) * HALF], woven[i][:], i * HALF, HALF)
 
-        early = 3 * QUARTER
+        early = S - BLOCK
         woven = tile("woven_1", [P, early, PACK], BF16)
         rows = tile("rows_1", [P, PACK, S], BF16)
         for j in range(PACK - 1):
@@ -152,15 +152,16 @@ def tile_picked_embpos_none_e_kernel(tc, xT, w1, w2_words, w2_scales, pos, offs,
             weave(nc.vector.tensor_copy, woven[:, part, 2:], rows[:, 2:, part])
             if i == 1:
                 quantise_x(1, tile("x_codes_1_0", [P, QUARTER], U32)[:], woven[:, :QUARTER, :], 0, QUARTER)
+        weave(nc.scalar.copy, woven[:, 3 * QUARTER :, 2:], rows[:, 2:, 3 * QUARTER : early])
         weave_w(0)
         second_codes = shared.tile([P, QUARTER], U32, name="x_codes_1_1", align_bytes=64, offset=0)
         quantise_x(1, second_codes[:], woven[:, QUARTER:HALF, :], QUARTER, QUARTER)
-        late = shared.tile([P, QUARTER, PACK], BF16, name="woven_late", align_bytes=64, offset=4 * QUARTER)
+        late = shared.tile([P, BLOCK, PACK], BF16, name="woven_late", align_bytes=64, offset=4 * QUARTER)
         weave(nc.scalar.copy, late[:], rows[:, :, early:])
         weave_w(1)
         last_codes = tile("x_codes_1_2", [P, HALF], U32, "w_raw_1")
-        quantise_x(1, last_codes[:, :QUARTER], woven[:, HALF:, :], HALF, QUARTER)
-        quantise_x(1, last_codes[:, QUARTER:], late[:], early, QUARTER)
+        quantise_x(1, last_codes[:, : early - HALF], woven[:, HALF:, :], HALF, early - HALF)
+        quantise_x(1, last_codes[:, early - HALF :], late[:], early, BLOCK)
 
         banks = {}
 

@@ -36,7 +36,6 @@ def tile_picked_embpos_none_e_kernel(tc, xT, w1, w2_words, w2_scales, pos, offs,
     nc = tc.nc
     with ExitStack() as ctx:
         keep = ctx.enter_context(tc.tile_pool(name="keep", bufs=1))
-        shared = ctx.enter_context(tc.tile_pool(name="shared", bufs=1))
         psum_h = ctx.enter_context(tc.psum_pool(name="psum_h", bufs=H_BANKS))
         psum_o = ctx.enter_context(tc.psum_pool(name="psum_o", bufs=8 - H_BANKS))
 
@@ -48,22 +47,20 @@ def tile_picked_embpos_none_e_kernel(tc, xT, w1, w2_words, w2_scales, pos, offs,
         w2_plane = tile("w2_plane", [P, N], U8)
         nc.gpsimd.memset(w2_plane[:].bitcast(I32), 0)
 
-        x_raw = [tile("x_raw_%d" % r, [P, T], F32) for r in range(PASSES * PACK)]
-        w_raw = [shared.tile([P, PACK, H], F32, name="w_raw_0", align_bytes=64, offset=0), tile("w_raw_1", [P, PACK, H], F32)]
+        x_pairs = [tile("x_pair_%d" % i, [P, 2 * T], F32) for i in range(2)]
+        x_single = [tile("x_single_%d" % j, [P, T], F32) for j in range(PACK)]
+        w_raw = [tile("w_raw_%d" % g, [P, PACK, H], F32) for g in range(PASSES)]
 
-        def load_x(r):
-            g, j = divmod(r, PACK)
-            nc.sync.dma_start(out=x_raw[r][:], in_=xT[g * K_PASS : (g + 1) * K_PASS, :].rearrange("(p j) t -> p j t", j=PACK)[:, j, :])
+        def x_rows(g, j, count):
+            return xT[g * K_PASS : (g + 1) * K_PASS, :].rearrange("(p j) t -> p (j t)", j=PACK)[:, j * T : (j + count) * T]
 
-        def load_w(g):
-            nc.sync.dma_start(out=w_raw[g][:], in_=w1[g * K_PASS : (g + 1) * K_PASS, :].rearrange("(p j) c -> p j c", j=PACK))
-
-        load_x(0)
+        nc.sync.dma_start(out=x_pairs[0][:], in_=x_rows(0, 0, 2))
         nc.sync.dma_start(offsets[:], offs)
-        for r in range(1, PASSES * PACK):
-            load_x(r)
+        nc.sync.dma_start(out=x_pairs[1][:], in_=x_rows(0, 2, 2))
+        for j in range(PACK):
+            nc.sync.dma_start(out=x_single[j][:], in_=x_rows(1, j, 1))
         for g in range(PASSES):
-            load_w(g)
+            nc.sync.dma_start(out=w_raw[g][:], in_=w1[g * K_PASS : (g + 1) * K_PASS, :].rearrange("(p j) c -> p j c", j=PACK))
 
         pos_rows = pos.rearrange("(p t) s -> p t s", t=PACK)
         pos_sb = []
@@ -80,17 +77,20 @@ def tile_picked_embpos_none_e_kernel(tc, xT, w1, w2_words, w2_scales, pos, offs,
                 in_=w2_scales[0, 4 * q : 4 * q + 4, :].bitcast(I32),
             )
 
-        def looked_up(r, start, count):
-            return x_raw[r][:].indirect(offsets[:, start // 16 : (start + count) // 16])
+        def entries(start, count):
+            return offsets[:, start // 16 : (start + count) // 16]
 
-        def gather_vector(target, r, start, count):
-            nc.vector.tensor_copy(target, looked_up(r, start, count))
+        def gather_vector(target, window, start, count):
+            nc.vector.tensor_copy(target, window.indirect(entries(start, count)))
 
-        def gather_scalar(target, r, start, count):
-            nc.scalar.activation(out=target, in_=looked_up(r, start, count), func=COPY)
+        def gather_scalar(target, window, start, count):
+            nc.scalar.activation(out=target, in_=window.indirect(entries(start, count)), func=COPY)
 
-        def weave(copy, woven, rows):
-            copy(out=woven.rearrange("p (c i) j -> p c j i", i=WALK), in_=rows.rearrange("p j (c i) -> p c j i", i=WALK))
+        def join(copy, dtype, woven, pairs):
+            copy(
+                out=woven.rearrange("p n j -> p (n j)").bitcast(dtype).rearrange("p (c i a) -> p c a i", i=WALK, a=2),
+                in_=pairs.rearrange("p a n e -> p a (n e)").bitcast(dtype).rearrange("p a (c i) -> p c a i", i=WALK),
+            )
 
         x_plane = [tile("x_plane_%d" % g, [P, S], U8) for g in range(PASSES)]
         x_codes = [{}, {}]
@@ -107,61 +107,44 @@ def tile_picked_embpos_none_e_kernel(tc, xT, w1, w2_words, w2_scales, pos, offs,
 
         def weave_w(g):
             woven = [tile("w_bf_%d_%d" % (g, u), [P, 2, P, PACK], BF16) for u in range(2)]
-            target = [woven[u][:].rearrange("p t m j -> p m j t") for u in range(2)]
-            source = [w_raw[g][:].rearrange("p j (m t) -> p m j t", t=PACK)[:, :, :, 2 * u : 2 * u + 2] for u in range(2)]
+            target = [woven[u][:].rearrange("p t m (a e) -> p m e a t", a=2) for u in range(2)]
+            source = [w_raw[g][:].rearrange("p (e a) (m t) -> p m e a t", a=2, t=PACK)[:, :, :, :, 2 * u : 2 * u + 2] for u in range(2)]
             cut = P - W_VECTOR_COLUMNS[g]
             nc.scalar.copy(out=target[1][:, :cut], in_=source[1][:, :cut])
             nc.vector.tensor_copy(out=target[0], in_=source[0])
-            if cut < P:
-                nc.vector.tensor_copy(out=target[1][:, cut:], in_=source[1][:, cut:])
+            nc.vector.tensor_copy(out=target[1][:, cut:], in_=source[1][:, cut:])
             for u in range(2):
                 cols = slice(2 * u * P, 2 * (u + 1) * P)
                 nc.vector.quantize_mx(
                     out=w_codes[g][:, cols].bitcast(FP8X4), scales=w_plane[g][:, cols], in_=woven[u][:].rearrange("p t m j -> p (t m j)")
                 )
 
-        def halves(name, shape, dtype):
-            return [tile("%s_%d" % (name, i), shape, dtype) for i in range(2)]
-
-        def gather_row(rows, e, r, vector_entries):
-            gather_vector(rows[:, e, :vector_entries], r, 0, vector_entries)
-            gather_scalar(rows[:, e, vector_entries:], r, vector_entries, S - vector_entries)
-
-        rows = tile("rows_0", [P, PACK, S], BF16)
-        for j in range(PACK):
-            gather_row(rows, j, j, HALF)
-        woven = halves("woven_0", [P, HALF, PACK], BF16)
+        pairs = tile("pairs_0", [P, 2, S, 2], BF16)
+        for e in range(2):
+            gather_scalar(pairs[:, 0, :, e], x_pairs[e][:], 0, S)
+            gather_vector(pairs[:, 1, :, e], x_pairs[e][:, T:], 0, S)
+        woven = [tile("woven_0_%d" % i, [P, HALF, PACK], BF16) for i in range(2)]
         first_codes = tile("x_codes_0", [P, S], U32)
-        for i in range(2):
-            weave(nc.vector.tensor_copy, woven[i][:], rows[:, :, i * HALF : (i + 1) * HALF])
+        join(nc.vector.tensor_copy, I32, woven[0][:], pairs[:, :, :HALF, :])
+        join(nc.vector.tensor_copy, I32, woven[1][:], pairs[:, :, HALF:, :])
         for i in range(2):
             quantise_x(0, first_codes[:, i * HALF : (i + 1) * HALF], woven[i][:], i * HALF, HALF)
 
-        early = S - BLOCK
-        woven = tile("woven_1", [P, early, PACK], BF16)
-        rows = tile("rows_1", [P, PACK, S], BF16)
-        for j in range(PACK - 1):
-            gather_row(rows, j, PACK + j, QUARTER if j else BLOCK)
-            if j == 1:
-                weave(nc.vector.tensor_copy, woven[:, :HALF, :2], rows[:, :2, :HALF])
-                weave(nc.vector.tensor_copy, woven[:, HALF:, :2], rows[:, :2, HALF:early])
-        for i in range(4):
-            (gather_scalar if i else gather_vector)(rows[:, PACK - 1, i * QUARTER : (i + 1) * QUARTER], 2 * PACK - 1, i * QUARTER, QUARTER)
-        for i in range(3):
-            part = slice(i * QUARTER, (i + 1) * QUARTER)
-            weave(nc.vector.tensor_copy, woven[:, part, 2:], rows[:, 2:, part])
-            if i == 1:
-                quantise_x(1, tile("x_codes_1_0", [P, QUARTER], U32)[:], woven[:, :QUARTER, :], 0, QUARTER)
-        weave(nc.scalar.copy, woven[:, 3 * QUARTER :, 2:], rows[:, 2:, 3 * QUARTER : early])
+        pairs = [tile("pairs_1_%d" % i, [P, 2, QUARTER, 2], BF16) for i in range(4)]
+        woven = [tile("woven_1_%d" % i, [P, QUARTER, PACK], BF16)[:] for i in range(2)]
+        woven_late = tile("woven_late", [P, HALF, PACK], BF16)
+        for j in range(PACK):
+            for i in range(4):
+                (gather_scalar if i else gather_vector)(pairs[i][:, j % 2, :, j // 2], x_single[j][:], i * QUARTER, QUARTER)
+        for i in (1, 0):
+            join(nc.vector.tensor_copy, I32, woven[i], pairs[i][:])
+        for i in (1, 0):
+            quantise_x(1, tile("x_codes_1_%d" % i, [P, QUARTER], U32)[:], woven[i], i * QUARTER, QUARTER)
         weave_w(0)
-        second_codes = shared.tile([P, QUARTER], U32, name="x_codes_1_1", align_bytes=64, offset=0)
-        quantise_x(1, second_codes[:], woven[:, QUARTER:HALF, :], QUARTER, QUARTER)
-        late = shared.tile([P, BLOCK, PACK], BF16, name="woven_late", align_bytes=64, offset=4 * QUARTER)
-        weave(nc.scalar.copy, late[:], rows[:, :, early:])
+        for i in range(2):
+            join(nc.scalar.copy, U32, woven_late[:, i * QUARTER : (i + 1) * QUARTER, :], pairs[2 + i][:])
         weave_w(1)
-        last_codes = tile("x_codes_1_2", [P, HALF], U32, "w_raw_1")
-        quantise_x(1, last_codes[:, : early - HALF], woven[:, HALF:, :], HALF, early - HALF)
-        quantise_x(1, last_codes[:, early - HALF :], late[:], early, BLOCK)
+        quantise_x(1, tile("x_codes_1_2", [P, HALF], U32, "w_raw_1")[:], woven_late[:], HALF, HALF)
 
         banks = {}
 
@@ -200,7 +183,10 @@ def tile_picked_embpos_none_e_kernel(tc, xT, w1, w2_words, w2_scales, pos, offs,
                     op=mybir.AluOpType.add,
                 )
 
-        h_codes = tile("h_codes", [P, S], U32)
+        h_codes = [
+            tile("h_codes_%d" % index, [P, width * BLOCK], U32, "pos_%d" % (S - POS_LOADS[-1]) if index == 2 else None)
+            for index, width in enumerate(OUT_GROUPS)
+        ]
         h_plane = tile("h_plane", [P, S], U8)
         result = tile("result", [P, S], F32)
 
@@ -208,20 +194,21 @@ def tile_picked_embpos_none_e_kernel(tc, xT, w1, w2_words, w2_scales, pos, offs,
             start = sum(OUT_GROUPS[:index]) * BLOCK
             cols = slice(start, start + OUT_GROUPS[index] * BLOCK)
             nc.vector.quantize_mx(
-                out=h_codes[:, cols].bitcast(FP8X4), scales=h_plane[:, cols], in_=h_tiles[index][:].rearrange("p n t -> p (n t)")
+                out=h_codes[index][:].bitcast(FP8X4), scales=h_plane[:, cols], in_=h_tiles[index][:].rearrange("p n t -> p (n t)")
             )
 
-        def second_product(copy, start, widths):
-            acc = psum_o.tile([P, sum(widths)], F32, name="out_bank")
+        def second_product(copy, indices):
+            start = sum(OUT_GROUPS[: indices[0]]) * BLOCK
+            acc = psum_o.tile([P, sum(OUT_GROUPS[index] for index in indices) * BLOCK], F32, name="out_bank")
             at = 0
-            for width in widths:
-                cols = slice(start + at, start + at + width)
+            for index in indices:
+                width = OUT_GROUPS[index] * BLOCK
                 nc.tensor.matmul_mx(
                     out=acc[:, at : at + width],
                     lhsT=w2_codes[:].bitcast(FP4X4),
                     lhsT_scale=w2_plane[:],
-                    rhs=h_codes[:, cols].bitcast(FP8X4),
-                    rhs_scale=h_plane[:, cols],
+                    rhs=h_codes[index][:].bitcast(FP8X4),
+                    rhs_scale=h_plane[:, start + at : start + at + width],
                     start=True,
                     stop=True,
                 )
@@ -249,16 +236,18 @@ def tile_picked_embpos_none_e_kernel(tc, xT, w1, w2_words, w2_scales, pos, offs,
             if b >= H_BANKS:
                 first_product(b, 0)
             first_product(b, 1)
-            add_pos(b)
+            if b != BLOCKS - 2:
+                add_pos(b)
             if b == 2:
                 quantise_h(0)
                 quantise_h(1)
-                second_product(nc.scalar.copy, 0, (2 * BLOCK, BLOCK))
+                second_product(nc.scalar.copy, (0, 1))
                 store(0, 3 * BLOCK)
-        for index in (2, 3, 4):
+        add_pos(BLOCKS - 2)
+        for index in (4, 3, 2):
             quantise_h(index)
-        second_product(nc.scalar.copy, 3 * BLOCK, (2 * BLOCK,))
-        store(3 * BLOCK, 2 * BLOCK)
-        second_product(nc.vector.tensor_copy, 5 * BLOCK, (2 * BLOCK,))
-        second_product(nc.scalar.copy, 7 * BLOCK, (BLOCK,))
+        second_product(nc.scalar.copy, (4,))
+        second_product(nc.scalar.copy, (3,))
         store(5 * BLOCK, 3 * BLOCK)
+        second_product(nc.vector.tensor_copy, (2,))
+        store(3 * BLOCK, 2 * BLOCK)

@@ -29,6 +29,7 @@ GPSIMD_BLOCK = 3
 H_BANKS = 4
 WARM_UPS = 7
 W_VECTOR_COLUMNS = (48, 40)
+X_PIECES = (384, 128, 256, 256)
 OUT_GROUPS = (2, 1, 2, 2, 1)
 
 
@@ -130,19 +131,19 @@ def tile_picked_embpos_none_e_kernel(tc, xT, w1, w2_words, w2_scales, pos, offs,
         for i in range(2):
             quantise_x(0, first_codes[:, i * HALF : (i + 1) * HALF], woven[i][:], i * HALF, HALF)
 
-        pairs = [tile("pairs_1_%d" % i, [P, 2, QUARTER, 2], BF16) for i in range(4)]
-        woven = [tile("woven_1_%d" % i, [P, QUARTER, PACK], BF16)[:] for i in range(2)]
+        pairs = [tile("pairs_1_%d" % i, [P, 2, width, 2], BF16) for i, width in enumerate(X_PIECES)]
+        woven = [tile("woven_1_%d" % i, [P, X_PIECES[i], PACK], BF16)[:] for i in range(2)]
         woven_late = tile("woven_late", [P, HALF, PACK], BF16)
         for j in range(PACK):
-            for i in range(4):
-                (gather_scalar if i else gather_vector)(pairs[i][:, j % 2, :, j // 2], x_single[j][:], i * QUARTER, QUARTER)
+            for i, width in enumerate(X_PIECES):
+                (gather_scalar if i else gather_vector)(pairs[i][:, j % 2, :, j // 2], x_single[j][:], sum(X_PIECES[:i]), width)
         for i in (1, 0):
             join(nc.vector.tensor_copy, I32, woven[i], pairs[i][:])
         for i in (1, 0):
-            quantise_x(1, tile("x_codes_1_%d" % i, [P, QUARTER], U32)[:], woven[i], i * QUARTER, QUARTER)
+            quantise_x(1, tile("x_codes_1_%d" % i, [P, X_PIECES[i]], U32)[:], woven[i], sum(X_PIECES[:i]), X_PIECES[i])
+        join(nc.scalar.copy, U32, woven_late[:, :QUARTER, :], pairs[2][:])
         weave_w(0)
-        for i in range(2):
-            join(nc.scalar.copy, U32, woven_late[:, i * QUARTER : (i + 1) * QUARTER, :], pairs[2 + i][:])
+        join(nc.scalar.copy, U32, woven_late[:, QUARTER:, :], pairs[3][:])
         weave_w(1)
         quantise_x(1, tile("x_codes_1_2", [P, HALF], U32, "w_raw_1")[:], woven_late[:], HALF, HALF)
 
@@ -183,10 +184,7 @@ def tile_picked_embpos_none_e_kernel(tc, xT, w1, w2_words, w2_scales, pos, offs,
                     op=mybir.AluOpType.add,
                 )
 
-        h_codes = [
-            tile("h_codes_%d" % index, [P, width * BLOCK], U32, "pos_%d" % (S - POS_LOADS[-1]) if index == 2 else None)
-            for index, width in enumerate(OUT_GROUPS)
-        ]
+        h_codes = tile("h_codes", [P, S], U32)
         h_plane = tile("h_plane", [P, S], U8)
         result = tile("result", [P, S], F32)
 
@@ -194,21 +192,20 @@ def tile_picked_embpos_none_e_kernel(tc, xT, w1, w2_words, w2_scales, pos, offs,
             start = sum(OUT_GROUPS[:index]) * BLOCK
             cols = slice(start, start + OUT_GROUPS[index] * BLOCK)
             nc.vector.quantize_mx(
-                out=h_codes[index][:].bitcast(FP8X4), scales=h_plane[:, cols], in_=h_tiles[index][:].rearrange("p n t -> p (n t)")
+                out=h_codes[:, cols].bitcast(FP8X4), scales=h_plane[:, cols], in_=h_tiles[index][:].rearrange("p n t -> p (n t)")
             )
 
-        def second_product(copy, indices):
-            start = sum(OUT_GROUPS[: indices[0]]) * BLOCK
-            acc = psum_o.tile([P, sum(OUT_GROUPS[index] for index in indices) * BLOCK], F32, name="out_bank")
+        def second_product(copy, start, widths):
+            acc = psum_o.tile([P, sum(widths)], F32, name="out_bank")
             at = 0
-            for index in indices:
-                width = OUT_GROUPS[index] * BLOCK
+            for width in widths:
+                cols = slice(start + at, start + at + width)
                 nc.tensor.matmul_mx(
                     out=acc[:, at : at + width],
                     lhsT=w2_codes[:].bitcast(FP4X4),
                     lhsT_scale=w2_plane[:],
-                    rhs=h_codes[index][:].bitcast(FP8X4),
-                    rhs_scale=h_plane[:, start + at : start + at + width],
+                    rhs=h_codes[:, cols].bitcast(FP8X4),
+                    rhs_scale=h_plane[:, cols],
                     start=True,
                     stop=True,
                 )
@@ -222,10 +219,10 @@ def tile_picked_embpos_none_e_kernel(tc, xT, w1, w2_words, w2_scales, pos, offs,
         for i in range(WARM_UPS):
             nc.tensor.matmul_mx(
                 out=warm[:],
-                lhsT=x_codes[1][0].bitcast(FP8X4),
-                lhsT_scale=x_plane[1][:, :BLOCK],
-                rhs=x_codes[1][1].bitcast(FP8X4),
-                rhs_scale=x_plane[1][:, BLOCK : 2 * BLOCK],
+                lhsT=x_codes[1][3].bitcast(FP8X4),
+                lhsT_scale=x_plane[1][:, 3 * BLOCK : 4 * BLOCK],
+                rhs=x_codes[1][3].bitcast(FP8X4),
+                rhs_scale=x_plane[1][:, 3 * BLOCK : 4 * BLOCK],
                 start=True,
                 stop=True,
             )
@@ -236,18 +233,16 @@ def tile_picked_embpos_none_e_kernel(tc, xT, w1, w2_words, w2_scales, pos, offs,
             if b >= H_BANKS:
                 first_product(b, 0)
             first_product(b, 1)
-            if b != BLOCKS - 2:
-                add_pos(b)
+            add_pos(b)
             if b == 2:
                 quantise_h(0)
                 quantise_h(1)
-                second_product(nc.scalar.copy, (0, 1))
+                second_product(nc.scalar.copy, 0, (2 * BLOCK, BLOCK))
                 store(0, 3 * BLOCK)
-        add_pos(BLOCKS - 2)
-        for index in (4, 3, 2):
+        for index in (2, 3, 4):
             quantise_h(index)
-        second_product(nc.scalar.copy, (4,))
-        second_product(nc.scalar.copy, (3,))
-        store(5 * BLOCK, 3 * BLOCK)
-        second_product(nc.vector.tensor_copy, (2,))
+        second_product(nc.scalar.copy, 3 * BLOCK, (2 * BLOCK,))
         store(3 * BLOCK, 2 * BLOCK)
+        second_product(nc.vector.tensor_copy, 5 * BLOCK, (2 * BLOCK,))
+        second_product(nc.scalar.copy, 7 * BLOCK, (BLOCK,))
+        store(5 * BLOCK, 3 * BLOCK)

@@ -29,7 +29,7 @@ GPSIMD_BLOCK = 3
 H_BANKS = 4
 WARM_UPS = 7
 W_VECTOR_COLUMNS = (48, 40)
-X_PIECES = (384, 128, 256, 256)
+VECTOR_ENTRIES = (384, 256)
 OUT_GROUPS = (2, 1, 2, 2, 1)
 
 
@@ -108,7 +108,8 @@ def tile_picked_embpos_none_e_kernel(tc, xT, w1, w2_words, w2_scales, pos, offs,
 
         def weave_w(g):
             woven = [tile("w_bf_%d_%d" % (g, u), [P, 2, P, PACK], BF16) for u in range(2)]
-            target = [woven[u][:].rearrange("p t m (a e) -> p m e a t", a=2) for u in range(2)]
+            places = ("p t m (a e) -> p m e a t", "p t m (e a) -> p m e a t")[g]
+            target = [woven[u][:].rearrange(places, a=2) for u in range(2)]
             source = [w_raw[g][:].rearrange("p (e a) (m t) -> p m e a t", a=2, t=PACK)[:, :, :, :, 2 * u : 2 * u + 2] for u in range(2)]
             cut = P - W_VECTOR_COLUMNS[g]
             nc.scalar.copy(out=target[1][:, :cut], in_=source[1][:, :cut])
@@ -126,21 +127,26 @@ def tile_picked_embpos_none_e_kernel(tc, xT, w1, w2_words, w2_scales, pos, offs,
             gather_vector(pairs[:, 1, :, e], x_pairs[e][:, T:], 0, S)
         woven = [tile("woven_0_%d" % i, [P, HALF, PACK], BF16) for i in range(2)]
         first_codes = tile("x_codes_0", [P, S], U32)
-        join(nc.vector.tensor_copy, I32, woven[0][:], pairs[:, :, :HALF, :])
-        join(nc.vector.tensor_copy, I32, woven[1][:], pairs[:, :, HALF:, :])
+        join(nc.vector.tensor_copy, F32, woven[0][:], pairs[:, :, :HALF, :])
+        join(nc.vector.tensor_copy, F32, woven[1][:], pairs[:, :, HALF:, :])
         for i in range(2):
             quantise_x(0, first_codes[:, i * HALF : (i + 1) * HALF], woven[i][:], i * HALF, HALF)
 
-        pairs = [tile("pairs_1_%d" % i, [P, 2, width, 2], BF16) for i, width in enumerate(X_PIECES)]
-        woven = [tile("woven_1_%d" % i, [P, X_PIECES[i], PACK], BF16)[:] for i in range(2)]
+        early = tile("pairs_1_0", [P, 2, HALF, 2], BF16)
+        pairs = [early[:, :, :QUARTER, :], early[:, :, QUARTER:, :]] + [tile("pairs_1_%d" % i, [P, 2, QUARTER, 2], BF16) for i in (2, 3)]
+        woven = [tile("woven_1_%d" % i, [P, QUARTER, PACK], BF16)[:] for i in range(2)]
         woven_late = tile("woven_late", [P, HALF, PACK], BF16)
         for j in range(PACK):
-            for i, width in enumerate(X_PIECES):
-                (gather_scalar if i else gather_vector)(pairs[i][:, j % 2, :, j // 2], x_single[j][:], sum(X_PIECES[:i]), width)
+            a, e = divmod(j, 2)
+            cut = VECTOR_ENTRIES[a]
+            gather_vector(early[:, a, :cut, e], x_single[j][:], 0, cut)
+            gather_scalar(early[:, a, cut:, e], x_single[j][:], cut, HALF - cut)
+            for i in (2, 3):
+                gather_scalar(pairs[i][:, a, :, e], x_single[j][:], i * QUARTER, QUARTER)
         for i in (1, 0):
-            join(nc.vector.tensor_copy, I32, woven[i], pairs[i][:])
+            join(nc.vector.tensor_copy, F32, woven[i], pairs[i])
         for i in (1, 0):
-            quantise_x(1, tile("x_codes_1_%d" % i, [P, X_PIECES[i]], U32)[:], woven[i], sum(X_PIECES[:i]), X_PIECES[i])
+            quantise_x(1, tile("x_codes_1_%d" % i, [P, QUARTER], U32)[:], woven[i], i * QUARTER, QUARTER)
         join(nc.scalar.copy, U32, woven_late[:, :QUARTER, :], pairs[2][:])
         weave_w(0)
         join(nc.scalar.copy, U32, woven_late[:, QUARTER:, :], pairs[3][:])

@@ -48,18 +48,17 @@ def tile_picked_embpos_none_e_kernel(tc, xT, w1, w2_words, w2_scales, pos, offs,
         w2_plane = tile("w2_plane", [P, N], U8)
         nc.gpsimd.memset(w2_plane[:].bitcast(I32), 0)
 
-        x_pairs = [tile("x_pair_%d" % i, [P, 2 * T], F32) for i in range(2)]
-        x_single = [tile("x_single_%d" % j, [P, T], F32) for j in range(PACK)]
+        x_raw = [tile("x_raw_%d" % r, [P, T], F32) for r in range(PASSES * PACK)]
         w_raw = [tile("w_raw_%d" % g, [P, PACK, H], F32) for g in range(PASSES)]
 
-        def x_rows(g, j, count):
-            return xT[g * K_PASS : (g + 1) * K_PASS, :].rearrange("(p j) t -> p (j t)", j=PACK)[:, j * T : (j + count) * T]
+        def load_x(r):
+            g, j = divmod(r, PACK)
+            nc.sync.dma_start(out=x_raw[r][:], in_=xT[g * K_PASS : (g + 1) * K_PASS, :].rearrange("(p j) t -> p j t", j=PACK)[:, j, :])
 
-        nc.sync.dma_start(out=x_pairs[0][:], in_=x_rows(0, 0, 2))
+        load_x(0)
         nc.sync.dma_start(offsets[:], offs)
-        nc.sync.dma_start(out=x_pairs[1][:], in_=x_rows(0, 2, 2))
-        for j in range(PACK):
-            nc.sync.dma_start(out=x_single[j][:], in_=x_rows(1, j, 1))
+        for r in range(1, PASSES * PACK):
+            load_x(r)
         for g in range(PASSES):
             nc.sync.dma_start(out=w_raw[g][:], in_=w1[g * K_PASS : (g + 1) * K_PASS, :].rearrange("(p j) c -> p j c", j=PACK))
 
@@ -89,8 +88,8 @@ def tile_picked_embpos_none_e_kernel(tc, xT, w1, w2_words, w2_scales, pos, offs,
 
         def join(copy, dtype, woven, pairs):
             copy(
-                out=woven.rearrange("p n j -> p (n j)").bitcast(dtype).rearrange("p (c i a) -> p c a i", i=WALK, a=2),
-                in_=pairs.rearrange("p a n e -> p a (n e)").bitcast(dtype).rearrange("p a (c i) -> p c a i", i=WALK),
+                out=woven.rearrange("p n j -> p (n j)").bitcast(dtype).rearrange("p (n a) -> p n a", a=2),
+                in_=pairs.rearrange("p a n e -> p a (n e)").bitcast(dtype).rearrange("p a n -> p n a"),
             )
 
         x_plane = [tile("x_plane_%d" % g, [P, S], U8) for g in range(PASSES)]
@@ -108,9 +107,8 @@ def tile_picked_embpos_none_e_kernel(tc, xT, w1, w2_words, w2_scales, pos, offs,
 
         def weave_w(g):
             woven = [tile("w_bf_%d_%d" % (g, u), [P, 2, P, PACK], BF16) for u in range(2)]
-            places = ("p t m (a e) -> p m e a t", "p t m (e a) -> p m e a t")[g]
-            target = [woven[u][:].rearrange(places, a=2) for u in range(2)]
-            source = [w_raw[g][:].rearrange("p (e a) (m t) -> p m e a t", a=2, t=PACK)[:, :, :, :, 2 * u : 2 * u + 2] for u in range(2)]
+            target = [woven[u][:].rearrange("p t m j -> p m j t") for u in range(2)]
+            source = [w_raw[g][:].rearrange("p j (m t) -> p m j t", t=PACK)[:, :, :, 2 * u : 2 * u + 2] for u in range(2)]
             cut = P - W_VECTOR_COLUMNS[g]
             nc.scalar.copy(out=target[1][:, :cut], in_=source[1][:, :cut])
             nc.vector.tensor_copy(out=target[0], in_=source[0])
@@ -122,9 +120,9 @@ def tile_picked_embpos_none_e_kernel(tc, xT, w1, w2_words, w2_scales, pos, offs,
                 )
 
         pairs = tile("pairs_0", [P, 2, S, 2], BF16)
-        for e in range(2):
-            gather_scalar(pairs[:, 0, :, e], x_pairs[e][:], 0, S)
-            gather_vector(pairs[:, 1, :, e], x_pairs[e][:, T:], 0, S)
+        for j in range(PACK):
+            gather_vector(pairs[:, j // 2, :HALF, j % 2], x_raw[j][:], 0, HALF)
+            gather_scalar(pairs[:, j // 2, HALF:, j % 2], x_raw[j][:], HALF, HALF)
         woven = [tile("woven_0_%d" % i, [P, HALF, PACK], BF16) for i in range(2)]
         first_codes = tile("x_codes_0", [P, S], U32)
         join(nc.vector.tensor_copy, F32, woven[0][:], pairs[:, :, :HALF, :])
@@ -139,10 +137,10 @@ def tile_picked_embpos_none_e_kernel(tc, xT, w1, w2_words, w2_scales, pos, offs,
         for j in range(PACK):
             a, e = divmod(j, 2)
             cut = VECTOR_ENTRIES[a]
-            gather_vector(early[:, a, :cut, e], x_single[j][:], 0, cut)
-            gather_scalar(early[:, a, cut:, e], x_single[j][:], cut, HALF - cut)
+            gather_vector(early[:, a, :cut, e], x_raw[PACK + j][:], 0, cut)
+            gather_scalar(early[:, a, cut:, e], x_raw[PACK + j][:], cut, HALF - cut)
             for i in (2, 3):
-                gather_scalar(pairs[i][:, a, :, e], x_single[j][:], i * QUARTER, QUARTER)
+                gather_scalar(pairs[i][:, a, :, e], x_raw[PACK + j][:], i * QUARTER, QUARTER)
         for i in (1, 0):
             join(nc.vector.tensor_copy, F32, woven[i], pairs[i])
         for i in (1, 0):

@@ -24,8 +24,9 @@ BLOCKS = S // BLOCK
 HALF = S // 2
 QUARTER = S // 4
 WALK = 4
-POS_LOADS = (384, 384, 256)
-GPSIMD_BLOCK = 3
+POS_LOADS = (384, 416, 224)
+GPSIMD_START = 3 * BLOCK
+GPSIMD_ENTRIES = 160
 H_BANKS = 4
 WARM_UPS = 7
 W_VECTOR_COLUMNS = (48, 40)
@@ -68,7 +69,7 @@ def tile_picked_embpos_none_e_kernel(tc, xT, w1, w2_words, w2_scales, pos, offs,
         for width in POS_LOADS:
             piece = tile("pos_%d" % start, [P, PACK, width], F32)
             nc.sync.dma_start(out=piece[:], in_=pos_rows[:, :, start : start + width])
-            pos_sb.extend(piece[:, :, c : c + BLOCK] for c in range(0, width, BLOCK))
+            pos_sb.append((start, width, piece))
             start += width
         nc.sync.dma_start(out=w2_codes[:].bitcast(I32), in_=w2_words[0].bitcast(I32))
         for q in range(4):
@@ -173,20 +174,40 @@ def tile_picked_embpos_none_e_kernel(tc, xT, w1, w2_words, w2_scales, pos, offs,
         ]
         h_blocks = [h_tiles[index][:, c * BLOCK : (c + 1) * BLOCK, :] for index, width in enumerate(OUT_GROUPS) for c in range(width)]
 
+        product = tile("product", [P, GPSIMD_ENTRIES, PACK], F32)
+
+        def pos_at(start, count):
+            first, piece = [(first, piece) for first, width, piece in pos_sb if first <= start < first + width][0]
+            return piece[:, :, start - first : start - first + count]
+
+        def add_vector(start, count):
+            b, c = divmod(start, BLOCK)
+            nc.vector.tensor_tensor(
+                out=h_blocks[b][:, c : c + count, :].rearrange("p (c i) t -> p c t i", i=WALK),
+                in0=banks[b][:, :, c : c + count].rearrange("p t (c i) -> p c t i", i=WALK),
+                in1=pos_at(start, count).rearrange("p t (c i) -> p c t i", i=WALK),
+                op=mybir.AluOpType.add,
+            )
+
         def add_pos(b):
-            if b == GPSIMD_BLOCK:
-                product = tile("product", [P, BLOCK, PACK], F32)
-                nc.scalar.copy(out=product[:], in_=banks[b][:].rearrange("p t n -> p n t"))
-                nc.gpsimd.tensor_tensor(
-                    out=h_blocks[b], in0=product[:], in1=pos_sb[b].rearrange("p t n -> p n t"), op=mybir.AluOpType.add
-                )
-            else:
-                nc.vector.tensor_tensor(
-                    out=h_blocks[b].rearrange("p (c i) t -> p c t i", i=WALK),
-                    in0=banks[b][:].rearrange("p t (c i) -> p c t i", i=WALK),
-                    in1=pos_sb[b].rearrange("p t (c i) -> p c t i", i=WALK),
-                    op=mybir.AluOpType.add,
-                )
+            start, stop = b * BLOCK, (b + 1) * BLOCK
+            gpsimd_stop = GPSIMD_START + GPSIMD_ENTRIES
+            if GPSIMD_START <= start < gpsimd_stop:
+                count = min(stop, gpsimd_stop) - start
+                at = start - GPSIMD_START
+                nc.scalar.copy(out=product[:, at : at + count], in_=banks[b][:, :, :count].rearrange("p t n -> p n t"))
+                start += count
+                if start == gpsimd_stop:
+                    nc.gpsimd.tensor_tensor(
+                        out=h_tiles[2][:, :GPSIMD_ENTRIES, :],
+                        in0=product[:],
+                        in1=pos_at(GPSIMD_START, GPSIMD_ENTRIES).rearrange("p t n -> p n t"),
+                        op=mybir.AluOpType.add,
+                    )
+            cuts = [start] + [first for first, width, piece in pos_sb if start < first < stop] + [stop]
+            for a, z in zip(cuts, cuts[1:]):
+                if a < z:
+                    add_vector(a, z - a)
 
         h_codes = tile("h_codes", [P, S], U32)
         h_plane = tile("h_plane", [P, S], U8)

@@ -24,9 +24,9 @@ BLOCKS = S // BLOCK
 HALF = S // 2
 QUARTER = S // 4
 WALK = 4
-POS_LOADS = (384, 416, 224)
+POS_LOADS = (384, 448, 192)
 GPSIMD_START = 3 * BLOCK
-GPSIMD_ENTRIES = 160
+GPSIMD_ENTRIES = 128
 H_BANKS = 4
 WARM_UPS = 7
 W_VECTOR_COLUMNS = (48, 40)

@@ -42,7 +42,7 @@ def tile_picked_embpos_none_e_kernel(tc, xT, w1, w2_words, w2_scales, pos, offs,
         psum_o = ctx.enter_context(tc.psum_pool(name="psum_o", bufs=8 - H_BANKS))
 
         def tile(name, shape, dtype, after=None):
-            return keep.tile(shape, dtype, name=name, tag=after or name, align_bytes=64)
+            return keep.tile(shape, dtype, name=name, tag=after or name, align_bytes=256)
 
         offsets = keep.tile([P, S // 16], U16, name="offsets")
         w2_codes = tile("w2_codes", [P, 2 * N], U8)

from contextlib import ExitStack

import concourse.mybir as mybir

K, T, S, H, N = 1024, 2048, 1024, 512, 128
FLOPS = 2 * K * H * S + 2 * H * N * S

F32 = mybir.dt.float32
BF16 = mybir.dt.bfloat16
I32 = mybir.dt.int32
U32 = mybir.dt.uint32
U16 = mybir.dt.uint16
U8 = mybir.dt.uint8
FP8X4 = mybir.dt.float8_e4m3fn_x4
FP4X4 = mybir.dt.float4_e2m1fn_x4
COPY = mybir.ActivationFunctionType.Copy

P = 128
PACK = 4
K_PASS = P * PACK
PASSES = K // K_PASS
BLOCK = 128
BLOCKS = S // BLOCK
HALF = S // 2
QUARTER = S // 4
WALK = 4
POS_LOADS = (384, 448, 192)
GPSIMD_START = 3 * BLOCK
GPSIMD_ENTRIES = 128
H_BANKS = 4
WARM_UPS = 7
W_VECTOR_COLUMNS = (48, 40)
VECTOR_ENTRIES = (384, 256)
OUT_GROUPS = (2, 1, 2, 2, 1)


def tile_picked_embpos_none_e_kernel(tc, xT, w1, w2_words, w2_scales, pos, offs, out):
    nc = tc.nc
    with ExitStack() as ctx:
        keep = ctx.enter_context(tc.tile_pool(name="keep", bufs=1))
        psum_h = ctx.enter_context(tc.psum_pool(name="psum_h", bufs=H_BANKS))
        psum_o = ctx.enter_context(tc.psum_pool(name="psum_o", bufs=8 - H_BANKS))

        def tile(name, shape, dtype, after=None):
            return keep.tile(shape, dtype, name=name, tag=after or name, align_bytes=256)

        offsets = keep.tile([P, S // 16], U16, name="offsets")
        w2_codes = tile("w2_codes", [P, 2 * N], U8)
        w2_plane = tile("w2_plane", [P, N], U8)
        nc.gpsimd.memset(w2_plane[:].bitcast(I32), 0)

        x_raw = [tile("x_raw_%d" % r, [P, T], F32) for r in range(PASSES * PACK)]
        w_raw = [tile("w_raw_%d" % g, [P, PACK, H], F32) for g in range(PASSES)]

        def load_x(r):
            g, j = divmod(r, PACK)
            nc.sync.dma_start(out=x_raw[r][:], in_=xT[g * K_PASS : (g + 1) * K_PASS, :].rearrange("(p j) t -> p j t", j=PACK)[:, j, :])

        load_x(0)
        nc.sync.dma_start(offsets[:], offs)
        for r in range(1, PASSES * PACK):
            load_x(r)
        for g in range(PASSES):
            nc.sync.dma_start(out=w_raw[g][:], in_=w1[g * K_PASS : (g + 1) * K_PASS, :].rearrange("(p j) c -> p j c", j=PACK))

        pos_rows = pos.rearrange("(p t) s -> p t s", t=PACK)
        pos_sb = []
        start = 0
        for width in POS_LOADS:
            piece = tile("pos_%d" % start, [P, PACK, width], F32)
            nc.sync.dma_start(out=piece[:], in_=pos_rows[:, :, start : start + width])
            pos_sb.append((start, width, piece))
            start += width
        nc.sync.dma_start(out=w2_codes[:].bitcast(I32), in_=w2_words[0].bitcast(I32))
        for q in range(4):
            nc.sync.dma_start(
                out=w2_plane[32 * q : 32 * q + 4, :].bitcast(I32),
                in_=w2_scales[0, 4 * q : 4 * q + 4, :].bitcast(I32),
            )

        def entries(start, count):
            return offsets[:, start // 16 : (start + count) // 16]

        def gather_vector(target, window, start, count):
            nc.vector.tensor_copy(target, window.indirect(entries(start, count)))

        def gather_scalar(target, window, start, count):
            nc.scalar.activation(out=target, in_=window.indirect(entries(start, count)), func=COPY)

        def join(copy, dtype, woven, pairs):
            copy(
                out=woven.rearrange("p n j -> p (n j)").bitcast(dtype).rearrange("p (n a) -> p n a", a=2),
                in_=pairs.rearrange("p a n e -> p a (n e)").bitcast(dtype).rearrange("p a n -> p n a"),
            )

        x_plane = [tile("x_plane_%d" % g, [P, S], U8) for g in range(PASSES)]
        x_codes = [{}, {}]

        def quantise_x(g, codes, woven, start, count):
            nc.vector.quantize_mx(
                out=codes.bitcast(FP8X4), scales=x_plane[g][:, start : start + count], in_=woven.rearrange("p n j -> p (n j)")
            )
            for c in range(0, count, BLOCK):
                x_codes[g][(start + c) // BLOCK] = codes[:, c : c + BLOCK]

        w_codes = [tile("w_codes_%d" % g, [P, H], U32) for g in range(PASSES)]
        w_plane = [tile("w_plane_%d" % g, [P, H], U8) for g in range(PASSES)]

        def weave_w(g):
            woven = [tile("w_bf_%d_%d" % (g, u), [P, 2, P, PACK], BF16) for u in range(2)]
            target = [woven[u][:].rearrange("p t m j -> p m j t") for u in range(2)]
            source = [w_raw[g][:].rearrange("p j (m t) -> p m j t", t=PACK)[:, :, :, 2 * u : 2 * u + 2] for u in range(2)]
            cut = P - W_VECTOR_COLUMNS[g]
            nc.scalar.copy(out=target[1][:, :cut], in_=source[1][:, :cut])
            nc.vector.tensor_copy(out=target[0], in_=source[0])
            nc.vector.tensor_copy(out=target[1][:, cut:], in_=source[1][:, cut:])
            for u in range(2):
                cols = slice(2 * u * P, 2 * (u + 1) * P)
                nc.vector.quantize_mx(
                    out=w_codes[g][:, cols].bitcast(FP8X4), scales=w_plane[g][:, cols], in_=woven[u][:].rearrange("p t m j -> p (t m j)")
                )

        pairs = tile("pairs_0", [P, 2, S, 2], BF16)
        for j in range(PACK):
            gather_vector(pairs[:, j // 2, :HALF, j % 2], x_raw[j][:], 0, HALF)
            gather_scalar(pairs[:, j // 2, HALF:, j % 2], x_raw[j][:], HALF, HALF)
        woven = [tile("woven_0_%d" % i, [P, HALF, PACK], BF16) for i in range(2)]
        first_codes = tile("x_codes_0", [P, S], U32)
        join(nc.vector.tensor_copy, F32, woven[0][:], pairs[:, :, :HALF, :])
        join(nc.vector.tensor_copy, F32, woven[1][:], pairs[:, :, HALF:, :])
        for i in range(2):
            quantise_x(0, first_codes[:, i * HALF : (i + 1) * HALF], woven[i][:], i * HALF, HALF)

        early = tile("pairs_1_0", [P, 2, HALF, 2], BF16)
        pairs = [early[:, :, :QUARTER, :], early[:, :, QUARTER:, :]] + [tile("pairs_1_%d" % i, [P, 2, QUARTER, 2], BF16) for i in (2, 3)]
        woven = [tile("woven_1_%d" % i, [P, QUARTER, PACK], BF16)[:] for i in range(2)]
        woven_late = tile("woven_late", [P, HALF, PACK], BF16)
        for j in range(PACK):
            a, e = divmod(j, 2)
            cut = VECTOR_ENTRIES[a]
            gather_vector(early[:, a, :cut, e], x_raw[PACK + j][:], 0, cut)
            gather_scalar(early[:, a, cut:, e], x_raw[PACK + j][:], cut, HALF - cut)
            for i in (2, 3):
                gather_scalar(pairs[i][:, a, :, e], x_raw[PACK + j][:], i * QUARTER, QUARTER)
        for i in (1, 0):
            join(nc.vector.tensor_copy, F32, woven[i], pairs[i])
        for i in (1, 0):
            quantise_x(1, tile("x_codes_1_%d" % i, [P, QUARTER], U32)[:], woven[i], i * QUARTER, QUARTER)
        join(nc.scalar.copy, U32, woven_late[:, :QUARTER, :], pairs[2][:])
        weave_w(0)
        join(nc.scalar.copy, U32, woven_late[:, QUARTER:, :], pairs[3][:])
        weave_w(1)
        quantise_x(1, tile("x_codes_1_2", [P, HALF], U32, "w_raw_1")[:], woven_late[:], HALF, HALF)

        banks = {}

        def first_product(b, g, tiles=range(PACK)):
            if b not in banks:
                banks[b] = psum_h.tile([P, PACK, BLOCK], F32, name="h_bank")
            for t in tiles:
                w_cols = slice(t * P, (t + 1) * P)
                nc.tensor.matmul_mx(
                    out=banks[b][:, t, :],
                    lhsT=w_codes[g][:, w_cols].bitcast(FP8X4),
                    lhsT_scale=w_plane[g][:, w_cols],
                    rhs=x_codes[g][b].bitcast(FP8X4),
                    rhs_scale=x_plane[g][:, b * BLOCK : (b + 1) * BLOCK],
                    start=(g == 0 and t == 0),
                    stop=(g == PASSES - 1 and t == PACK - 1),
                )

        h_tiles = [
            tile("h_%d" % index, [P, width * BLOCK, PACK], BF16, "h_0" if index == 2 else None) for index, width in enumerate(OUT_GROUPS)
        ]
        h_blocks = [h_tiles[index][:, c * BLOCK : (c + 1) * BLOCK, :] for index, width in enumerate(OUT_GROUPS) for c in range(width)]

        product = tile("product", [P, GPSIMD_ENTRIES, PACK], F32)

        def pos_at(start, count):
            first, piece = [(first, piece) for first, width, piece in pos_sb if first <= start < first + width][0]
            return piece[:, :, start - first : start - first + count]

        def add_vector(start, count):
            b, c = divmod(start, BLOCK)
            nc.vector.tensor_tensor(
                out=h_blocks[b][:, c : c + count, :].rearrange("p (c i) t -> p c t i", i=WALK),
                in0=banks[b][:, :, c : c + count].rearrange("p t (c i) -> p c t i", i=WALK),
                in1=pos_at(start, count).rearrange("p t (c i) -> p c t i", i=WALK),
                op=mybir.AluOpType.add,
            )

        def add_pos(b):
            start, stop = b * BLOCK, (b + 1) * BLOCK
            gpsimd_stop = GPSIMD_START + GPSIMD_ENTRIES
            if GPSIMD_START <= start < gpsimd_stop:
                count = min(stop, gpsimd_stop) - start
                at = start - GPSIMD_START
                nc.scalar.copy(out=product[:, at : at + count], in_=banks[b][:, :, :count].rearrange("p t n -> p n t"))
                start += count
                if start == gpsimd_stop:
                    nc.gpsimd.tensor_tensor(
                        out=h_tiles[2][:, :GPSIMD_ENTRIES, :],
                        in0=product[:],
                        in1=pos_at(GPSIMD_START, GPSIMD_ENTRIES).rearrange("p t n -> p n t"),
                        op=mybir.AluOpType.add,
                    )
            cuts = [start] + [first for first, width, piece in pos_sb if start < first < stop] + [stop]
            for a, z in zip(cuts, cuts[1:]):
                if a < z:
                    add_vector(a, z - a)

        h_codes = tile("h_codes", [P, S], U32)
        h_plane = tile("h_plane", [P, S], U8)
        result = tile("result", [P, S], F32)

        def quantise_h(index):
            start = sum(OUT_GROUPS[:index]) * BLOCK
            cols = slice(start, start + OUT_GROUPS[index] * BLOCK)
            nc.vector.quantize_mx(
                out=h_codes[:, cols].bitcast(FP8X4), scales=h_plane[:, cols], in_=h_tiles[index][:].rearrange("p n t -> p (n t)")
            )

        def second_product(copy, start, widths):
            acc = psum_o.tile([P, sum(widths)], F32, name="out_bank")
            at = 0
            for width in widths:
                cols = slice(start + at, start + at + width)
                nc.tensor.matmul_mx(
                    out=acc[:, at : at + width],
                    lhsT=w2_codes[:].bitcast(FP4X4),
                    lhsT_scale=w2_plane[:],
                    rhs=h_codes[:, cols].bitcast(FP8X4),
                    rhs_scale=h_plane[:, cols],
                    start=True,
                    stop=True,
                )
                at += width
            copy(out=result[:, start : start + at], in_=acc[:])

        def store(start, width):
            nc.sync.dma_start(out=out[:, start : start + width], in_=result[:, start : start + width])

        warm = psum_o.tile([P, BLOCK], F32, name="out_bank")
        for i in range(WARM_UPS):
            nc.tensor.matmul_mx(
                out=warm[:],
                lhsT=x_codes[1][3].bitcast(FP8X4),
                lhsT_scale=x_plane[1][:, 3 * BLOCK : 4 * BLOCK],
                rhs=x_codes[1][3].bitcast(FP8X4),
                rhs_scale=x_plane[1][:, 3 * BLOCK : 4 * BLOCK],
                start=True,
                stop=True,
            )
        for tiles in ((0, 1), (2, 3)):
            for b in range(H_BANKS):
                first_product(b, 0, tiles)
        for b in range(BLOCKS):
            if b >= H_BANKS:
                first_product(b, 0)
            first_product(b, 1)
            add_pos(b)
            if b == 2:
                quantise_h(0)
                quantise_h(1)
                second_product(nc.scalar.copy, 0, (2 * BLOCK, BLOCK))
                store(0, 3 * BLOCK)
        for index in (2, 3, 4):
            quantise_h(index)
        second_product(nc.scalar.copy, 3 * BLOCK, (2 * BLOCK,))
        store(3 * BLOCK, 2 * BLOCK)
        second_product(nc.vector.tensor_copy, 5 * BLOCK, (2 * BLOCK,))
        second_product(nc.scalar.copy, 7 * BLOCK, (BLOCK,))
        store(5 * BLOCK, 3 * BLOCK)
